import numpy as np
import ml_dtypes


def mxq(x, axis, fmt="e4m3"):
    dtype, down = {"e4m3": (ml_dtypes.float8_e4m3fn, 7), "e5m2": (ml_dtypes.float8_e5m2, 14)}[fmt]
    v = np.moveaxis(np.asarray(x, np.float32).astype(ml_dtypes.bfloat16).astype(np.float64), axis, -1)
    blocks = v.reshape(v.shape[:-1] + (-1, 32))
    amax = np.abs(blocks).max(-1, keepdims=True)
    byte = np.maximum(np.where(amax > 0, np.frexp(amax)[1] - 1 + 127, 0) - down, 1)
    scale = np.exp2(byte - 127.0)
    codes = (blocks / scale).astype(np.float32).astype(dtype).astype(np.float64)
    return np.moveaxis((codes * scale).reshape(v.shape), -1, axis)


WIDE = False


def mx_kscale(k):
    if not WIDE:
        return np.ones(k)
    levels = np.array([24, -24, 12, -12, 0])
    if k % 512:
        return np.exp2(np.random.permutation(np.resize(levels, k // 32))).repeat(32)
    a = np.empty((k // 512, 16))
    for p in range(k // 512):
        a[p, :8] = np.random.permutation(np.resize(levels, 8))
        for g in range(8):
            far = levels[np.abs(levels - a[p, g]) >= 10]
            a[p, g + 8] = far[np.random.randint(len(far))]
    return np.exp2(a.ravel()).repeat(32)


def f64(x):
    return np.asarray(x).astype(np.float64)


def striped(idx):
    return np.tile(idx.reshape(-1, 16).T, (8, 1)).astype(np.uint16)


def unstriped(offs):
    return offs[:16].T.reshape(-1).astype(np.int64)


E2M1 = np.array([0.0, 0.5, 1.0, 1.5, 2.0, 3.0, 4.0, 6.0, -0.0, -0.5, -1.0, -1.5, -2.0, -3.0, -4.0, -6.0])


def pack_weight(w, fmt):
    k, n = w.shape
    w = f64(np.asarray(w, np.float32).astype(ml_dtypes.bfloat16)).reshape(k // 32, 32, n)
    amax = np.abs(w).max(1)
    if fmt == "e4m3":
        byte = np.frexp(amax)[1] - 1 + 127 - 7
    else:
        mant, ex = np.frexp(amax / 6.0)
        byte = np.where(mant > 0.5, ex, ex - 1) + 127
    byte = np.clip(np.where(amax > 0, byte, 1), 1, 254)
    scaled = (w * np.exp2(127.0 - byte)[:, None, :]).reshape(k, n).astype(np.float32)
    by_word = np.ascontiguousarray(scaled.reshape(k // 512, 128, 4, n).transpose(0, 1, 3, 2))
    if fmt == "e4m3":
        words = by_word.astype(ml_dtypes.float8_e4m3fn).view(np.uint8)
    else:
        c = by_word.astype(ml_dtypes.float4_e2m1fn).view(np.uint8) & 0xF
        words = (c[..., 0::2] | (c[..., 1::2] << 4)).reshape(k // 512, 128, 2 * n)
    return np.ascontiguousarray(words), np.ascontiguousarray(byte.astype(np.uint8).reshape(k // 512, 16, n))


def unpack_weight(words, scales, fmt):
    g, _, n = scales.shape
    words = np.ascontiguousarray(words).reshape(g, 128, n, -1)
    if fmt == "e4m3":
        vals = words.view(ml_dtypes.float8_e4m3fn).astype(np.float64)
    else:
        nib = np.empty((g, 128, n, 4), np.uint8)
        nib[..., 0::2] = words & 0xF
        nib[..., 1::2] = words >> 4
        vals = E2M1[nib]
    vals = vals * np.repeat(np.exp2(scales.astype(np.float64) - 127.0), 8, axis=1)[..., None]
    return vals.transpose(0, 1, 3, 2).reshape(g * 512, n)


def pack_table4(v):
    words, scales = pack_weight(v, "e2m1")
    g, t = words.shape[0] // 2, v.shape[1]
    return np.ascontiguousarray(words.reshape(g, 2, 128, t, 2).transpose(0, 2, 3, 1, 4).reshape(g, 128, t, 4)), scales


def unpack_table4(words, scales):
    g, _, t, _ = words.shape
    return unpack_weight(words.reshape(g, 128, t, 2, 2).transpose(0, 3, 1, 2, 4).reshape(2 * g, 128, 2 * t), scales, "e2m1")


def planes(y):
    n, m = y.shape
    v = y.astype(np.float32).astype(ml_dtypes.bfloat16).astype(np.float64).reshape(n // 32, 32, m)
    top = np.abs(v).max(1)
    byte = np.clip(np.where(top > 0, np.frexp(top)[1] - 1 + 127 - 7, 1), 1, 254)
    codes = (v * np.exp2(127.0 - byte)[:, None, :]).reshape(n, m).astype(np.float32).astype(ml_dtypes.float8_e4m3fn).view(np.uint8)
    words = codes.reshape(n // 512, 128, 4, m).transpose(0, 1, 3, 2)
    return np.ascontiguousarray(words), np.ascontiguousarray(byte.astype(np.uint8).reshape(n // 512, 16, m))


def sigm(f):
    return 1.0 / (1.0 + np.exp(-np.maximum(f, -700.0)))


K, L, N, T, J = 512, 1024, 512, 2048, 1024


def setup_inputs():
    n = np.random.standard_normal
    s = mx_kscale(K)[:, None]
    s2 = mx_kscale(L)[:, None]
    p_tab = pack_weight(n((K, T)) * s, "e4m3")
    p_tab2 = pack_table4(n((L, T)) * s2)
    p_wt = pack_weight(n((L, N)) / np.sqrt(L) / s2, "e4m3")
    return {
        "tab_words": p_tab[0],
        "tab_scales": p_tab[1],
        "tab2_words": p_tab2[0],
        "tab2_scales": p_tab2[1],
        "zv": (n((K, N)) / np.sqrt(K) / s).astype(np.float32),
        "zt": (n((L, N)) / np.sqrt(L) / s2).astype(np.float32),
        "b": (0.3 * n(N)).astype(np.float32),
        "wv": (n((K, N)) / np.sqrt(K) / s).astype(np.float32),
        "wt_words": p_wt[0],
        "wt_scales": p_wt[1],
        "wgo": np.tile(np.random.uniform(0.5, 2.0, J), (128, 1)).astype(np.float32),
        "offs": striped(np.random.permutation(T)[:J]),
        "offs2": striped(np.random.permutation(T)[:J]),
    }


def reference(tab_words, tab_scales, tab2_words, tab2_scales, zv, zt, b, wv, wt_words, wt_scales, wgo, offs, offs2):
    idx = unstriped(offs)
    idx2 = unstriped(offs2)
    tab_ = unpack_weight(tab_words, tab_scales, "e4m3")[:, idx]
    tab2_ = unpack_table4(tab2_words, tab2_scales)[:, idx2]
    zv_ = mxq(f64(zv), 0, "e4m3")
    zt_ = mxq(f64(zt), 0, "e4m3")
    z = zv_.T @ tab_ + zt_.T @ tab2_
    gate = sigm(z + f64(b)[:, None])
    wv_ = mxq(f64(wv), 0, "e4m3")
    wt_ = unpack_weight(wt_words, wt_scales, "e4m3")
    hv = wv_.T @ tab_
    ht = wt_.T @ tab2_
    av = np.maximum(hv, 0.0)
    at = np.maximum(ht, 0.0)
    out = np.zeros((N, T))
    out[:, idx] = f64(wgo)[0] * (at + gate * (av - at))
    return (out,) + planes(out)

@@ -1,0 +1,228 @@
+from contextlib import ExitStack
+
+import concourse.mybir as mybir
+
+K, L, N, T, J = 512, 1024, 512, 2048, 1024
+FLOPS = 2 * N * J * (K + L) * 2
+
+F32 = mybir.dt.float32
+BF16 = mybir.dt.bfloat16
+I32 = mybir.dt.int32
+U32 = mybir.dt.uint32
+U16 = mybir.dt.uint16
+U8 = mybir.dt.uint8
+FP8X4 = mybir.dt.float8_e4m3fn_x4
+FP4X4 = mybir.dt.float4_e2m1fn_x4
+ALU = mybir.AluOpType
+ACT = mybir.ActivationFunctionType
+
+P = 128
+PACK = 4
+HALF = 512
+QUARTER = 512
+
+
+def tile_list_gmu_relu_scatP_kernel(
+    tc, tab_words, tab_scales, tab2_words, tab2_scales, zv, zt, b, wv, wt_words, wt_scales, wgo, offs, offs2, out_0, out_1, out_2
+):
+    nc = tc.nc
+    with ExitStack() as ctx:
+        keep = ctx.enter_context(tc.tile_pool(name="keep", bufs=1))
+        ring = ctx.enter_context(tc.tile_pool(name="ring", bufs=2))
+        psum = ctx.enter_context(tc.psum_pool(name="psum", bufs=2))
+
+        def held(shape, dtype, name):
+            return keep.tile(shape, dtype, name=name, align_bytes=64)
+
+        list1 = keep.tile([P, J // 16], U16, name="list1")
+        list2 = keep.tile([P, J // 16], U16, name="list2")
+        v_words = held([P, T], U32, "v_words")
+        v2_words = held([P, T], U32, "v2_words")
+        v_scales = held([P, T], U8, "v_scales")
+        v2_scales = held([P, T], U8, "v2_scales")
+        wt_raw = held([P, 2, N], I32, "wt_raw")
+        wt_scales_raw = held([P, 2 * N], U8, "wt_scales_raw")
+        picked2_scales = held([P, J], U8, "picked2_scales")
+        picked2_scales_b = held([P, J], U8, "picked2_scales_b")
+        windows = [held([P, T], F32, "window%d" % t) for t in range(PACK)]
+        raw = {name: held([P, PACK, N], F32, "raw_" + name) for name in ("wv", "zv", "zt0", "zt1")}
+        bias = held([P, PACK], F32, "bias")
+        neg_bias = held([P, PACK], F32, "neg_bias")
+        weight = held([P, J], F32, "weight")
+
+        for tile in (v2_scales, v_scales, wt_scales_raw, picked2_scales_b):
+            nc.vector.memset(tile[:].bitcast(I32), 0)
+        nc.vector.memset(windows[0][:], 0.0)
+        nc.vector.memset(windows[1][:], 0.0)
+        nc.gpsimd.memset(windows[2][:], 0.0)
+        nc.gpsimd.memset(windows[3][:], 0.0)
+
+        def table_view(words):
+            return words[0].rearrange("p t i -> p (t i)").bitcast(I32)
+
+        def load_weight(name, rows):
+            nc.sync.dma_start(raw[name][:], rows.rearrange("(p j) n -> p j n", j=PACK))
+
+        nc.sync.dma_start(list2[:], offs2)
+        nc.sync.dma_start(v2_words[:].bitcast(I32), table_view(tab2_words))
+        nc.sync.dma_start(list1[:], offs)
+        for q in range(4):
+            nc.sync.dma_start(v2_scales[32 * q : 32 * q + 8, :].bitcast(I32), tab2_scales[:, 4 * q : 4 * q + 4, :].bitcast(I32))
+        nc.sync.dma_start(v_words[:].bitcast(I32), table_view(tab_words))
+        load_weight("wv", wv)
+        for q in range(4):
+            nc.sync.dma_start(v_scales[32 * q : 32 * q + 4, :].bitcast(I32), tab_scales[0, 4 * q : 4 * q + 4, :].bitcast(I32))
+        load_weight("zv", zv)
+        nc.sync.dma_start(wt_raw[:], wt_words.rearrange("a p n i -> p a (n i)").bitcast(I32))
+        for q in range(4):
+            nc.sync.dma_start(
+                wt_scales_raw[32 * q : 32 * q + 4, :].bitcast(I32).rearrange("r (a n) -> r a n", a=2),
+                wt_scales[:, 4 * q : 4 * q + 4, :].bitcast(I32).rearrange("a r n -> r a n"),
+            )
+        nc.sync.dma_start(bias[:], b.rearrange("(p t) -> p t", t=PACK))
+        load_weight("zt0", zt[0:512, :])
+        load_weight("zt1", zt[512:1024, :])
+        nc.sync.dma_start(weight[:], wgo)
+
+        def half_of(offsets, h):
+            return offsets[:, 32 * h : 32 * h + 32]
+
+        nc.vector.tensor_copy(picked2_scales[:], v2_scales[:].indirect(list2[:]))
+        nc.gpsimd.dma_start(picked2_scales_b[0:100, :].bitcast(I32), picked2_scales[4:104, :].bitcast(I32))
+
+        picked = {}
+
+        def pick(h):
+            both = held([P, HALF], U32, "picked2_both%d" % h)
+            nc.vector.tensor_copy(both[:], v2_words[:].indirect(half_of(list2, h)))
+            words = held([P, HALF], U32, "picked_words%d" % h)
+            nc.vector.tensor_copy(words[:], v_words[:].indirect(half_of(list1, h)))
+            parted = held([P, 2, 2 * HALF], U8, "picked2_words%d" % h)
+            nc.vector.tensor_copy(parted[:].bitcast(U16), both[:].bitcast(U16).rearrange("p (j d) -> p d j", d=2))
+            scales = held([P, HALF], U8, "picked_scales%d" % h)
+            nc.vector.tensor_copy(scales[:], v_scales[:].indirect(half_of(list1, h)))
+            picked[h] = (words, scales, parted)
+
+        quantised = {}
+
+        def quantise_weight(name, copy):
+            grouped = ring.tile([P, PACK, P, PACK], BF16, name="grouped", align_bytes=64)
+            copy(grouped[:].rearrange("p t m j -> p m j t"), raw[name][:].rearrange("p j (m t) -> p m j t", t=PACK))
+            codes = held([P, N], U32, "codes_" + name)
+            scales = held([P, N], U8, "scales_" + name)
+            nc.vector.quantize_mx(out=codes[:].bitcast(FP8X4), scales=scales[:], in_=grouped[:].rearrange("p t m j -> p (t m j)"))
+            quantised[name] = (codes, scales)
+
+        pick(0)
+        quantise_weight("wv", nc.scalar.copy)
+        quantise_weight("zv", nc.scalar.copy)
+        wt_codes = held([P, 2, N], I32, "wt_codes")
+        wt_planes = held([P, 2 * N], U8, "wt_planes")
+        nc.vector.tensor_copy(
+            wt_codes[:].rearrange("p a (t m) -> p a m t", t=PACK), wt_raw[:].rearrange("p a (m t) -> p a m t", t=PACK)
+        )
+        nc.vector.tensor_copy(
+            wt_planes[:].rearrange("p (a t m) -> p a m t", a=2, t=PACK),
+            wt_scales_raw[:].rearrange("p (a m t) -> p a m t", a=2, t=PACK),
+        )
+        nc.vector.tensor_scalar_mul(neg_bias[:], bias[:], -1.0)
+        quantise_weight("zt0", nc.scalar.copy)
+        quantise_weight("zt1", nc.vector.tensor_copy)
+
+        results = {}
+
+        gates = {}
+
+        def blend(t, h, stage):
+            words, scales, parted = picked[h]
+            cols = slice(P * t, P * (t + 1))
+            items = slice(HALF * h, HALF * (h + 1))
+            v_side = (words[:].bitcast(FP8X4), scales[:])
+            v2_side = [
+                (parted[:, 0, :].bitcast(FP4X4), picked2_scales[:, items]),
+                (parted[:, 1, :].bitcast(FP4X4), picked2_scales_b[:, items]),
+            ]
+
+            def chip(name):
+                return quantised[name][0][:, cols].bitcast(FP8X4), quantised[name][1][:, cols]
+
+            def packed(a):
+                return wt_codes[:, a, cols].bitcast(FP8X4), wt_planes[:, N * a + P * t : N * a + P * (t + 1)]
+
+            def product(acc, passes):
+                for i, (lhs, rhs) in enumerate(passes):
+                    nc.tensor.matmul_mx(
+                        out=acc[:], lhsT=lhs[0], lhsT_scale=lhs[1], rhs=rhs[0], rhs_scale=rhs[1],
+                        start=(i == 0), stop=(i == len(passes) - 1),
+                    )
+
+            if stage == "gate":
+                z = psum.tile([P, HALF], F32, name="z")
+                product(z, [(chip("zv"), v_side), (chip("zt0"), v2_side[0]), (chip("zt1"), v2_side[1])])
+                gate = held([P, HALF], F32, "gate%d%d" % (t, h))
+                nc.scalar.activation(gate[:], z[:], ACT.Sigmoid, bias=bias[:, t : t + 1], scale=1.0)
+                rest = held([P, HALF], F32, "rest%d%d" % (t, h))
+                nc.scalar.activation(rest[:], z[:], ACT.Sigmoid, bias=neg_bias[:, t : t + 1], scale=-1.0)
+                gates[t, h] = (gate, rest)
+                return
+            gate, rest = gates[t, h]
+            hv = psum.tile([P, HALF], F32, name="hv", bufs=3)
+            product(hv, [(chip("wv"), v_side)])
+            ht = psum.tile([P, HALF], F32, name="ht", bufs=3)
+            product(ht, [(packed(0), v2_side[0]), (packed(1), v2_side[1])])
+            gv = ring.tile([P, HALF], F32, name="gv")
+            nc.vector.scalar_tensor_tensor(gv[:], hv[:], 0.0, gate[:], ALU.max, ALU.mult)
+            gt = ring.tile([P, HALF], F32, name="gt")
+            nc.vector.scalar_tensor_tensor(gt[:], ht[:], 0.0, rest[:], ALU.max, ALU.mult)
+            total = ring.tile([P, HALF], F32, name="total")
+            nc.gpsimd.tensor_tensor(total[:], gv[:], gt[:], ALU.add)
+            result = ring.tile([P, HALF], F32, name="result", bufs=3)
+            nc.gpsimd.tensor_tensor(result[:], total[:], weight[:, items], ALU.mult)
+            results[t, h] = result
+
+        rows_of = out_0.rearrange("(p t) c -> t p c", t=PACK)
+        pairs = [[held([P, 2, QUARTER], BF16, "pair%d_%d" % (u, q)) for q in range(4)] for u in range(2)]
+        woven = [held([P, QUARTER, PACK], BF16, "woven%d" % q) for q in range(4)]
+
+        def round_window(t, q, copy):
+            copy(pairs[t // 2][q][:, t % 2, :], windows[t][:, QUARTER * q : QUARTER * (q + 1)])
+
+        def weave(u, q, copy):
+            copy(woven[q][:, :, 2 * u : 2 * u + 2], pairs[u][q][:].rearrange("p e c -> p c e"))
+
+        def place(t, h):
+            nc.vector.tensor_copy(windows[t][:].indirect(half_of(list1, h)), results[t, h][:])
+            if h == 1:
+                nc.sync.dma_start(rows_of[t], windows[t][:])
+                if t < PACK - 1:
+                    for q in range(4):
+                        round_window(t, q, nc.scalar.copy)
+                if t == 1:
+                    for q in range(4):
+                        weave(0, q, nc.scalar.copy)
+
+        order = [(0, 0), (1, 0), (0, 1), (1, 1), (2, 0), (2, 1), (3, 0), (3, 1)]
+        for i in range(2):
+            blend(*order[i], "gate")
+            blend(*order[i], "mix")
+        pick(1)
+        for i in range(2, len(order)):
+            blend(*order[i], "gate")
+        for i in range(len(order)):
+            place(*order[i])
+            if i + 2 < len(order):
+                blend(*order[i + 2], "mix")
+
+        out_scales = held([P, T], U8, "out_scales")
+        words_view = table_view(out_1)
+        for q in range(4):
+            copy = nc.vector.tensor_copy if q < 2 else nc.scalar.copy
+            round_window(PACK - 1, q, copy)
+            weave(1, q, copy)
+        for q in range(4):
+            cols = slice(QUARTER * q, QUARTER * (q + 1))
+            out_codes = held([P, QUARTER], U32, "out_codes%d" % q)
+            nc.vector.quantize_mx(out=out_codes[:].bitcast(FP8X4), scales=out_scales[:, cols], in_=woven[q][:].rearrange("p c t -> p (c t)"))
+            nc.sync.dma_start(words_view[:, cols], out_codes[:].bitcast(I32))
+        for q in range(4):
+            nc.scalar.dma_start(out_2[0, 4 * q : 4 * q + 4, :].bitcast(I32), out_scales[32 * q : 32 * q + 4, :].bitcast(I32))

@@ -1,6 +1,7 @@
 from contextlib import ExitStack
 
 import concourse.mybir as mybir
+from concourse.masks import make_identity
 
 K, L, N, T, J = 512, 1024, 512, 2048, 1024
 FLOPS = 2 * N * J * (K + L) * 2
@@ -31,8 +32,8 @@ def tile_list_gmu_relu_scatP_kernel(
         ring = ctx.enter_context(tc.tile_pool(name="ring", bufs=2))
         psum = ctx.enter_context(tc.psum_pool(name="psum", bufs=2))
 
-        def held(shape, dtype, name):
-            return keep.tile(shape, dtype, name=name, align_bytes=64)
+        def held(shape, dtype, name, tag=""):
+            return keep.tile(shape, dtype, name=name, tag=tag or name, align_bytes=64)
 
         list1 = keep.tile([P, J // 16], U16, name="list1")
         list2 = keep.tile([P, J // 16], U16, name="list2")
@@ -43,36 +44,46 @@ def tile_list_gmu_relu_scatP_kernel(
         wt_raw = held([P, 2, N], I32, "wt_raw")
         wt_scales_raw = held([P, 2 * N], U8, "wt_scales_raw")
         picked2_scales = held([P, J], U8, "picked2_scales")
-        picked2_scales_b = held([P, J], U8, "picked2_scales_b")
+        planes2 = [held([P, J], U8, "planes2_%d" % a) for a in range(2)]
         windows = [held([P, T], F32, "window%d" % t) for t in range(PACK)]
-        raw = {name: held([P, PACK, N], F32, "raw_" + name) for name in ("wv", "zv", "zt0", "zt1")}
+        names = ("zv", "zt0", "zt1", "wv")
+        raw = {name: held([P, PACK, N], F32, "raw_" + name) for name in names}
         bias = held([P, PACK], F32, "bias")
-        neg_bias = held([P, PACK], F32, "neg_bias")
-        weight = held([P, J], F32, "weight")
+        weight_cols = held([P, J // P], F32, "weight_cols")
+        ident = held([P, P], F32, "ident")
 
-        for tile in (v2_scales, v_scales, wt_scales_raw, picked2_scales_b):
-            nc.vector.memset(tile[:].bitcast(I32), 0)
-        nc.vector.memset(windows[0][:], 0.0)
-        nc.vector.memset(windows[1][:], 0.0)
-        nc.gpsimd.memset(windows[2][:], 0.0)
-        nc.gpsimd.memset(windows[3][:], 0.0)
+        nc.vector.memset(v_scales[:].bitcast(I32), 0)
+        nc.gpsimd.memset(wt_scales_raw[:].bitcast(I32), 0)
+        for q in range(4):
+            nc.vector.memset(v2_scales[32 * q : 32 * q + 24, :].bitcast(I32), 0)
+        for tile in planes2:
+            nc.gpsimd.memset(tile[:].bitcast(I32), 0)
+        make_identity(nc, ident[:])
+        warm = held([P, 1], F32, "warm")
+        nc.scalar.activation(warm[:], ident[:, 0:1], ACT.Sigmoid)
+        for t in range(PACK):
+            for s in range(2):
+                nc.gpsimd.memset(windows[t][:, 1024 * s : 1024 * (s + 1)], 0.0)
 
         def table_view(words):
             return words[0].rearrange("p t i -> p (t i)").bitcast(I32)
+
+        def load_table(tile, words):
+            nc.sync.dma_start(tile[:].bitcast(I32), table_view(words))
 
         def load_weight(name, rows):
             nc.sync.dma_start(raw[name][:], rows.rearrange("(p j) n -> p j n", j=PACK))
 
         nc.sync.dma_start(list2[:], offs2)
-        nc.sync.dma_start(v2_words[:].bitcast(I32), table_view(tab2_words))
-        nc.sync.dma_start(list1[:], offs)
         for q in range(4):
-            nc.sync.dma_start(v2_scales[32 * q : 32 * q + 8, :].bitcast(I32), tab2_scales[:, 4 * q : 4 * q + 4, :].bitcast(I32))
-        nc.sync.dma_start(v_words[:].bitcast(I32), table_view(tab_words))
-        load_weight("wv", wv)
+            nc.sync.dma_start(v2_scales[32 * q + 24 : 32 * q + 32, :].bitcast(I32), tab2_scales[:, 4 * q : 4 * q + 4, :].bitcast(I32))
+        load_table(v2_words, tab2_words)
+        nc.sync.dma_start(list1[:], offs)
+        load_weight("zv", zv)
+        load_table(v_words, tab_words)
         for q in range(4):
             nc.sync.dma_start(v_scales[32 * q : 32 * q + 4, :].bitcast(I32), tab_scales[0, 4 * q : 4 * q + 4, :].bitcast(I32))
-        load_weight("zv", zv)
+        load_weight("zt0", zt[0:512, :])
         nc.sync.dma_start(wt_raw[:], wt_words.rearrange("a p n i -> p a (n i)").bitcast(I32))
         for q in range(4):
             nc.sync.dma_start(
@@ -80,42 +91,37 @@ def tile_list_gmu_relu_scatP_kernel(
                 wt_scales[:, 4 * q : 4 * q + 4, :].bitcast(I32).rearrange("a r n -> r a n"),
             )
         nc.sync.dma_start(bias[:], b.rearrange("(p t) -> p t", t=PACK))
-        load_weight("zt0", zt[0:512, :])
         load_weight("zt1", zt[512:1024, :])
-        nc.sync.dma_start(weight[:], wgo)
-
-        def half_of(offsets, h):
-            return offsets[:, 32 * h : 32 * h + 32]
+        load_weight("wv", wv)
+        with nc.allow_non_contiguous_dma(reason="one weight for each partition and block of items"):
+            nc.sync.dma_start(weight_cols[:], wgo[0].rearrange("(c p) -> p c", p=P))
 
         nc.vector.tensor_copy(picked2_scales[:], v2_scales[:].indirect(list2[:]))
-        nc.gpsimd.dma_start(picked2_scales_b[0:100, :].bitcast(I32), picked2_scales[4:104, :].bitcast(I32))
-
-        picked = {}
-
-        def pick(h):
-            both = held([P, HALF], U32, "picked2_both%d" % h)
-            nc.vector.tensor_copy(both[:], v2_words[:].indirect(half_of(list2, h)))
-            words = held([P, HALF], U32, "picked_words%d" % h)
-            nc.vector.tensor_copy(words[:], v_words[:].indirect(half_of(list1, h)))
-            parted = held([P, 2, 2 * HALF], U8, "picked2_words%d" % h)
-            nc.vector.tensor_copy(parted[:].bitcast(U16), both[:].bitcast(U16).rearrange("p (j d) -> p d j", d=2))
-            scales = held([P, HALF], U8, "picked_scales%d" % h)
-            nc.vector.tensor_copy(scales[:], v_scales[:].indirect(half_of(list1, h)))
-            picked[h] = (words, scales, parted)
+        for a in range(2):
+            nc.gpsimd.dma_start(planes2[a][0:100, :].bitcast(I32), picked2_scales[24 + 4 * a : 124 + 4 * a, :].bitcast(I32))
+        both = held([P, J], U32, "picked2_both")
+        nc.vector.tensor_copy(both[:], v2_words[:].indirect(list2[:]))
+        parted = held([P, 2, 2 * J], U8, "picked2_words")
+        nc.vector.tensor_copy(parted[:].bitcast(U16), both[:].bitcast(U16).rearrange("p (j d) -> p d j", d=2))
+        picked_words = held([P, J], U32, "picked_words")
+        nc.vector.tensor_copy(picked_words[:], v_words[:].indirect(list1[:]))
+        picked_scales = held([P, J], U8, "picked_scales")
+        nc.vector.tensor_copy(picked_scales[:], v_scales[:].indirect(list1[:]))
 
         quantised = {}
 
-        def quantise_weight(name, copy):
-            grouped = ring.tile([P, PACK, P, PACK], BF16, name="grouped", align_bytes=64)
-            copy(grouped[:].rearrange("p t m j -> p m j t"), raw[name][:].rearrange("p j (m t) -> p m j t", t=PACK))
-            codes = held([P, N], U32, "codes_" + name)
-            scales = held([P, N], U8, "scales_" + name)
+        def quantise_weight(name, t0, t1, copy):
+            count = t1 - t0
+            grouped = held([P, count, P, PACK], BF16, "grouped_%s%d" % (name, t0))
+            copy(grouped[:].rearrange("p t m j -> p m j t"), raw[name][:].rearrange("p j (m t) -> p m j t", t=PACK)[:, :, :, t0:t1])
+            codes = held([P, count * P], U32, "codes_%s%d" % (name, t0))
+            scales = held([P, count * P], U8, "scales_%s%d" % (name, t0))
             nc.vector.quantize_mx(out=codes[:].bitcast(FP8X4), scales=scales[:], in_=grouped[:].rearrange("p t m j -> p (t m j)"))
-            quantised[name] = (codes, scales)
+            for t in range(t0, t1):
+                cols = slice(P * (t - t0), P * (t - t0 + 1))
+                quantised[name, t] = (codes[:, cols].bitcast(FP8X4), scales[:, cols])
 
-        pick(0)
-        quantise_weight("wv", nc.scalar.copy)
-        quantise_weight("zv", nc.scalar.copy)
+        quantise_weight("zv", 0, 4, nc.scalar.copy)
         wt_codes = held([P, 2, N], I32, "wt_codes")
         wt_planes = held([P, 2 * N], U8, "wt_planes")
         nc.vector.tensor_copy(
@@ -125,104 +131,135 @@ def tile_list_gmu_relu_scatP_kernel(
             wt_planes[:].rearrange("p (a t m) -> p a m t", a=2, t=PACK),
             wt_scales_raw[:].rearrange("p (a m t) -> p a m t", a=2, t=PACK),
         )
-        nc.vector.tensor_scalar_mul(neg_bias[:], bias[:], -1.0)
-        quantise_weight("zt0", nc.scalar.copy)
-        quantise_weight("zt1", nc.vector.tensor_copy)
 
-        results = {}
+        quantise_weight("zt0", 0, 4, nc.scalar.copy)
+        quantise_weight("zt1", 0, 4, nc.scalar.copy)
+        quantise_weight("wv", 0, 2, nc.vector.tensor_copy)
 
-        gates = {}
+        def product(acc, passes):
+            for i, (lhs, rhs) in enumerate(passes):
+                nc.tensor.matmul_mx(
+                    out=acc[:], lhsT=lhs[0], lhsT_scale=lhs[1], rhs=rhs[0], rhs_scale=rhs[1],
+                    start=(i == 0), stop=(i == len(passes) - 1),
+                )
 
-        def blend(t, h, stage):
-            words, scales, parted = picked[h]
-            cols = slice(P * t, P * (t + 1))
-            items = slice(HALF * h, HALF * (h + 1))
-            v_side = (words[:].bitcast(FP8X4), scales[:])
-            v2_side = [
-                (parted[:, 0, :].bitcast(FP4X4), picked2_scales[:, items]),
-                (parted[:, 1, :].bitcast(FP4X4), picked2_scales_b[:, items]),
-            ]
-
-            def chip(name):
-                return quantised[name][0][:, cols].bitcast(FP8X4), quantised[name][1][:, cols]
-
-            def packed(a):
-                return wt_codes[:, a, cols].bitcast(FP8X4), wt_planes[:, N * a + P * t : N * a + P * (t + 1)]
-
-            def product(acc, passes):
-                for i, (lhs, rhs) in enumerate(passes):
-                    nc.tensor.matmul_mx(
-                        out=acc[:], lhsT=lhs[0], lhsT_scale=lhs[1], rhs=rhs[0], rhs_scale=rhs[1],
-                        start=(i == 0), stop=(i == len(passes) - 1),
-                    )
-
-            if stage == "gate":
-                z = psum.tile([P, HALF], F32, name="z")
-                product(z, [(chip("zv"), v_side), (chip("zt0"), v2_side[0]), (chip("zt1"), v2_side[1])])
-                gate = held([P, HALF], F32, "gate%d%d" % (t, h))
-                nc.scalar.activation(gate[:], z[:], ACT.Sigmoid, bias=bias[:, t : t + 1], scale=1.0)
-                rest = held([P, HALF], F32, "rest%d%d" % (t, h))
-                nc.scalar.activation(rest[:], z[:], ACT.Sigmoid, bias=neg_bias[:, t : t + 1], scale=-1.0)
-                gates[t, h] = (gate, rest)
-                return
-            gate, rest = gates[t, h]
-            hv = psum.tile([P, HALF], F32, name="hv", bufs=3)
-            product(hv, [(chip("wv"), v_side)])
-            ht = psum.tile([P, HALF], F32, name="ht", bufs=3)
-            product(ht, [(packed(0), v2_side[0]), (packed(1), v2_side[1])])
-            gv = ring.tile([P, HALF], F32, name="gv")
-            nc.vector.scalar_tensor_tensor(gv[:], hv[:], 0.0, gate[:], ALU.max, ALU.mult)
-            gt = ring.tile([P, HALF], F32, name="gt")
-            nc.vector.scalar_tensor_tensor(gt[:], ht[:], 0.0, rest[:], ALU.max, ALU.mult)
-            total = ring.tile([P, HALF], F32, name="total")
-            nc.gpsimd.tensor_tensor(total[:], gv[:], gt[:], ALU.add)
-            result = ring.tile([P, HALF], F32, name="result", bufs=3)
-            nc.gpsimd.tensor_tensor(result[:], total[:], weight[:, items], ALU.mult)
-            results[t, h] = result
+        order = [(0, 0), (1, 0), (0, 1), (1, 1), (2, 0), (3, 0), (2, 1), (3, 1)]
 
         rows_of = out_0.rearrange("(p t) c -> t p c", t=PACK)
-        pairs = [[held([P, 2, QUARTER], BF16, "pair%d_%d" % (u, q)) for q in range(4)] for u in range(2)]
-        woven = [held([P, QUARTER, PACK], BF16, "woven%d" % q) for q in range(4)]
+        text = {}
+        mixed = {}
 
-        def round_window(t, q, copy):
-            copy(pairs[t // 2][q][:, t % 2, :], windows[t][:, QUARTER * q : QUARTER * (q + 1)])
+        def sides(h):
+            items = slice(HALF * h, HALF * (h + 1))
+            v_side = (picked_words[:, items].bitcast(FP8X4), picked_scales[:, items])
+            v2_side = [
+                (parted[:, a, 2 * HALF * h : 2 * HALF * (h + 1)].bitcast(FP4X4), plane[:, items])
+                for a, plane in enumerate(planes2)
+            ]
+            return v_side, v2_side
 
-        def weave(u, q, copy):
-            copy(woven[q][:, :, 2 * u : 2 * u + 2], pairs[u][q][:].rearrange("p e c -> p c e"))
+        def text_part(s):
+            t, h = order[s]
+            v2_side = sides(h)[1]
+            packed = [
+                (wt_codes[:, a, P * t : P * (t + 1)].bitcast(FP8X4), wt_planes[:, N * a + P * t : N * a + P * (t + 1)]) for a in range(2)
+            ]
+            ht = psum.tile([P, HALF], F32, name="ht")
+            product(ht, [(packed[0], v2_side[0]), (packed[1], v2_side[1])])
+            at = held([P, HALF], F32, "at%d" % s)
+            nc.scalar.activation(at[:], ht[:], ACT.Relu)
+            text[s] = at
 
-        def place(t, h):
-            nc.vector.tensor_copy(windows[t][:].indirect(half_of(list1, h)), results[t, h][:])
+        diffs = {}
+
+        def picture_part(s):
+            t, h = order[s]
+            hv = psum.tile([P, HALF], F32, name="hv")
+            product(hv, [(quantised["wv", t], sides(h)[0])])
+            diffs[s] = held([P, HALF], F32, "diff%d" % s)[:]
+            nc.vector.scalar_tensor_tensor(diffs[s], hv[:], 0.0, text[s][:], ALU.max, ALU.subtract)
+
+        def front(s):
+            t, h = order[s]
+            v_side, v2_side = sides(h)
+            z = psum.tile([P, HALF], F32, name="z")
+            product(z, [(quantised["zv", t], v_side), (quantised["zt0", t], v2_side[0]), (quantised["zt1", t], v2_side[1])])
+            gate = held([P, HALF], F32, "gate%d" % s)
+            nc.scalar.activation(gate[:], z[:], ACT.Sigmoid, bias=bias[:, t : t + 1], scale=1.0)
+            diff = diffs[s]
+            if s == len(order) - 1:
+                gated = held([P, HALF], F32, "gated_last", tag="pair01")
+            else:
+                gated = ring.tile([P, HALF], F32, name="gated", bufs=3)
+            nc.gpsimd.tensor_tensor(gated[:], diff, gate[:], ALU.mult)
+            mixed[s] = gated
+
+        def back(s):
+            t, h = order[s]
+            summed = psum.tile([P, 4, P], F32, name="summed", bufs=1)
+            for c in range(4):
+                cols = slice(P * c, P * (c + 1))
+                nc.tensor.matmul(summed[:, c, :], lhsT=text[s][:, cols], rhs=ident[:], is_transpose=True, start=True, stop=False)
+                nc.tensor.matmul(summed[:, c, :], lhsT=mixed[s][:, cols], rhs=ident[:], is_transpose=True, start=False, stop=True)
+            weighted = ring.tile([P, 4, P], F32, name="weighted")
+            for c in range(4):
+                nc.scalar.activation(weighted[:, c, :], summed[:, c, :], ACT.Copy, scale=weight_cols[:, 4 * h + c : 4 * h + c + 1])
+            turned = psum.tile([P, 4, P], F32, name="turned", bufs=1)
+            for c in range(4):
+                nc.tensor.transpose(turned[:, c, :], weighted[:, c, :], ident[:])
+            result = ring.tile([P, HALF], F32, name="result", bufs=6)
+            nc.scalar.copy(result[:], turned[:].rearrange("p c j -> p (c j)"))
+            nc.vector.tensor_copy(windows[t][:].indirect(list1[:, 32 * h : 32 * h + 32]), result[:])
             if h == 1:
                 nc.sync.dma_start(rows_of[t], windows[t][:])
-                if t < PACK - 1:
-                    for q in range(4):
-                        round_window(t, q, nc.scalar.copy)
-                if t == 1:
-                    for q in range(4):
-                        weave(0, q, nc.scalar.copy)
 
-        order = [(0, 0), (1, 0), (0, 1), (1, 1), (2, 0), (2, 1), (3, 0), (3, 1)]
-        for i in range(2):
-            blend(*order[i], "gate")
-            blend(*order[i], "mix")
-        pick(1)
-        for i in range(2, len(order)):
-            blend(*order[i], "gate")
-        for i in range(len(order)):
-            place(*order[i])
-            if i + 2 < len(order):
-                blend(*order[i + 2], "mix")
+        def difference(s):
+            text_part(s)
+            picture_part(s)
+
+        difference(0)
+        front(0)
+        difference(1)
+        difference(2)
+        front(1)
+        difference(3)
+        quantise_weight("wv", 2, 4, nc.vector.tensor_copy)
+        back(0)
+        difference(4)
+        difference(5)
+        front(2)
+        difference(6)
+        difference(7)
+        for s in range(1, len(order)):
+            back(s)
+            if s + 2 < len(order):
+                front(s + 2)
+
+        def round_on_gpsimd(out, in_):
+            nc.gpsimd.tensor_scalar(out, in_, 1.0, -0.0, ALU.mult, ALU.add)
+
+        pair01 = held([P, 2, T], BF16, "pair01")
+        pair23 = [held([P, 2, QUARTER], BF16, "pair23_%d" % q)[:] for q in range(2)]
+        woven = [held([P, QUARTER, PACK], BF16, "woven%d" % q, tag="raw_" + names[q]) for q in range(4)]
+        quarters = [slice(QUARTER * q, QUARTER * (q + 1)) for q in range(4)]
+        for t in range(2):
+            round_on_gpsimd(pair01[:, t, :], windows[t][:])
+        for q in range(4):
+            nc.scalar.copy(woven[q][:, :, 0:2], pair01[:, :, quarters[q]].rearrange("p e c -> p c e"))
+        late = held([P, 2, 2, QUARTER], BF16, "pair23_late", tag="pair01")
+        pair23.extend([late[:, 0], late[:, 1]])
+        for q in range(4):
+            round_on_gpsimd(pair23[q][:, 0, :], windows[2][:, quarters[q]])
 
         out_scales = held([P, T], U8, "out_scales")
         words_view = table_view(out_1)
         for q in range(4):
             copy = nc.vector.tensor_copy if q < 2 else nc.scalar.copy
-            round_window(PACK - 1, q, copy)
-            weave(1, q, copy)
+            copy(pair23[q][:, 1, :], windows[3][:, quarters[q]])
+            copy(woven[q][:, :, 2:4], pair23[q].rearrange("p e c -> p c e"))
         for q in range(4):
-            cols = slice(QUARTER * q, QUARTER * (q + 1))
-            out_codes = held([P, QUARTER], U32, "out_codes%d" % q)
-            nc.vector.quantize_mx(out=out_codes[:].bitcast(FP8X4), scales=out_scales[:, cols], in_=woven[q][:].rearrange("p c t -> p (c t)"))
-            nc.sync.dma_start(words_view[:, cols], out_codes[:].bitcast(I32))
+            out_codes = held([P, QUARTER], U32, "out_codes%d" % q, tag="at%d" % q)
+            nc.vector.quantize_mx(out=out_codes[:].bitcast(FP8X4), scales=out_scales[:, quarters[q]], in_=woven[q][:].rearrange("p c t -> p (c t)"))
+            nc.sync.dma_start(words_view[:, quarters[q]], out_codes[:].bitcast(I32))
         for q in range(4):
             nc.scalar.dma_start(out_2[0, 4 * q : 4 * q + 4, :].bitcast(I32), out_scales[32 * q : 32 * q + 4, :].bitcast(I32))

@@ -45,25 +45,28 @@ def tile_list_gmu_relu_scatP_kernel(
         wt_scales_raw = held([P, 2 * N], U8, "wt_scales_raw")
         picked2_scales = held([P, J], U8, "picked2_scales")
         planes2 = [held([P, J], U8, "planes2_%d" % a) for a in range(2)]
-        windows = [held([P, T], F32, "window%d" % t) for t in range(PACK)]
-        names = ("zv", "zt0", "zt1", "wv")
+        names = ("wv", "zv", "zt0", "zt1")
         raw = {name: held([P, PACK, N], F32, "raw_" + name) for name in names}
         bias = held([P, PACK], F32, "bias")
         weight_cols = held([P, J // P], F32, "weight_cols")
         ident = held([P, P], F32, "ident")
 
+        warm = held([P, 2], F32, "warm")
+        nc.gpsimd.memset(warm[:, 0:1], 0.0)
+        nc.scalar.activation(warm[:, 1:2], warm[:, 0:1], ACT.Sigmoid)
+        nc.vector.memset(wt_scales_raw[:].bitcast(I32), 0)
         nc.vector.memset(v_scales[:].bitcast(I32), 0)
-        nc.gpsimd.memset(wt_scales_raw[:].bitcast(I32), 0)
         for q in range(4):
-            nc.vector.memset(v2_scales[32 * q : 32 * q + 24, :].bitcast(I32), 0)
+            nc.gpsimd.memset(v2_scales[32 * q : 32 * q + 24, :].bitcast(I32), 0)
         for tile in planes2:
-            nc.gpsimd.memset(tile[:].bitcast(I32), 0)
+            nc.vector.memset(tile[:].bitcast(I32), 0)
         make_identity(nc, ident[:])
-        warm = held([P, 1], F32, "warm")
-        nc.scalar.activation(warm[:], ident[:, 0:1], ACT.Sigmoid)
-        for t in range(PACK):
-            for s in range(2):
-                nc.gpsimd.memset(windows[t][:, 1024 * s : 1024 * (s + 1)], 0.0)
+        windows = {}
+
+        def open_window(t, tag=""):
+            windows[t] = held([P, T], F32, "window%d" % t, tag=tag)
+            nc.vector.memset(windows[t][:], 0.0)
+
 
         def table_view(words):
             return words[0].rearrange("p t i -> p (t i)").bitcast(I32)
@@ -79,30 +82,41 @@ def tile_list_gmu_relu_scatP_kernel(
             nc.sync.dma_start(v2_scales[32 * q + 24 : 32 * q + 32, :].bitcast(I32), tab2_scales[:, 4 * q : 4 * q + 4, :].bitcast(I32))
         load_table(v2_words, tab2_words)
         nc.sync.dma_start(list1[:], offs)
+        load_weight("wv", wv)
         load_weight("zv", zv)
-        load_table(v_words, tab_words)
-        for q in range(4):
-            nc.sync.dma_start(v_scales[32 * q : 32 * q + 4, :].bitcast(I32), tab_scales[0, 4 * q : 4 * q + 4, :].bitcast(I32))
-        load_weight("zt0", zt[0:512, :])
         nc.sync.dma_start(wt_raw[:], wt_words.rearrange("a p n i -> p a (n i)").bitcast(I32))
         for q in range(4):
             nc.sync.dma_start(
                 wt_scales_raw[32 * q : 32 * q + 4, :].bitcast(I32).rearrange("r (a n) -> r a n", a=2),
                 wt_scales[:, 4 * q : 4 * q + 4, :].bitcast(I32).rearrange("a r n -> r a n"),
             )
+        load_table(v_words, tab_words)
+        for q in range(4):
+            nc.sync.dma_start(v_scales[32 * q : 32 * q + 4, :].bitcast(I32), tab_scales[0, 4 * q : 4 * q + 4, :].bitcast(I32))
         nc.sync.dma_start(bias[:], b.rearrange("(p t) -> p t", t=PACK))
+        load_weight("zt0", zt[0:512, :])
         load_weight("zt1", zt[512:1024, :])
-        load_weight("wv", wv)
         with nc.allow_non_contiguous_dma(reason="one weight for each partition and block of items"):
             nc.sync.dma_start(weight_cols[:], wgo[0].rearrange("(c p) -> p c", p=P))
 
         nc.vector.tensor_copy(picked2_scales[:], v2_scales[:].indirect(list2[:]))
         for a in range(2):
-            nc.gpsimd.dma_start(planes2[a][0:100, :].bitcast(I32), picked2_scales[24 + 4 * a : 124 + 4 * a, :].bitcast(I32))
+            nc.scalar.dma_start(planes2[a][0:100, :].bitcast(I32), picked2_scales[24 + 4 * a : 124 + 4 * a, :].bitcast(I32))
         both = held([P, J], U32, "picked2_both")
         nc.vector.tensor_copy(both[:], v2_words[:].indirect(list2[:]))
         parted = held([P, 2, 2 * J], U8, "picked2_words")
         nc.vector.tensor_copy(parted[:].bitcast(U16), both[:].bitcast(U16).rearrange("p (j d) -> p d j", d=2))
+        wt_codes = [held([P, 2, 2, P], I32, "wt_codes%d" % u) for u in range(2)]
+        wt_planes = held([P, 2 * N], U8, "wt_planes")
+        nc.vector.tensor_copy(
+            wt_planes[:].rearrange("p (a t m) -> p a m t", a=2, t=PACK),
+            wt_scales_raw[:].rearrange("p (a m t) -> p a m t", a=2, t=PACK),
+        )
+        for u in range(2):
+            nc.vector.tensor_copy(
+                wt_codes[u][:].rearrange("p a t m -> p a m t"),
+                wt_raw[:].rearrange("p a (m t) -> p a m t", t=PACK)[:, :, :, 2 * u : 2 * u + 2],
+            )
         picked_words = held([P, J], U32, "picked_words")
         nc.vector.tensor_copy(picked_words[:], v_words[:].indirect(list1[:]))
         picked_scales = held([P, J], U8, "picked_scales")
@@ -110,9 +124,9 @@ def tile_list_gmu_relu_scatP_kernel(
 
         quantised = {}
 
-        def quantise_weight(name, t0, t1, copy):
+        def quantise_weight(name, t0, t1, copy, tag=""):
             count = t1 - t0
-            grouped = held([P, count, P, PACK], BF16, "grouped_%s%d" % (name, t0))
+            grouped = held([P, count, P, PACK], BF16, "grouped_%s%d" % (name, t0), tag=tag)
             copy(grouped[:].rearrange("p t m j -> p m j t"), raw[name][:].rearrange("p j (m t) -> p m j t", t=PACK)[:, :, :, t0:t1])
             codes = held([P, count * P], U32, "codes_%s%d" % (name, t0))
             scales = held([P, count * P], U8, "scales_%s%d" % (name, t0))
@@ -120,21 +134,6 @@ def tile_list_gmu_relu_scatP_kernel(
             for t in range(t0, t1):
                 cols = slice(P * (t - t0), P * (t - t0 + 1))
                 quantised[name, t] = (codes[:, cols].bitcast(FP8X4), scales[:, cols])
-
-        quantise_weight("zv", 0, 4, nc.scalar.copy)
-        wt_codes = held([P, 2, N], I32, "wt_codes")
-        wt_planes = held([P, 2 * N], U8, "wt_planes")
-        nc.vector.tensor_copy(
-            wt_codes[:].rearrange("p a (t m) -> p a m t", t=PACK), wt_raw[:].rearrange("p a (m t) -> p a m t", t=PACK)
-        )
-        nc.vector.tensor_copy(
-            wt_planes[:].rearrange("p (a t m) -> p a m t", a=2, t=PACK),
-            wt_scales_raw[:].rearrange("p (a m t) -> p a m t", a=2, t=PACK),
-        )
-
-        quantise_weight("zt0", 0, 4, nc.scalar.copy)
-        quantise_weight("zt1", 0, 4, nc.scalar.copy)
-        quantise_weight("wv", 0, 2, nc.vector.tensor_copy)
 
         def product(acc, passes):
             for i, (lhs, rhs) in enumerate(passes):
@@ -158,26 +157,28 @@ def tile_list_gmu_relu_scatP_kernel(
             ]
             return v_side, v2_side
 
-        def text_part(s):
+        def text_part(s, at):
             t, h = order[s]
             v2_side = sides(h)[1]
             packed = [
-                (wt_codes[:, a, P * t : P * (t + 1)].bitcast(FP8X4), wt_planes[:, N * a + P * t : N * a + P * (t + 1)]) for a in range(2)
+                (wt_codes[t // 2][:, a, t % 2, :].bitcast(FP8X4), wt_planes[:, N * a + P * t : N * a + P * (t + 1)]) for a in range(2)
             ]
-            ht = psum.tile([P, HALF], F32, name="ht")
+            if s in (2, 3):
+                ht = psum.tile([P, HALF], F32, name="ht_early", tag=("summed", "turned")[s - 2], bufs=1)
+            else:
+                ht = psum.tile([P, HALF], F32, name="ht")
             product(ht, [(packed[0], v2_side[0]), (packed[1], v2_side[1])])
-            at = held([P, HALF], F32, "at%d" % s)
-            nc.scalar.activation(at[:], ht[:], ACT.Relu)
+            nc.scalar.activation(at, ht[:], ACT.Relu)
             text[s] = at
 
         diffs = {}
 
-        def picture_part(s):
+        def picture_part(s, diff):
             t, h = order[s]
             hv = psum.tile([P, HALF], F32, name="hv")
             product(hv, [(quantised["wv", t], sides(h)[0])])
-            diffs[s] = held([P, HALF], F32, "diff%d" % s)[:]
-            nc.vector.scalar_tensor_tensor(diffs[s], hv[:], 0.0, text[s][:], ALU.max, ALU.subtract)
+            diffs[s] = diff
+            nc.vector.scalar_tensor_tensor(diffs[s], hv[:], 0.0, text[s], ALU.max, ALU.subtract)
 
         def front(s):
             t, h = order[s]
@@ -187,11 +188,8 @@ def tile_list_gmu_relu_scatP_kernel(
             gate = held([P, HALF], F32, "gate%d" % s)
             nc.scalar.activation(gate[:], z[:], ACT.Sigmoid, bias=bias[:, t : t + 1], scale=1.0)
             diff = diffs[s]
-            if s == len(order) - 1:
-                gated = held([P, HALF], F32, "gated_last", tag="pair01")
-            else:
-                gated = ring.tile([P, HALF], F32, name="gated", bufs=3)
-            nc.gpsimd.tensor_tensor(gated[:], diff, gate[:], ALU.mult)
+            gated = held([P, HALF], F32, "gated%d" % s)
+            nc.vector.tensor_tensor(gated[:], diff, gate[:], ALU.mult)
             mixed[s] = gated
 
         def back(s):
@@ -201,55 +199,58 @@ def tile_list_gmu_relu_scatP_kernel(
                 cols = slice(P * c, P * (c + 1))
                 nc.tensor.matmul(summed[:, c, :], lhsT=text[s][:, cols], rhs=ident[:], is_transpose=True, start=True, stop=False)
                 nc.tensor.matmul(summed[:, c, :], lhsT=mixed[s][:, cols], rhs=ident[:], is_transpose=True, start=False, stop=True)
-            weighted = ring.tile([P, 4, P], F32, name="weighted")
+            if s == len(order) - 1:
+                weighted = held([P, 4, P], F32, "weighted_last", tag="pair01")
+            else:
+                weighted = ring.tile([P, 4, P], F32, name="weighted")
             for c in range(4):
                 nc.scalar.activation(weighted[:, c, :], summed[:, c, :], ACT.Copy, scale=weight_cols[:, 4 * h + c : 4 * h + c + 1])
             turned = psum.tile([P, 4, P], F32, name="turned", bufs=1)
             for c in range(4):
                 nc.tensor.transpose(turned[:, c, :], weighted[:, c, :], ident[:])
-            result = ring.tile([P, HALF], F32, name="result", bufs=6)
+            result = ring.tile([P, HALF], F32, name="result", bufs=8)
             nc.scalar.copy(result[:], turned[:].rearrange("p c j -> p (c j)"))
             nc.vector.tensor_copy(windows[t][:].indirect(list1[:, 32 * h : 32 * h + 32]), result[:])
             if h == 1:
                 nc.sync.dma_start(rows_of[t], windows[t][:])
 
-        def difference(s):
-            text_part(s)
-            picture_part(s)
+        def two(name, tag=""):
+            both_steps = held([P, 2, HALF], F32, name, tag=tag)
+            return both_steps[:, 0, :], both_steps[:, 1, :]
 
-        difference(0)
+        quantise_weight("wv", 0, 4, nc.scalar.copy)
+        quantise_weight("zv", 0, 4, nc.scalar.copy)
+        for s, at in enumerate(two("at01") + two("at23")):
+            text_part(s, at)
+        for s, diff in enumerate(two("diff01") + two("diff23")):
+            picture_part(s, diff)
+        quantise_weight("zt0", 0, 4, nc.scalar.copy)
+        quantise_weight("zt1", 0, 4, nc.scalar.copy)
         front(0)
-        difference(1)
-        difference(2)
         front(1)
-        difference(3)
-        quantise_weight("wv", 2, 4, nc.vector.tensor_copy)
-        back(0)
-        difference(4)
-        difference(5)
-        front(2)
-        difference(6)
-        difference(7)
-        for s in range(1, len(order)):
+        for s, (at, diff) in enumerate(zip(two("at45") + two("at67"), two("diff45") + two("diff67"))):
+            text_part(4 + s, at)
+            picture_part(4 + s, diff)
+        for s in range(2, len(order)):
+            front(s)
+        open_window(0, "raw_wv")
+        open_window(1, "raw_zv")
+        open_window(2, "raw_zt0")
+        open_window(3, "raw_zt1")
+        for s in range(len(order)):
             back(s)
-            if s + 2 < len(order):
-                front(s + 2)
-
-        def round_on_gpsimd(out, in_):
-            nc.gpsimd.tensor_scalar(out, in_, 1.0, -0.0, ALU.mult, ALU.add)
 
         pair01 = held([P, 2, T], BF16, "pair01")
-        pair23 = [held([P, 2, QUARTER], BF16, "pair23_%d" % q)[:] for q in range(2)]
-        woven = [held([P, QUARTER, PACK], BF16, "woven%d" % q, tag="raw_" + names[q]) for q in range(4)]
+        woven_tags = ("picked2_both", "wt_raw", "grouped_wv0", "grouped_zv0")
+        woven = [held([P, QUARTER, PACK], BF16, "woven%d" % q, tag=woven_tags[q]) for q in range(4)]
         quarters = [slice(QUARTER * q, QUARTER * (q + 1)) for q in range(4)]
         for t in range(2):
-            round_on_gpsimd(pair01[:, t, :], windows[t][:])
+            nc.scalar.copy(pair01[:, t, :], windows[t][:])
         for q in range(4):
             nc.scalar.copy(woven[q][:, :, 0:2], pair01[:, :, quarters[q]].rearrange("p e c -> p c e"))
-        late = held([P, 2, 2, QUARTER], BF16, "pair23_late", tag="pair01")
-        pair23.extend([late[:, 0], late[:, 1]])
-        for q in range(4):
-            round_on_gpsimd(pair23[q][:, 0, :], windows[2][:, quarters[q]])
+        late = held([P, 4, 2, QUARTER], BF16, "pair23", tag="pair01")
+        pair23 = [late[:, q] for q in range(4)]
+        nc.scalar.copy(late[:, :, 0, :], windows[2][:].rearrange("p (q c) -> p q c", q=4))
 
         out_scales = held([P, T], U8, "out_scales")
         words_view = table_view(out_1)
@@ -258,7 +259,7 @@ def tile_list_gmu_relu_scatP_kernel(
             copy(pair23[q][:, 1, :], windows[3][:, quarters[q]])
             copy(woven[q][:, :, 2:4], pair23[q].rearrange("p e c -> p c e"))
         for q in range(4):
-            out_codes = held([P, QUARTER], U32, "out_codes%d" % q, tag="at%d" % q)
+            out_codes = held([P, QUARTER], U32, "out_codes%d" % q, tag=("v_words", "v2_words", "", "")[q])
             nc.vector.quantize_mx(out=out_codes[:].bitcast(FP8X4), scales=out_scales[:, quarters[q]], in_=woven[q][:].rearrange("p c t -> p (c t)"))
             nc.sync.dma_start(words_view[:, quarters[q]], out_codes[:].bitcast(I32))
         for q in range(4):

@@ -61,12 +61,7 @@ def tile_list_gmu_relu_scatP_kernel(
         for tile in planes2:
             nc.vector.memset(tile[:].bitcast(I32), 0)
         make_identity(nc, ident[:])
-        windows = {}
-
-        def open_window(t, tag=""):
-            windows[t] = held([P, T], F32, "window%d" % t, tag=tag)
-            nc.vector.memset(windows[t][:], 0.0)
-
+        windows = [held([P, T], F32, "window%d" % t) for t in range(PACK)]
 
         def table_view(words):
             return words[0].rearrange("p t i -> p (t i)").bitcast(I32)
@@ -101,7 +96,10 @@ def tile_list_gmu_relu_scatP_kernel(
 
         nc.vector.tensor_copy(picked2_scales[:], v2_scales[:].indirect(list2[:]))
         for a in range(2):
-            nc.scalar.dma_start(planes2[a][0:100, :].bitcast(I32), picked2_scales[24 + 4 * a : 124 + 4 * a, :].bitcast(I32))
+            nc.gpsimd.dma_start(planes2[a][0:100, :].bitcast(I32), picked2_scales[24 + 4 * a : 124 + 4 * a, :].bitcast(I32))
+        for t in range(PACK):
+            for s in range(2):
+                nc.gpsimd.memset(windows[t][:, 1024 * s : 1024 * (s + 1)], 0.0)
         both = held([P, J], U32, "picked2_both")
         nc.vector.tensor_copy(both[:], v2_words[:].indirect(list2[:]))
         parted = held([P, 2, 2 * J], U8, "picked2_words")
@@ -164,7 +162,7 @@ def tile_list_gmu_relu_scatP_kernel(
                 (wt_codes[t // 2][:, a, t % 2, :].bitcast(FP8X4), wt_planes[:, N * a + P * t : N * a + P * (t + 1)]) for a in range(2)
             ]
             if s in (2, 3):
-                ht = psum.tile([P, HALF], F32, name="ht_early", tag=("summed", "turned")[s - 2], bufs=1)
+                ht = psum.tile([P, HALF], F32, name="ht_early", tag="z", bufs=4)
             else:
                 ht = psum.tile([P, HALF], F32, name="ht")
             product(ht, [(packed[0], v2_side[0]), (packed[1], v2_side[1])])
@@ -183,32 +181,30 @@ def tile_list_gmu_relu_scatP_kernel(
         def front(s):
             t, h = order[s]
             v_side, v2_side = sides(h)
-            z = psum.tile([P, HALF], F32, name="z")
+            z = psum.tile([P, HALF], F32, name="z", bufs=4)
             product(z, [(quantised["zv", t], v_side), (quantised["zt0", t], v2_side[0]), (quantised["zt1", t], v2_side[1])])
             gate = held([P, HALF], F32, "gate%d" % s)
             nc.scalar.activation(gate[:], z[:], ACT.Sigmoid, bias=bias[:, t : t + 1], scale=1.0)
             diff = diffs[s]
-            gated = held([P, HALF], F32, "gated%d" % s)
-            nc.vector.tensor_tensor(gated[:], diff, gate[:], ALU.mult)
+            gated = held([P, HALF], F32, "gated%d" % s, tag="pair01" if s == len(order) - 1 else "")
+            engine = nc.vector if s == 0 else nc.gpsimd
+            engine.tensor_tensor(gated[:], diff, gate[:], ALU.mult)
             mixed[s] = gated
 
         def back(s):
             t, h = order[s]
-            summed = psum.tile([P, 4, P], F32, name="summed", bufs=1)
+            summed = psum.tile([P, 4, P], F32, name="summed", tag="ht")
             for c in range(4):
                 cols = slice(P * c, P * (c + 1))
                 nc.tensor.matmul(summed[:, c, :], lhsT=text[s][:, cols], rhs=ident[:], is_transpose=True, start=True, stop=False)
                 nc.tensor.matmul(summed[:, c, :], lhsT=mixed[s][:, cols], rhs=ident[:], is_transpose=True, start=False, stop=True)
-            if s == len(order) - 1:
-                weighted = held([P, 4, P], F32, "weighted_last", tag="pair01")
-            else:
-                weighted = ring.tile([P, 4, P], F32, name="weighted")
+            weighted = ring.tile([P, 4, P], F32, name="weighted", bufs=3)
             for c in range(4):
                 nc.scalar.activation(weighted[:, c, :], summed[:, c, :], ACT.Copy, scale=weight_cols[:, 4 * h + c : 4 * h + c + 1])
-            turned = psum.tile([P, 4, P], F32, name="turned", bufs=1)
+            turned = psum.tile([P, 4, P], F32, name="turned", tag="hv")
             for c in range(4):
                 nc.tensor.transpose(turned[:, c, :], weighted[:, c, :], ident[:])
-            result = ring.tile([P, HALF], F32, name="result", bufs=8)
+            result = ring.tile([P, HALF], F32, name="result", bufs=7)
             nc.scalar.copy(result[:], turned[:].rearrange("p c j -> p (c j)"))
             nc.vector.tensor_copy(windows[t][:].indirect(list1[:, 32 * h : 32 * h + 32]), result[:])
             if h == 1:
@@ -220,37 +216,40 @@ def tile_list_gmu_relu_scatP_kernel(
 
         quantise_weight("wv", 0, 4, nc.scalar.copy)
         quantise_weight("zv", 0, 4, nc.scalar.copy)
-        for s, at in enumerate(two("at01") + two("at23")):
+        for s, at in enumerate(two("at01")):
             text_part(s, at)
-        for s, diff in enumerate(two("diff01") + two("diff23")):
-            picture_part(s, diff)
         quantise_weight("zt0", 0, 4, nc.scalar.copy)
-        quantise_weight("zt1", 0, 4, nc.scalar.copy)
+        quantise_weight("zt1", 0, 2, nc.vector.tensor_copy)
+        first = two("diff01", "grouped_zt10") + two("diff23")
+        picture_part(0, first[0])
         front(0)
+        quantise_weight("zt1", 2, 4, nc.vector.tensor_copy)
+        picture_part(1, first[1])
         front(1)
-        for s, (at, diff) in enumerate(zip(two("at45") + two("at67"), two("diff45") + two("diff67"))):
-            text_part(4 + s, at)
-            picture_part(4 + s, diff)
-        for s in range(2, len(order)):
-            front(s)
-        open_window(0, "raw_wv")
-        open_window(1, "raw_zv")
-        open_window(2, "raw_zt0")
-        open_window(3, "raw_zt1")
+        held_back = held([P, 4, HALF], F32, "at2345", tag="raw_zt0")
+        later_texts = tuple(held_back[:, i, :] for i in range(4)) + two("at67")
+        for s, (at, diff) in enumerate(zip(later_texts, first[2:] + two("diff45") + two("diff67"))):
+            text_part(2 + s, at)
+            picture_part(2 + s, diff)
         for s in range(len(order)):
             back(s)
+            if s + 2 < len(order):
+                front(s + 2)
+
+        def round_on_gpsimd(out, in_):
+            nc.gpsimd.tensor_scalar(out, in_, 1.0, -0.0, ALU.mult, ALU.add)
 
         pair01 = held([P, 2, T], BF16, "pair01")
-        woven_tags = ("picked2_both", "wt_raw", "grouped_wv0", "grouped_zv0")
+        woven_tags = ("raw_wv", "raw_zv", "raw_zt0", "raw_zt1")
         woven = [held([P, QUARTER, PACK], BF16, "woven%d" % q, tag=woven_tags[q]) for q in range(4)]
         quarters = [slice(QUARTER * q, QUARTER * (q + 1)) for q in range(4)]
         for t in range(2):
-            nc.scalar.copy(pair01[:, t, :], windows[t][:])
+            round_on_gpsimd(pair01[:, t, :], windows[t][:])
         for q in range(4):
             nc.scalar.copy(woven[q][:, :, 0:2], pair01[:, :, quarters[q]].rearrange("p e c -> p c e"))
         late = held([P, 4, 2, QUARTER], BF16, "pair23", tag="pair01")
         pair23 = [late[:, q] for q in range(4)]
-        nc.scalar.copy(late[:, :, 0, :], windows[2][:].rearrange("p (q c) -> p q c", q=4))
+        round_on_gpsimd(late[:, :, 0, :], windows[2][:].rearrange("p (q c) -> p q c", q=4))
 
         out_scales = held([P, T], U8, "out_scales")
         words_view = table_view(out_1)
@@ -259,7 +258,7 @@ def tile_list_gmu_relu_scatP_kernel(
             copy(pair23[q][:, 1, :], windows[3][:, quarters[q]])
             copy(woven[q][:, :, 2:4], pair23[q].rearrange("p e c -> p c e"))
         for q in range(4):
-            out_codes = held([P, QUARTER], U32, "out_codes%d" % q, tag=("v_words", "v2_words", "", "")[q])
+            out_codes = held([P, QUARTER], U32, "out_codes%d" % q, tag=("v_words", "v2_words", "picked2_both", "wt_raw")[q])
             nc.vector.quantize_mx(out=out_codes[:].bitcast(FP8X4), scales=out_scales[:, quarters[q]], in_=woven[q][:].rearrange("p c t -> p (c t)"))
             nc.sync.dma_start(words_view[:, quarters[q]], out_codes[:].bitcast(I32))
         for q in range(4):

@@ -29,7 +29,6 @@ def tile_list_gmu_relu_scatP_kernel(
     nc = tc.nc
     with ExitStack() as ctx:
         keep = ctx.enter_context(tc.tile_pool(name="keep", bufs=1))
-        ring = ctx.enter_context(tc.tile_pool(name="ring", bufs=2))
         psum = ctx.enter_context(tc.psum_pool(name="psum", bufs=2))
 
         def held(shape, dtype, name, tag=""):
@@ -48,7 +47,9 @@ def tile_list_gmu_relu_scatP_kernel(
         names = ("wv", "zv", "zt0", "zt1")
         raw = {name: held([P, PACK, N], F32, "raw_" + name) for name in names}
         bias = held([P, PACK], F32, "bias")
+        weight_rows = held([P, P], F32, "weight_rows")
         weight_cols = held([P, J // P], F32, "weight_cols")
+        weight = held([P, J], F32, "weight")
         ident = held([P, P], F32, "ident")
 
         warm = held([P, 2], F32, "warm")
@@ -60,8 +61,16 @@ def tile_list_gmu_relu_scatP_kernel(
             nc.gpsimd.memset(v2_scales[32 * q : 32 * q + 24, :].bitcast(I32), 0)
         for tile in planes2:
             nc.vector.memset(tile[:].bitcast(I32), 0)
+        nc.gpsimd.memset(weight_rows[:], 0.0)
         make_identity(nc, ident[:])
-        windows = [held([P, T], F32, "window%d" % t) for t in range(PACK)]
+        windows = {}
+
+        def open_window(t, pieces, tag=""):
+            windows[t] = held([P, T], F32, "window%d" % t, tag=tag)
+            for s in range(pieces):
+                nc.gpsimd.memset(windows[t][:, T // pieces * s : T // pieces * (s + 1)], 0.0)
+
+        open_window(0, 1)
 
         def table_view(words):
             return words[0].rearrange("p t i -> p (t i)").bitcast(I32)
@@ -91,15 +100,14 @@ def tile_list_gmu_relu_scatP_kernel(
         nc.sync.dma_start(bias[:], b.rearrange("(p t) -> p t", t=PACK))
         load_weight("zt0", zt[0:512, :])
         load_weight("zt1", zt[512:1024, :])
-        with nc.allow_non_contiguous_dma(reason="one weight for each partition and block of items"):
-            nc.sync.dma_start(weight_cols[:], wgo[0].rearrange("(c p) -> p c", p=P))
+        nc.sync.dma_start(weight_rows[0 : J // P, :], wgo[0].rearrange("(c p) -> c p", p=P))
+        nc.sync.dma_start(weight[:], wgo)
 
         nc.vector.tensor_copy(picked2_scales[:], v2_scales[:].indirect(list2[:]))
         for a in range(2):
             nc.gpsimd.dma_start(planes2[a][0:100, :].bitcast(I32), picked2_scales[24 + 4 * a : 124 + 4 * a, :].bitcast(I32))
-        for t in range(PACK):
-            for s in range(2):
-                nc.gpsimd.memset(windows[t][:, 1024 * s : 1024 * (s + 1)], 0.0)
+        for t in range(1, PACK):
+            open_window(t, 4)
         both = held([P, J], U32, "picked2_both")
         nc.vector.tensor_copy(both[:], v2_words[:].indirect(list2[:]))
         parted = held([P, 2, 2 * J], U8, "picked2_words")
@@ -144,6 +152,8 @@ def tile_list_gmu_relu_scatP_kernel(
 
         rows_of = out_0.rearrange("(p t) c -> t p c", t=PACK)
         text = {}
+        totals = []
+        woven_tags = ("raw_wv", "raw_zv", "grouped_zt00", "raw_zt1")
         mixed = {}
 
         def sides(h):
@@ -186,26 +196,37 @@ def tile_list_gmu_relu_scatP_kernel(
             gate = held([P, HALF], F32, "gate%d" % s)
             nc.scalar.activation(gate[:], z[:], ACT.Sigmoid, bias=bias[:, t : t + 1], scale=1.0)
             diff = diffs[s]
-            gated = held([P, HALF], F32, "gated%d" % s, tag="pair01" if s == len(order) - 1 else "")
-            engine = nc.vector if s == 0 else nc.gpsimd
+            gated = held([P, HALF], F32, "gated%d" % s)
+            engine = nc.vector if s < 2 else nc.gpsimd
             engine.tensor_tensor(gated[:], diff, gate[:], ALU.mult)
             mixed[s] = gated
 
-        def back(s):
-            t, h = order[s]
+        def finish_by_transposes(s, result):
+            h = order[s][1]
             summed = psum.tile([P, 4, P], F32, name="summed", tag="ht")
             for c in range(4):
                 cols = slice(P * c, P * (c + 1))
                 nc.tensor.matmul(summed[:, c, :], lhsT=text[s][:, cols], rhs=ident[:], is_transpose=True, start=True, stop=False)
                 nc.tensor.matmul(summed[:, c, :], lhsT=mixed[s][:, cols], rhs=ident[:], is_transpose=True, start=False, stop=True)
-            weighted = ring.tile([P, 4, P], F32, name="weighted", bufs=3)
+            weighted = held([P, 4, P], F32, "weighted%d" % s)
             for c in range(4):
                 nc.scalar.activation(weighted[:, c, :], summed[:, c, :], ACT.Copy, scale=weight_cols[:, 4 * h + c : 4 * h + c + 1])
             turned = psum.tile([P, 4, P], F32, name="turned", tag="hv")
             for c in range(4):
                 nc.tensor.transpose(turned[:, c, :], weighted[:, c, :], ident[:])
-            result = ring.tile([P, HALF], F32, name="result", bufs=7)
             nc.scalar.copy(result[:], turned[:].rearrange("p c j -> p (c j)"))
+
+        def finish_on_gpsimd(s, result):
+            h = order[s][1]
+            if s % 2 == 0:
+                totals.extend(two("total%d_%d" % (s, s + 1), "gated3"))
+            nc.gpsimd.tensor_tensor(totals[s - 4], mixed[s][:], text[s], ALU.add)
+            nc.gpsimd.tensor_tensor(result[:], totals[s - 4], weight[:, HALF * h : HALF * (h + 1)], ALU.mult)
+
+        def back(s):
+            t, h = order[s]
+            result = held([P, HALF], F32, "result%d" % s, tag="gate%d" % s)
+            (finish_by_transposes if s < 4 else finish_on_gpsimd)(s, result)
             nc.vector.tensor_copy(windows[t][:].indirect(list1[:, 32 * h : 32 * h + 32]), result[:])
             if h == 1:
                 nc.sync.dma_start(rows_of[t], windows[t][:])
@@ -218,6 +239,9 @@ def tile_list_gmu_relu_scatP_kernel(
         quantise_weight("zv", 0, 4, nc.scalar.copy)
         for s, at in enumerate(two("at01")):
             text_part(s, at)
+        turned_weight = psum.tile([P, P], F32, name="turned_weight", tag="ht")
+        nc.tensor.transpose(turned_weight[:], weight_rows[:], ident[:])
+        nc.scalar.copy(weight_cols[:], turned_weight[:, 0 : J // P])
         quantise_weight("zt0", 0, 4, nc.scalar.copy)
         quantise_weight("zt1", 0, 2, nc.vector.tensor_copy)
         first = two("diff01", "grouped_zt10") + two("diff23")
@@ -233,21 +257,23 @@ def tile_list_gmu_relu_scatP_kernel(
             picture_part(2 + s, diff)
         for s in range(len(order)):
             back(s)
-            if s + 2 < len(order):
-                front(s + 2)
+            if s in (0, 1, 5):
+                first_of_pair = {0: 2, 1: 4, 5: 6}[s]
+                front(first_of_pair)
+                front(first_of_pair + 1)
 
         def round_on_gpsimd(out, in_):
             nc.gpsimd.tensor_scalar(out, in_, 1.0, -0.0, ALU.mult, ALU.add)
 
-        pair01 = held([P, 2, T], BF16, "pair01")
-        woven_tags = ("raw_wv", "raw_zv", "raw_zt0", "raw_zt1")
+        pair01 = held([P, 2, T], BF16, "pair01", tag="weighted3")
         woven = [held([P, QUARTER, PACK], BF16, "woven%d" % q, tag=woven_tags[q]) for q in range(4)]
         quarters = [slice(QUARTER * q, QUARTER * (q + 1)) for q in range(4)]
         for t in range(2):
-            round_on_gpsimd(pair01[:, t, :], windows[t][:])
+            for s in range(2):
+                nc.scalar.copy(pair01[:, t, 1024 * s : 1024 * (s + 1)], windows[t][:, 1024 * s : 1024 * (s + 1)])
         for q in range(4):
             nc.scalar.copy(woven[q][:, :, 0:2], pair01[:, :, quarters[q]].rearrange("p e c -> p c e"))
-        late = held([P, 4, 2, QUARTER], BF16, "pair23", tag="pair01")
+        late = held([P, 4, 2, QUARTER], BF16, "pair23", tag="gated3")
         pair23 = [late[:, q] for q in range(4)]
         round_on_gpsimd(late[:, :, 0, :], windows[2][:].rearrange("p (q c) -> p q c", q=4))
 

@@ -58,9 +58,9 @@ def tile_list_gmu_relu_scatP_kernel(
         nc.vector.memset(wt_scales_raw[:].bitcast(I32), 0)
         nc.vector.memset(v_scales[:].bitcast(I32), 0)
         for q in range(4):
-            nc.gpsimd.memset(v2_scales[32 * q : 32 * q + 24, :].bitcast(I32), 0)
+            (nc.gpsimd, nc.vector)[q % 2].memset(v2_scales[32 * q : 32 * q + 24, :].bitcast(I32), 0)
         for tile in planes2:
-            nc.vector.memset(tile[:].bitcast(I32), 0)
+            nc.gpsimd.memset(tile[:].bitcast(I32), 0)
         nc.gpsimd.memset(weight_rows[:], 0.0)
         make_identity(nc, ident[:])
         windows = {}
@@ -106,23 +106,20 @@ def tile_list_gmu_relu_scatP_kernel(
         nc.vector.tensor_copy(picked2_scales[:], v2_scales[:].indirect(list2[:]))
         for a in range(2):
             nc.gpsimd.dma_start(planes2[a][0:100, :].bitcast(I32), picked2_scales[24 + 4 * a : 124 + 4 * a, :].bitcast(I32))
-        for t in range(1, PACK):
-            open_window(t, 4)
         both = held([P, J], U32, "picked2_both")
         nc.vector.tensor_copy(both[:], v2_words[:].indirect(list2[:]))
         parted = held([P, 2, 2 * J], U8, "picked2_words")
         nc.vector.tensor_copy(parted[:].bitcast(U16), both[:].bitcast(U16).rearrange("p (j d) -> p d j", d=2))
-        wt_codes = [held([P, 2, 2, P], I32, "wt_codes%d" % u) for u in range(2)]
+        wt_codes = held([P, 2, N], I32, "wt_codes")
         wt_planes = held([P, 2 * N], U8, "wt_planes")
         nc.vector.tensor_copy(
-            wt_planes[:].rearrange("p (a t m) -> p a m t", a=2, t=PACK),
-            wt_scales_raw[:].rearrange("p (a m t) -> p a m t", a=2, t=PACK),
+            wt_codes[:].rearrange("p a (t m) -> p a m t", t=PACK), wt_raw[:].rearrange("p a (m t) -> p a m t", t=PACK)
         )
-        for u in range(2):
-            nc.vector.tensor_copy(
-                wt_codes[u][:].rearrange("p a t m -> p a m t"),
-                wt_raw[:].rearrange("p a (m t) -> p a m t", t=PACK)[:, :, :, 2 * u : 2 * u + 2],
-            )
+        nc.vector.tensor_copy(
+            wt_planes[:].rearrange("p (a t m) -> p a t m", a=2, t=PACK),
+            wt_scales_raw[:].rearrange("p (a m t) -> p a t m", a=2, t=PACK),
+        )
+        open_window(1, 4, "wt_scales_raw")
         picked_words = held([P, J], U32, "picked_words")
         nc.vector.tensor_copy(picked_words[:], v_words[:].indirect(list1[:]))
         picked_scales = held([P, J], U8, "picked_scales")
@@ -169,7 +166,7 @@ def tile_list_gmu_relu_scatP_kernel(
             t, h = order[s]
             v2_side = sides(h)[1]
             packed = [
-                (wt_codes[t // 2][:, a, t % 2, :].bitcast(FP8X4), wt_planes[:, N * a + P * t : N * a + P * (t + 1)]) for a in range(2)
+                (wt_codes[:, a, P * t : P * (t + 1)].bitcast(FP8X4), wt_planes[:, N * a + P * t : N * a + P * (t + 1)]) for a in range(2)
             ]
             if s in (2, 3):
                 ht = psum.tile([P, HALF], F32, name="ht_early", tag="z", bufs=4)
@@ -223,10 +220,15 @@ def tile_list_gmu_relu_scatP_kernel(
             nc.gpsimd.tensor_tensor(totals[s - 4], mixed[s][:], text[s], ALU.add)
             nc.gpsimd.tensor_tensor(result[:], totals[s - 4], weight[:, HALF * h : HALF * (h + 1)], ALU.mult)
 
+        def finish_first(s, result):
+            total = held([P, HALF], F32, "total_first")
+            nc.vector.tensor_tensor(total[:], mixed[s][:], text[s], ALU.add)
+            nc.gpsimd.tensor_tensor(result[:], total[:], weight[:, 0:HALF], ALU.mult)
+
         def back(s):
             t, h = order[s]
             result = held([P, HALF], F32, "result%d" % s, tag="gate%d" % s)
-            (finish_by_transposes if s < 4 else finish_on_gpsimd)(s, result)
+            (finish_first if s == 0 else finish_by_transposes if s < 4 else finish_on_gpsimd)(s, result)
             nc.vector.tensor_copy(windows[t][:].indirect(list1[:, 32 * h : 32 * h + 32]), result[:])
             if h == 1:
                 nc.sync.dma_start(rows_of[t], windows[t][:])
@@ -237,6 +239,7 @@ def tile_list_gmu_relu_scatP_kernel(
 
         quantise_weight("wv", 0, 4, nc.scalar.copy)
         quantise_weight("zv", 0, 4, nc.scalar.copy)
+        open_window(2, 4, "grouped_zv0")
         for s, at in enumerate(two("at01")):
             text_part(s, at)
         turned_weight = psum.tile([P, P], F32, name="turned_weight", tag="ht")
@@ -256,6 +259,8 @@ def tile_list_gmu_relu_scatP_kernel(
             text_part(2 + s, at)
             picture_part(2 + s, diff)
         for s in range(len(order)):
+            if s == 5:
+                open_window(3, 4, "gated1")
             back(s)
             if s in (0, 1, 5):
                 first_of_pair = {0: 2, 1: 4, 5: 6}[s]

@@ -20,7 +20,19 @@ ACT = mybir.ActivationFunctionType
 P = 128
 PACK = 4
 HALF = 512
-QUARTER = 512
+BLOCKS = HALF // P
+QUADRANT = 32
+QUARTER = T // 4
+LIST_COLS = HALF // 16
+
+LOADED_ROW = QUADRANT - 8
+MOVED_ROWS = 3 * QUADRANT + 4
+
+STEPS = [(0, 0), (1, 0), (0, 1), (1, 1), (2, 0), (3, 0), (2, 1), (3, 1)]
+FIRST_GPSIMD_STEP = 4
+VECTOR_PRODUCTS = 2
+PIECES = [slice(0, 512), slice(512, 1024), slice(1024, 1536), slice(1536, 1792), slice(1792, 2048)]
+VECTOR_PIECES = 2
 
 
 def tile_list_gmu_relu_scatP_kernel(
@@ -34,6 +46,10 @@ def tile_list_gmu_relu_scatP_kernel(
         def held(shape, dtype, name, tag=""):
             return keep.tile(shape, dtype, name=name, tag=tag or name, align_bytes=64)
 
+        def two(name, tag=""):
+            both_steps = held([P, 2, HALF], F32, name, tag=tag)
+            return both_steps[:, 0, :], both_steps[:, 1, :]
+
         list1 = keep.tile([P, J // 16], U16, name="list1")
         list2 = keep.tile([P, J // 16], U16, name="list2")
         v_words = held([P, T], U32, "v_words")
@@ -44,8 +60,7 @@ def tile_list_gmu_relu_scatP_kernel(
         wt_scales_raw = held([P, 2 * N], U8, "wt_scales_raw")
         picked2_scales = held([P, J], U8, "picked2_scales")
         planes2 = [held([P, J], U8, "planes2_%d" % a) for a in range(2)]
-        names = ("wv", "zv", "zt0", "zt1")
-        raw = {name: held([P, PACK, N], F32, "raw_" + name) for name in names}
+        raw = {name: held([P, PACK, N], F32, "raw_" + name) for name in ("wv", "zv", "zt0", "zt1")}
         bias = held([P, PACK], F32, "bias")
         weight_rows = held([P, P], F32, "weight_rows")
         weight_cols = held([P, J // P], F32, "weight_cols")
@@ -55,48 +70,50 @@ def tile_list_gmu_relu_scatP_kernel(
         warm = held([P, 2], F32, "warm")
         nc.gpsimd.memset(warm[:, 0:1], 0.0)
         nc.scalar.activation(warm[:, 1:2], warm[:, 0:1], ACT.Sigmoid)
+
         nc.vector.memset(wt_scales_raw[:].bitcast(I32), 0)
         nc.vector.memset(v_scales[:].bitcast(I32), 0)
         for q in range(4):
-            (nc.gpsimd, nc.vector)[q % 2].memset(v2_scales[32 * q : 32 * q + 24, :].bitcast(I32), 0)
-        for tile in planes2:
-            nc.gpsimd.memset(tile[:].bitcast(I32), 0)
+            (nc.gpsimd, nc.vector)[q % 2].memset(v2_scales[QUADRANT * q : QUADRANT * q + LOADED_ROW, :].bitcast(I32), 0)
+        for plane in planes2:
+            nc.gpsimd.memset(plane[:].bitcast(I32), 0)
         nc.gpsimd.memset(weight_rows[:], 0.0)
         make_identity(nc, ident[:])
+
         windows = {}
 
-        def open_window(t, pieces, tag=""):
+        def open_window(t, parts, tag=""):
             windows[t] = held([P, T], F32, "window%d" % t, tag=tag)
-            for s in range(pieces):
-                nc.gpsimd.memset(windows[t][:, T // pieces * s : T // pieces * (s + 1)], 0.0)
+            for i in range(parts):
+                nc.gpsimd.memset(windows[t][:, T // parts * i : T // parts * (i + 1)], 0.0)
 
         open_window(0, 1)
 
-        def table_view(words):
+        def words_view(words):
             return words[0].rearrange("p t i -> p (t i)").bitcast(I32)
 
-        def load_table(tile, words):
-            nc.sync.dma_start(tile[:].bitcast(I32), table_view(words))
+        def scale_rows(tile, q, first, count):
+            return tile[QUADRANT * q + first : QUADRANT * q + first + count, :].bitcast(I32)
 
         def load_weight(name, rows):
             nc.sync.dma_start(raw[name][:], rows.rearrange("(p j) n -> p j n", j=PACK))
 
         nc.sync.dma_start(list2[:], offs2)
         for q in range(4):
-            nc.sync.dma_start(v2_scales[32 * q + 24 : 32 * q + 32, :].bitcast(I32), tab2_scales[:, 4 * q : 4 * q + 4, :].bitcast(I32))
-        load_table(v2_words, tab2_words)
+            nc.sync.dma_start(scale_rows(v2_scales, q, LOADED_ROW, 8), tab2_scales[:, 4 * q : 4 * q + 4, :].bitcast(I32))
+        nc.sync.dma_start(v2_words[:].bitcast(I32), words_view(tab2_words))
         nc.sync.dma_start(list1[:], offs)
         load_weight("wv", wv)
         load_weight("zv", zv)
         nc.sync.dma_start(wt_raw[:], wt_words.rearrange("a p n i -> p a (n i)").bitcast(I32))
         for q in range(4):
             nc.sync.dma_start(
-                wt_scales_raw[32 * q : 32 * q + 4, :].bitcast(I32).rearrange("r (a n) -> r a n", a=2),
+                scale_rows(wt_scales_raw, q, 0, 4).rearrange("r (a n) -> r a n", a=2),
                 wt_scales[:, 4 * q : 4 * q + 4, :].bitcast(I32).rearrange("a r n -> r a n"),
             )
-        load_table(v_words, tab_words)
+        nc.sync.dma_start(v_words[:].bitcast(I32), words_view(tab_words))
         for q in range(4):
-            nc.sync.dma_start(v_scales[32 * q : 32 * q + 4, :].bitcast(I32), tab_scales[0, 4 * q : 4 * q + 4, :].bitcast(I32))
+            nc.sync.dma_start(scale_rows(v_scales, q, 0, 4), tab_scales[0, 4 * q : 4 * q + 4, :].bitcast(I32))
         nc.sync.dma_start(bias[:], b.rearrange("(p t) -> p t", t=PACK))
         load_weight("zt0", zt[0:512, :])
         load_weight("zt1", zt[512:1024, :])
@@ -105,11 +122,13 @@ def tile_list_gmu_relu_scatP_kernel(
 
         nc.vector.tensor_copy(picked2_scales[:], v2_scales[:].indirect(list2[:]))
         for a in range(2):
-            nc.gpsimd.dma_start(planes2[a][0:100, :].bitcast(I32), picked2_scales[24 + 4 * a : 124 + 4 * a, :].bitcast(I32))
+            first_row = LOADED_ROW + 4 * a
+            nc.gpsimd.dma_start(planes2[a][0:MOVED_ROWS, :].bitcast(I32), picked2_scales[first_row : first_row + MOVED_ROWS, :].bitcast(I32))
         both = held([P, J], U32, "picked2_both")
         nc.vector.tensor_copy(both[:], v2_words[:].indirect(list2[:]))
         parted = held([P, 2, 2 * J], U8, "picked2_words")
         nc.vector.tensor_copy(parted[:].bitcast(U16), both[:].bitcast(U16).rearrange("p (j d) -> p d j", d=2))
+
         wt_codes = held([P, 2, N], I32, "wt_codes")
         wt_planes = held([P, 2 * N], U8, "wt_planes")
         nc.vector.tensor_copy(
@@ -127,12 +146,12 @@ def tile_list_gmu_relu_scatP_kernel(
 
         quantised = {}
 
-        def quantise_weight(name, t0, t1, copy, tag=""):
+        def quantise_weight(name, t0, t1, copy):
             count = t1 - t0
-            grouped = held([P, count, P, PACK], BF16, "grouped_%s%d" % (name, t0), tag=tag)
+            grouped = held([P, count, P, PACK], BF16, "grouped_%s_%d" % (name, t0))
             copy(grouped[:].rearrange("p t m j -> p m j t"), raw[name][:].rearrange("p j (m t) -> p m j t", t=PACK)[:, :, :, t0:t1])
-            codes = held([P, count * P], U32, "codes_%s%d" % (name, t0))
-            scales = held([P, count * P], U8, "scales_%s%d" % (name, t0))
+            codes = held([P, count * P], U32, "codes_%s_%d" % (name, t0))
+            scales = held([P, count * P], U8, "scales_%s_%d" % (name, t0))
             nc.vector.quantize_mx(out=codes[:].bitcast(FP8X4), scales=scales[:], in_=grouped[:].rearrange("p t m j -> p (t m j)"))
             for t in range(t0, t1):
                 cols = slice(P * (t - t0), P * (t - t0 + 1))
@@ -145,152 +164,152 @@ def tile_list_gmu_relu_scatP_kernel(
                     start=(i == 0), stop=(i == len(passes) - 1),
                 )
 
-        order = [(0, 0), (1, 0), (0, 1), (1, 1), (2, 0), (3, 0), (2, 1), (3, 1)]
+        def items_of(h):
+            return slice(HALF * h, HALF * (h + 1))
 
-        rows_of = out_0.rearrange("(p t) c -> t p c", t=PACK)
-        text = {}
-        totals = []
-        woven_tags = ("raw_wv", "raw_zv", "grouped_zt00", "raw_zt1")
-        mixed = {}
+        def v_side(h):
+            return picked_words[:, items_of(h)].bitcast(FP8X4), picked_scales[:, items_of(h)]
 
-        def sides(h):
-            items = slice(HALF * h, HALF * (h + 1))
-            v_side = (picked_words[:, items].bitcast(FP8X4), picked_scales[:, items])
-            v2_side = [
-                (parted[:, a, 2 * HALF * h : 2 * HALF * (h + 1)].bitcast(FP4X4), plane[:, items])
-                for a, plane in enumerate(planes2)
-            ]
-            return v_side, v2_side
+        def v2_side(h, a):
+            return parted[:, a, 2 * HALF * h : 2 * HALF * (h + 1)].bitcast(FP4X4), planes2[a][:, items_of(h)]
 
-        def text_part(s, at):
-            t, h = order[s]
-            v2_side = sides(h)[1]
-            packed = [
-                (wt_codes[:, a, P * t : P * (t + 1)].bitcast(FP8X4), wt_planes[:, N * a + P * t : N * a + P * (t + 1)]) for a in range(2)
-            ]
+        def wt_side(t, a):
+            return wt_codes[:, a, P * t : P * (t + 1)].bitcast(FP8X4), wt_planes[:, N * a + P * t : N * a + P * (t + 1)]
+
+        ats, diffs, gateds, totals = {}, {}, {}, []
+
+        def make_at(s, at):
+            t, h = STEPS[s]
             if s in (2, 3):
-                ht = psum.tile([P, HALF], F32, name="ht_early", tag="z", bufs=4)
+                ht = psum.tile([P, HALF], F32, name="ht_in_z_bank", tag="z", bufs=4)
             else:
                 ht = psum.tile([P, HALF], F32, name="ht")
-            product(ht, [(packed[0], v2_side[0]), (packed[1], v2_side[1])])
+            product(ht, [(wt_side(t, a), v2_side(h, a)) for a in range(2)])
             nc.scalar.activation(at, ht[:], ACT.Relu)
-            text[s] = at
+            ats[s] = at
 
-        diffs = {}
-
-        def picture_part(s, diff):
-            t, h = order[s]
+        def make_diff(s, diff):
+            t, h = STEPS[s]
             hv = psum.tile([P, HALF], F32, name="hv")
-            product(hv, [(quantised["wv", t], sides(h)[0])])
+            product(hv, [(quantised["wv", t], v_side(h))])
+            nc.vector.scalar_tensor_tensor(diff, hv[:], 0.0, ats[s], ALU.max, ALU.subtract)
             diffs[s] = diff
-            nc.vector.scalar_tensor_tensor(diffs[s], hv[:], 0.0, text[s], ALU.max, ALU.subtract)
 
-        def front(s):
-            t, h = order[s]
-            v_side, v2_side = sides(h)
+        def make_gated(s):
+            t, h = STEPS[s]
             z = psum.tile([P, HALF], F32, name="z", bufs=4)
-            product(z, [(quantised["zv", t], v_side), (quantised["zt0", t], v2_side[0]), (quantised["zt1", t], v2_side[1])])
+            product(z, [(quantised["zv", t], v_side(h)), (quantised["zt0", t], v2_side(h, 0)), (quantised["zt1", t], v2_side(h, 1))])
             gate = held([P, HALF], F32, "gate%d" % s)
             nc.scalar.activation(gate[:], z[:], ACT.Sigmoid, bias=bias[:, t : t + 1], scale=1.0)
-            diff = diffs[s]
-            gated = held([P, HALF], F32, "gated%d" % s)
-            engine = nc.vector if s < 2 else nc.gpsimd
-            engine.tensor_tensor(gated[:], diff, gate[:], ALU.mult)
-            mixed[s] = gated
+            gateds[s] = held([P, HALF], F32, "gated%d" % s)
+            engine = nc.vector if s < VECTOR_PRODUCTS else nc.gpsimd
+            engine.tensor_tensor(gateds[s][:], diffs[s], gate[:], ALU.mult)
+
+        def finish_on_vector(s, result):
+            total = held([P, HALF], F32, "total_first")
+            nc.vector.tensor_tensor(total[:], gateds[s][:], ats[s], ALU.add)
+            nc.vector.tensor_tensor(result[:], total[:], weight[:, items_of(STEPS[s][1])], ALU.mult)
 
         def finish_by_transposes(s, result):
-            h = order[s][1]
-            summed = psum.tile([P, 4, P], F32, name="summed", tag="ht")
-            for c in range(4):
+            h = STEPS[s][1]
+            summed = psum.tile([P, BLOCKS, P], F32, name="summed", tag="ht")
+            for c in range(BLOCKS):
                 cols = slice(P * c, P * (c + 1))
-                nc.tensor.matmul(summed[:, c, :], lhsT=text[s][:, cols], rhs=ident[:], is_transpose=True, start=True, stop=False)
-                nc.tensor.matmul(summed[:, c, :], lhsT=mixed[s][:, cols], rhs=ident[:], is_transpose=True, start=False, stop=True)
-            weighted = held([P, 4, P], F32, "weighted%d" % s)
-            for c in range(4):
-                nc.scalar.activation(weighted[:, c, :], summed[:, c, :], ACT.Copy, scale=weight_cols[:, 4 * h + c : 4 * h + c + 1])
-            turned = psum.tile([P, 4, P], F32, name="turned", tag="hv")
-            for c in range(4):
+                nc.tensor.matmul(summed[:, c, :], lhsT=ats[s][:, cols], rhs=ident[:], is_transpose=True, start=True, stop=False)
+                nc.tensor.matmul(summed[:, c, :], lhsT=gateds[s][:, cols], rhs=ident[:], is_transpose=True, start=False, stop=True)
+            weighted = held([P, BLOCKS, P], F32, "weighted%d" % s)
+            for c in range(BLOCKS):
+                col = BLOCKS * h + c
+                nc.scalar.activation(weighted[:, c, :], summed[:, c, :], ACT.Copy, scale=weight_cols[:, col : col + 1])
+            turned = psum.tile([P, BLOCKS, P], F32, name="turned", tag="hv")
+            for c in range(BLOCKS):
                 nc.tensor.transpose(turned[:, c, :], weighted[:, c, :], ident[:])
             nc.scalar.copy(result[:], turned[:].rearrange("p c j -> p (c j)"))
 
         def finish_on_gpsimd(s, result):
-            h = order[s][1]
             if s % 2 == 0:
                 totals.extend(two("total%d_%d" % (s, s + 1), "gated3"))
-            nc.gpsimd.tensor_tensor(totals[s - 4], mixed[s][:], text[s], ALU.add)
-            nc.gpsimd.tensor_tensor(result[:], totals[s - 4], weight[:, HALF * h : HALF * (h + 1)], ALU.mult)
+            total = totals[s - FIRST_GPSIMD_STEP]
+            nc.gpsimd.tensor_tensor(total, gateds[s][:], ats[s], ALU.add)
+            nc.gpsimd.tensor_tensor(result[:], total, weight[:, items_of(STEPS[s][1])], ALU.mult)
 
-        def finish_first(s, result):
-            total = held([P, HALF], F32, "total_first")
-            nc.vector.tensor_tensor(total[:], mixed[s][:], text[s], ALU.add)
-            nc.gpsimd.tensor_tensor(result[:], total[:], weight[:, 0:HALF], ALU.mult)
+        rows_of = out_0.rearrange("(p t) c -> t p c", t=PACK)
 
-        def back(s):
-            t, h = order[s]
+        def place(s):
+            t, h = STEPS[s]
             result = held([P, HALF], F32, "result%d" % s, tag="gate%d" % s)
-            (finish_first if s == 0 else finish_by_transposes if s < 4 else finish_on_gpsimd)(s, result)
-            nc.vector.tensor_copy(windows[t][:].indirect(list1[:, 32 * h : 32 * h + 32]), result[:])
+            if s == 0:
+                finish_on_vector(s, result)
+            elif s < FIRST_GPSIMD_STEP:
+                finish_by_transposes(s, result)
+            else:
+                finish_on_gpsimd(s, result)
+            nc.vector.tensor_copy(windows[t][:].indirect(list1[:, LIST_COLS * h : LIST_COLS * (h + 1)]), result[:])
             if h == 1:
                 nc.sync.dma_start(rows_of[t], windows[t][:])
 
-        def two(name, tag=""):
-            both_steps = held([P, 2, HALF], F32, name, tag=tag)
-            return both_steps[:, 0, :], both_steps[:, 1, :]
-
-        quantise_weight("wv", 0, 4, nc.scalar.copy)
-        quantise_weight("zv", 0, 4, nc.scalar.copy)
-        open_window(2, 4, "grouped_zv0")
+        quantise_weight("wv", 0, PACK, nc.scalar.copy)
+        quantise_weight("zv", 0, PACK, nc.scalar.copy)
+        open_window(2, 4, "grouped_zv_0")
         for s, at in enumerate(two("at01")):
-            text_part(s, at)
+            make_at(s, at)
         turned_weight = psum.tile([P, P], F32, name="turned_weight", tag="ht")
         nc.tensor.transpose(turned_weight[:], weight_rows[:], ident[:])
         nc.scalar.copy(weight_cols[:], turned_weight[:, 0 : J // P])
-        quantise_weight("zt0", 0, 4, nc.scalar.copy)
-        quantise_weight("zt1", 0, 2, nc.vector.tensor_copy)
-        first = two("diff01", "grouped_zt10") + two("diff23")
-        picture_part(0, first[0])
-        front(0)
-        quantise_weight("zt1", 2, 4, nc.vector.tensor_copy)
-        picture_part(1, first[1])
-        front(1)
-        held_back = held([P, 4, HALF], F32, "at2345", tag="raw_zt0")
-        later_texts = tuple(held_back[:, i, :] for i in range(4)) + two("at67")
-        for s, (at, diff) in enumerate(zip(later_texts, first[2:] + two("diff45") + two("diff67"))):
-            text_part(2 + s, at)
-            picture_part(2 + s, diff)
-        for s in range(len(order)):
-            if s == 5:
-                open_window(3, 4, "gated1")
-            back(s)
-            if s in (0, 1, 5):
-                first_of_pair = {0: 2, 1: 4, 5: 6}[s]
-                front(first_of_pair)
-                front(first_of_pair + 1)
+        quantise_weight("zt0", 0, PACK, nc.scalar.copy)
 
-        def round_on_gpsimd(out, in_):
-            nc.gpsimd.tensor_scalar(out, in_, 1.0, -0.0, ALU.mult, ALU.add)
+        quantise_weight("zt1", 0, 2, nc.vector.tensor_copy)
+        first_diffs = two("diff01", "grouped_zt1_0") + two("diff23")
+        make_diff(0, first_diffs[0])
+        make_gated(0)
+        quantise_weight("zt1", 2, PACK, nc.vector.tensor_copy)
+        make_diff(1, first_diffs[1])
+        make_gated(1)
+
+        at2345 = held([P, 4, HALF], F32, "at2345", tag="raw_zt0")
+        later_ats = tuple(at2345[:, i, :] for i in range(4)) + two("at67")
+        later_diffs = first_diffs[2:] + two("diff45") + two("diff67")
+        for s in range(2, len(STEPS)):
+            make_at(s, later_ats[s - 2])
+            make_diff(s, later_diffs[s - 2])
+
+        place(0)
+        make_gated(2)
+        make_gated(3)
+        place(1)
+        make_gated(4)
+        make_gated(5)
+        for s in (2, 3, 4):
+            place(s)
+        open_window(3, 4, "gated1")
+        place(5)
+        make_gated(6)
+        make_gated(7)
+        place(6)
+        place(7)
 
         pair01 = held([P, 2, T], BF16, "pair01", tag="weighted3")
-        woven = [held([P, QUARTER, PACK], BF16, "woven%d" % q, tag=woven_tags[q]) for q in range(4)]
-        quarters = [slice(QUARTER * q, QUARTER * (q + 1)) for q in range(4)]
+        woven_tags = ("raw_wv", "raw_zv", "grouped_zt0_0", "raw_zt1", "")
+        woven = [held([P, c.stop - c.start, PACK], BF16, "woven%d" % i, tag=woven_tags[i]) for i, c in enumerate(PIECES)]
         for t in range(2):
-            for s in range(2):
-                nc.scalar.copy(pair01[:, t, 1024 * s : 1024 * (s + 1)], windows[t][:, 1024 * s : 1024 * (s + 1)])
-        for q in range(4):
-            nc.scalar.copy(woven[q][:, :, 0:2], pair01[:, :, quarters[q]].rearrange("p e c -> p c e"))
-        late = held([P, 4, 2, QUARTER], BF16, "pair23", tag="gated3")
-        pair23 = [late[:, q] for q in range(4)]
-        round_on_gpsimd(late[:, :, 0, :], windows[2][:].rearrange("p (q c) -> p q c", q=4))
+            for u in range(2):
+                cols = slice(T // 2 * u, T // 2 * (u + 1))
+                nc.scalar.copy(pair01[:, t, cols], windows[t][:, cols])
+        for i, c in enumerate(PIECES):
+            nc.scalar.copy(woven[i][:, :, 0:2], pair01[:, :, c].rearrange("p e c -> p c e"))
+        pairs23 = held([P, 4, 2, QUARTER], BF16, "pairs23", tag="gated3")
+        pair23 = [pairs23[:, c.start // QUARTER, :, c.start % QUARTER : c.start % QUARTER + c.stop - c.start] for c in PIECES]
+        nc.gpsimd.tensor_scalar(pairs23[:, :, 0, :], windows[2][:].rearrange("p (q c) -> p q c", q=4), 1.0, -0.0, ALU.mult, ALU.add)
 
         out_scales = held([P, T], U8, "out_scales")
-        words_view = table_view(out_1)
+        for i, c in enumerate(PIECES):
+            copy = nc.vector.tensor_copy if i < VECTOR_PIECES else nc.scalar.copy
+            copy(pair23[i][:, 1, :], windows[3][:, c])
+            copy(woven[i][:, :, 2:4], pair23[i].rearrange("p e c -> p c e"))
+        codes_tags = ("v_words", "v2_words", "picked2_both", "wt_raw", "")
+        for i, c in enumerate(PIECES):
+            out_codes = held([P, c.stop - c.start], U32, "out_codes%d" % i, tag=codes_tags[i])
+            nc.vector.quantize_mx(out=out_codes[:].bitcast(FP8X4), scales=out_scales[:, c], in_=woven[i][:].rearrange("p c t -> p (c t)"))
+            nc.sync.dma_start(words_view(out_1)[:, c], out_codes[:].bitcast(I32))
         for q in range(4):
-            copy = nc.vector.tensor_copy if q < 2 else nc.scalar.copy
-            copy(pair23[q][:, 1, :], windows[3][:, quarters[q]])
-            copy(woven[q][:, :, 2:4], pair23[q].rearrange("p e c -> p c e"))
-        for q in range(4):
-            out_codes = held([P, QUARTER], U32, "out_codes%d" % q, tag=("v_words", "v2_words", "picked2_both", "wt_raw")[q])
-            nc.vector.quantize_mx(out=out_codes[:].bitcast(FP8X4), scales=out_scales[:, quarters[q]], in_=woven[q][:].rearrange("p c t -> p (c t)"))
-            nc.sync.dma_start(words_view[:, quarters[q]], out_codes[:].bitcast(I32))
-        for q in range(4):
-            nc.scalar.dma_start(out_2[0, 4 * q : 4 * q + 4, :].bitcast(I32), out_scales[32 * q : 32 * q + 4, :].bitcast(I32))
+            nc.scalar.dma_start(out_2[0, 4 * q : 4 * q + 4, :].bitcast(I32), scale_rows(out_scales, q, 0, 4))

@@ -20,19 +20,18 @@ ACT = mybir.ActivationFunctionType
 P = 128
 PACK = 4
 HALF = 512
-BLOCKS = HALF // P
 QUADRANT = 32
 QUARTER = T // 4
 LIST_COLS = HALF // 16
-
 LOADED_ROW = QUADRANT - 8
 MOVED_ROWS = 3 * QUADRANT + 4
+KIB = 1024
+BLOCKS = HALF // P
 
 STEPS = [(0, 0), (1, 0), (0, 1), (1, 1), (2, 0), (3, 0), (2, 1), (3, 1)]
-FIRST_GPSIMD_STEP = 4
-VECTOR_PRODUCTS = 2
 PIECES = [slice(0, 512), slice(512, 1024), slice(1024, 1536), slice(1536, 1792), slice(1792, 2048)]
-VECTOR_PIECES = 2
+SHARES = [slice(0, 512), slice(512, 1024), slice(1024, 1152), slice(1152, 1536), slice(1536, 1792), slice(1792, 2048)]
+VECTOR_SHARES = 3
 
 
 def tile_list_gmu_relu_scatP_kernel(
@@ -40,18 +39,32 @@ def tile_list_gmu_relu_scatP_kernel(
 ):
     nc = tc.nc
     with ExitStack() as ctx:
+        lists = ctx.enter_context(tc.tile_pool(name="lists", bufs=1))
         keep = ctx.enter_context(tc.tile_pool(name="keep", bufs=1))
-        psum = ctx.enter_context(tc.psum_pool(name="psum", bufs=2))
+        psum = ctx.enter_context(tc.psum_pool(name="psum", bufs=1))
 
-        def held(shape, dtype, name, tag=""):
-            return keep.tile(shape, dtype, name=name, tag=tag or name, align_bytes=64)
+        sizes = {F32: 4, I32: 4, U32: 4, BF16: 2, U8: 1}
+        places = {"free": 0}
 
-        def two(name, tag=""):
-            both_steps = held([P, 2, HALF], F32, name, tag=tag)
-            return both_steps[:, 0, :], both_steps[:, 1, :]
+        def reserve(name, size):
+            places[name] = places["free"]
+            places["free"] = places["free"] + size
 
-        list1 = keep.tile([P, J // 16], U16, name="list1")
-        list2 = keep.tile([P, J // 16], U16, name="list2")
+        def held(shape, dtype, name, over="", shift=0):
+            if not over:
+                size = sizes[dtype]
+                for count in shape[1:]:
+                    size = size * count
+                reserve(name, (size + 63) // 64 * 64)
+            else:
+                places[name] = places[over] + shift
+            return keep.tile(shape, dtype, name=name, align_bytes=64, offset=places[name])
+
+        list1 = lists.tile([P, J // 16], U16, name="list1")
+        list2 = lists.tile([P, J // 16], U16, name="list2")
+        reserve("room12", 16 * KIB)
+        reserve("room_late", 10 * KIB)
+        reserve("room3", 8 * KIB)
         v_words = held([P, T], U32, "v_words")
         v2_words = held([P, T], U32, "v2_words")
         v_scales = held([P, T], U8, "v_scales")
@@ -62,19 +75,19 @@ def tile_list_gmu_relu_scatP_kernel(
         planes2 = [held([P, J], U8, "planes2_%d" % a) for a in range(2)]
         raw = {name: held([P, PACK, N], F32, "raw_" + name) for name in ("wv", "zv", "zt0", "zt1")}
         bias = held([P, PACK], F32, "bias")
+        weight = held([P, J], F32, "weight")
         weight_rows = held([P, P], F32, "weight_rows")
         weight_cols = held([P, J // P], F32, "weight_cols")
-        weight = held([P, J], F32, "weight")
         ident = held([P, P], F32, "ident")
 
         warm = held([P, 2], F32, "warm")
         nc.gpsimd.memset(warm[:, 0:1], 0.0)
         nc.scalar.activation(warm[:, 1:2], warm[:, 0:1], ACT.Sigmoid)
 
+        for q in range(4):
+            nc.vector.memset(v2_scales[QUADRANT * q : QUADRANT * q + LOADED_ROW, :].bitcast(I32), 0)
         nc.vector.memset(wt_scales_raw[:].bitcast(I32), 0)
         nc.vector.memset(v_scales[:].bitcast(I32), 0)
-        for q in range(4):
-            (nc.gpsimd, nc.vector)[q % 2].memset(v2_scales[QUADRANT * q : QUADRANT * q + LOADED_ROW, :].bitcast(I32), 0)
         for plane in planes2:
             nc.gpsimd.memset(plane[:].bitcast(I32), 0)
         nc.gpsimd.memset(weight_rows[:], 0.0)
@@ -82,12 +95,12 @@ def tile_list_gmu_relu_scatP_kernel(
 
         windows = {}
 
-        def open_window(t, parts, tag=""):
-            windows[t] = held([P, T], F32, "window%d" % t, tag=tag)
+        def open_window(t, engine, parts, over="", shift=0):
+            windows[t] = held([P, T], F32, "window%d" % t, over=over, shift=shift)
             for i in range(parts):
-                nc.gpsimd.memset(windows[t][:, T // parts * i : T // parts * (i + 1)], 0.0)
+                engine.memset(windows[t][:, T // parts * i : T // parts * (i + 1)], 0.0)
 
-        open_window(0, 1)
+        open_window(0, nc.vector, 1)
 
         def words_view(words):
             return words[0].rearrange("p t i -> p (t i)").bitcast(I32)
@@ -102,213 +115,221 @@ def tile_list_gmu_relu_scatP_kernel(
         for q in range(4):
             nc.sync.dma_start(scale_rows(v2_scales, q, LOADED_ROW, 8), tab2_scales[:, 4 * q : 4 * q + 4, :].bitcast(I32))
         nc.sync.dma_start(v2_words[:].bitcast(I32), words_view(tab2_words))
-        nc.sync.dma_start(list1[:], offs)
-        load_weight("wv", wv)
-        load_weight("zv", zv)
         nc.sync.dma_start(wt_raw[:], wt_words.rearrange("a p n i -> p a (n i)").bitcast(I32))
+        nc.sync.dma_start(list1[:], offs)
         for q in range(4):
             nc.sync.dma_start(
                 scale_rows(wt_scales_raw, q, 0, 4).rearrange("r (a n) -> r a n", a=2),
                 wt_scales[:, 4 * q : 4 * q + 4, :].bitcast(I32).rearrange("a r n -> r a n"),
             )
-        nc.sync.dma_start(v_words[:].bitcast(I32), words_view(tab_words))
-        for q in range(4):
-            nc.sync.dma_start(scale_rows(v_scales, q, 0, 4), tab_scales[0, 4 * q : 4 * q + 4, :].bitcast(I32))
-        nc.sync.dma_start(bias[:], b.rearrange("(p t) -> p t", t=PACK))
-        load_weight("zt0", zt[0:512, :])
-        load_weight("zt1", zt[512:1024, :])
-        nc.sync.dma_start(weight_rows[0 : J // P, :], wgo[0].rearrange("(c p) -> c p", p=P))
-        nc.sync.dma_start(weight[:], wgo)
-
+        load_weight("wv", wv)
         nc.vector.tensor_copy(picked2_scales[:], v2_scales[:].indirect(list2[:]))
         for a in range(2):
             first_row = LOADED_ROW + 4 * a
-            nc.gpsimd.dma_start(planes2[a][0:MOVED_ROWS, :].bitcast(I32), picked2_scales[first_row : first_row + MOVED_ROWS, :].bitcast(I32))
+            nc.sync.dma_start(planes2[a][0:MOVED_ROWS, :].bitcast(I32), picked2_scales[first_row : first_row + MOVED_ROWS, :].bitcast(I32))
+        for q in range(4):
+            nc.sync.dma_start(scale_rows(v_scales, q, 0, 4), tab_scales[0, 4 * q : 4 * q + 4, :].bitcast(I32))
+        nc.sync.dma_start(v_words[:].bitcast(I32), words_view(tab_words))
+        load_weight("zv", zv)
+        nc.sync.dma_start(bias[:], b.rearrange("(p t) -> p t", t=PACK))
+        load_weight("zt0", zt[0:512, :])
+        load_weight("zt1", zt[512:1024, :])
+        nc.sync.dma_start(weight[:], wgo)
+        nc.sync.dma_start(weight_rows[0 : J // P, :], wgo[0].rearrange("(c p) -> c p", p=P))
+
         both = held([P, J], U32, "picked2_both")
         nc.vector.tensor_copy(both[:], v2_words[:].indirect(list2[:]))
         parted = held([P, 2, 2 * J], U8, "picked2_words")
         nc.vector.tensor_copy(parted[:].bitcast(U16), both[:].bitcast(U16).rearrange("p (j d) -> p d j", d=2))
 
-        wt_codes = held([P, 2, N], I32, "wt_codes")
-        wt_planes = held([P, 2 * N], U8, "wt_planes")
-        nc.vector.tensor_copy(
-            wt_codes[:].rearrange("p a (t m) -> p a m t", t=PACK), wt_raw[:].rearrange("p a (m t) -> p a m t", t=PACK)
-        )
-        nc.vector.tensor_copy(
-            wt_planes[:].rearrange("p (a t m) -> p a t m", a=2, t=PACK),
-            wt_scales_raw[:].rearrange("p (a m t) -> p a t m", a=2, t=PACK),
-        )
-        open_window(1, 4, "wt_scales_raw")
-        picked_words = held([P, J], U32, "picked_words")
-        nc.vector.tensor_copy(picked_words[:], v_words[:].indirect(list1[:]))
+        wt_codes, wt_planes = [], []
+        for u in range(2):
+            wt_codes.append(held([P, 2, 2, P], I32, "wt_codes%d" % u))
+            wt_planes.append(held([P, 2, 2, P], U8, "wt_planes%d" % u))
+            nc.gpsimd.tensor_copy(
+                wt_codes[u][:].rearrange("p a t m -> p a m t"), wt_raw[:].rearrange("p a (m t) -> p a m t", t=PACK)[:, :, :, 2 * u : 2 * u + 2]
+            )
+            nc.gpsimd.tensor_copy(wt_planes[u][:], wt_scales_raw[:].rearrange("p (a m t) -> p a t m", a=2, t=PACK)[:, :, 2 * u : 2 * u + 2, :])
         picked_scales = held([P, J], U8, "picked_scales")
         nc.vector.tensor_copy(picked_scales[:], v_scales[:].indirect(list1[:]))
 
         quantised = {}
 
-        def quantise_weight(name, t0, t1, copy):
-            count = t1 - t0
-            grouped = held([P, count, P, PACK], BF16, "grouped_%s_%d" % (name, t0))
-            copy(grouped[:].rearrange("p t m j -> p m j t"), raw[name][:].rearrange("p j (m t) -> p m j t", t=PACK)[:, :, :, t0:t1])
-            codes = held([P, count * P], U32, "codes_%s_%d" % (name, t0))
-            scales = held([P, count * P], U8, "scales_%s_%d" % (name, t0))
+        def quantise_weight(name, u, copy, over="", shift=0):
+            grouped = held([P, 2, P, PACK], BF16, "grouped_%s_%d" % (name, u), over=over, shift=shift)
+            copy(grouped[:].rearrange("p t m j -> p m j t"), raw[name][:].rearrange("p j (m t) -> p m j t", t=PACK)[:, :, :, 2 * u : 2 * u + 2])
+            codes = held([P, 2 * P], U32, "codes_%s_%d" % (name, u))
+            scales = held([P, 2 * P], U8, "scales_%s_%d" % (name, u))
             nc.vector.quantize_mx(out=codes[:].bitcast(FP8X4), scales=scales[:], in_=grouped[:].rearrange("p t m j -> p (t m j)"))
-            for t in range(t0, t1):
-                cols = slice(P * (t - t0), P * (t - t0 + 1))
-                quantised[name, t] = (codes[:, cols].bitcast(FP8X4), scales[:, cols])
+            for i in range(2):
+                cols = slice(P * i, P * (i + 1))
+                quantised[name, 2 * u + i] = (codes[:, cols].bitcast(FP8X4), scales[:, cols])
 
-        def product(acc, passes):
+        def product(s, name, passes):
+            acc = psum.tile([P, HALF], F32, name="%s%d" % (name, s), tag="bank%d" % s)
             for i, (lhs, rhs) in enumerate(passes):
                 nc.tensor.matmul_mx(
                     out=acc[:], lhsT=lhs[0], lhsT_scale=lhs[1], rhs=rhs[0], rhs_scale=rhs[1],
                     start=(i == 0), stop=(i == len(passes) - 1),
                 )
+            return acc
 
         def items_of(h):
             return slice(HALF * h, HALF * (h + 1))
-
-        def v_side(h):
-            return picked_words[:, items_of(h)].bitcast(FP8X4), picked_scales[:, items_of(h)]
 
         def v2_side(h, a):
             return parted[:, a, 2 * HALF * h : 2 * HALF * (h + 1)].bitcast(FP4X4), planes2[a][:, items_of(h)]
 
         def wt_side(t, a):
-            return wt_codes[:, a, P * t : P * (t + 1)].bitcast(FP8X4), wt_planes[:, N * a + P * t : N * a + P * (t + 1)]
+            return wt_codes[t // 2][:, a, t % 2, :].bitcast(FP8X4), wt_planes[t // 2][:, a, t % 2, :]
 
-        ats, diffs, gateds, totals = {}, {}, {}, []
+        def two(name, over="", shift=0):
+            pair = held([P, 2, HALF], F32, name, over=over, shift=shift)
+            return pair[:, 0, :], pair[:, 1, :]
 
-        def make_at(s, at):
+        ats = two("at01") + two("at23") + two("at45") + two("at67")
+        diffs, gates = {}, {}
+
+        def make_at(s):
             t, h = STEPS[s]
-            if s in (2, 3):
-                ht = psum.tile([P, HALF], F32, name="ht_in_z_bank", tag="z", bufs=4)
-            else:
-                ht = psum.tile([P, HALF], F32, name="ht")
-            product(ht, [(wt_side(t, a), v2_side(h, a)) for a in range(2)])
-            nc.scalar.activation(at, ht[:], ACT.Relu)
-            ats[s] = at
+            ht = product(s, "ht", [(wt_side(t, a), v2_side(h, a)) for a in range(2)])
+            nc.scalar.activation(ats[s], ht[:], ACT.Relu)
+
+        quantise_weight("wv", 0, nc.scalar.copy)
+        picked_words = held([P, J], U32, "picked_words")
+        nc.vector.tensor_copy(picked_words[:], v_words[:].indirect(list1[:]))
+        quantise_weight("wv", 1, nc.scalar.copy, over="room12", shift=7 * KIB)
+
+        def v_side(h):
+            return picked_words[:, items_of(h)].bitcast(FP8X4), picked_scales[:, items_of(h)]
 
         def make_diff(s, diff):
             t, h = STEPS[s]
-            hv = psum.tile([P, HALF], F32, name="hv")
-            product(hv, [(quantised["wv", t], v_side(h))])
+            hv = product(s, "hv", [(quantised["wv", t], v_side(h))])
             nc.vector.scalar_tensor_tensor(diff, hv[:], 0.0, ats[s], ALU.max, ALU.subtract)
             diffs[s] = diff
 
-        def make_gated(s):
+        def make_gate(s):
             t, h = STEPS[s]
-            z = psum.tile([P, HALF], F32, name="z", bufs=4)
-            product(z, [(quantised["zv", t], v_side(h)), (quantised["zt0", t], v2_side(h, 0)), (quantised["zt1", t], v2_side(h, 1))])
-            gate = held([P, HALF], F32, "gate%d" % s)
-            nc.scalar.activation(gate[:], z[:], ACT.Sigmoid, bias=bias[:, t : t + 1], scale=1.0)
-            gateds[s] = held([P, HALF], F32, "gated%d" % s)
-            engine = nc.vector if s < VECTOR_PRODUCTS else nc.gpsimd
-            engine.tensor_tensor(gateds[s][:], diffs[s], gate[:], ALU.mult)
+            z = product(s, "z", [(quantised["zv", t], v_side(h)), (quantised["zt0", t], v2_side(h, 0)), (quantised["zt1", t], v2_side(h, 1))])
+            gates[s] = held([P, HALF], F32, "gate%d" % s)
+            nc.scalar.activation(gates[s][:], z[:], ACT.Sigmoid, bias=bias[:, t : t + 1], scale=1.0)
 
-        def finish_on_vector(s, result):
-            total = held([P, HALF], F32, "total_first")
-            nc.vector.tensor_tensor(total[:], gateds[s][:], ats[s], ALU.add)
-            nc.vector.tensor_tensor(result[:], total[:], weight[:, items_of(STEPS[s][1])], ALU.mult)
-
-        def finish_by_transposes(s, result):
-            h = STEPS[s][1]
-            summed = psum.tile([P, BLOCKS, P], F32, name="summed", tag="ht")
-            for c in range(BLOCKS):
-                cols = slice(P * c, P * (c + 1))
-                nc.tensor.matmul(summed[:, c, :], lhsT=ats[s][:, cols], rhs=ident[:], is_transpose=True, start=True, stop=False)
-                nc.tensor.matmul(summed[:, c, :], lhsT=gateds[s][:, cols], rhs=ident[:], is_transpose=True, start=False, stop=True)
-            weighted = held([P, BLOCKS, P], F32, "weighted%d" % s)
-            for c in range(BLOCKS):
-                col = BLOCKS * h + c
-                nc.scalar.activation(weighted[:, c, :], summed[:, c, :], ACT.Copy, scale=weight_cols[:, col : col + 1])
-            turned = psum.tile([P, BLOCKS, P], F32, name="turned", tag="hv")
-            for c in range(BLOCKS):
-                nc.tensor.transpose(turned[:, c, :], weighted[:, c, :], ident[:])
-            nc.scalar.copy(result[:], turned[:].rearrange("p c j -> p (c j)"))
-
-        def finish_on_gpsimd(s, result):
-            if s % 2 == 0:
-                totals.extend(two("total%d_%d" % (s, s + 1), "gated3"))
-            total = totals[s - FIRST_GPSIMD_STEP]
-            nc.gpsimd.tensor_tensor(total, gateds[s][:], ats[s], ALU.add)
-            nc.gpsimd.tensor_tensor(result[:], total, weight[:, items_of(STEPS[s][1])], ALU.mult)
+        for s in range(4):
+            make_at(s)
+        quantise_weight("zv", 0, nc.scalar.copy)
+        quantise_weight("zt0", 0, nc.scalar.copy)
+        early_diffs = two("diff01", over="room3") + two("diff23")
+        make_at(4)
+        make_at(5)
+        make_diff(0, early_diffs[0])
+        make_diff(1, early_diffs[1])
+        make_at(6)
+        make_at(7)
+        quantise_weight("zt1", 0, nc.scalar.copy, over="room_late")
+        for s in range(2, 4):
+            make_diff(s, early_diffs[s])
+        open_window(1, nc.gpsimd, 4, "room12")
+        open_window(2, nc.gpsimd, 4, "room12", 8 * KIB)
+        make_gate(0)
+        make_gate(1)
+        late_diffs = held([P, 4, HALF], F32, "diff4567", over="room_late", shift=2 * KIB - 64)
+        for s in range(4, 8):
+            make_diff(s, late_diffs[:, s - 4, :])
+        make_gate(2)
+        make_gate(3)
+        turned_weight = psum.tile([P, P], F32, name="turned_weight", tag="bank0")
+        nc.tensor.transpose(turned_weight[:], weight_rows[:], ident[:])
+        nc.scalar.copy(weight_cols[:], turned_weight[:, 0 : J // P])
+        for name in ("zv", "zt0", "zt1"):
+            quantise_weight(name, 1, nc.scalar.copy)
+        for s in range(4, 8):
+            make_gate(s)
 
         rows_of = out_0.rearrange("(p t) c -> t p c", t=PACK)
 
-        def place(s):
+        def offsets_of(h):
+            return list1[:, LIST_COLS * h : LIST_COLS * (h + 1)]
+
+        def place(s, result):
             t, h = STEPS[s]
-            result = held([P, HALF], F32, "result%d" % s, tag="gate%d" % s)
-            if s == 0:
-                finish_on_vector(s, result)
-            elif s < FIRST_GPSIMD_STEP:
-                finish_by_transposes(s, result)
-            else:
-                finish_on_gpsimd(s, result)
-            nc.vector.tensor_copy(windows[t][:].indirect(list1[:, LIST_COLS * h : LIST_COLS * (h + 1)]), result[:])
+            nc.vector.tensor_copy(windows[t][:].indirect(offsets_of(h)), result[:])
             if h == 1:
                 nc.sync.dma_start(rows_of[t], windows[t][:])
 
-        quantise_weight("wv", 0, PACK, nc.scalar.copy)
-        quantise_weight("zv", 0, PACK, nc.scalar.copy)
-        open_window(2, 4, "grouped_zv_0")
-        for s, at in enumerate(two("at01")):
-            make_at(s, at)
-        turned_weight = psum.tile([P, P], F32, name="turned_weight", tag="ht")
-        nc.tensor.transpose(turned_weight[:], weight_rows[:], ident[:])
-        nc.scalar.copy(weight_cols[:], turned_weight[:, 0 : J // P])
-        quantise_weight("zt0", 0, PACK, nc.scalar.copy)
+        reserve("room_result5", 2 * KIB)
+        reserve("room_result6", 2 * KIB)
+        result_rooms = {5: ("room_result5", 0), 6: ("room_result6", 0)}
+        last_blocks = ("", "room_result6", "room_result5", "raw_zt0")
 
-        quantise_weight("zt1", 0, 2, nc.vector.tensor_copy)
-        first_diffs = two("diff01", "grouped_zt1_0") + two("diff23")
-        make_diff(0, first_diffs[0])
-        make_gated(0)
-        quantise_weight("zt1", 2, PACK, nc.vector.tensor_copy)
-        make_diff(1, first_diffs[1])
-        make_gated(1)
+        def result_of(s):
+            over, shift = result_rooms.get(s, ("gate%d" % s, 0))
+            return held([P, HALF], F32, "result%d" % s, over=over, shift=shift)
 
-        at2345 = held([P, 4, HALF], F32, "at2345", tag="raw_zt0")
-        later_ats = tuple(at2345[:, i, :] for i in range(4)) + two("at67")
-        later_diffs = first_diffs[2:] + two("diff45") + two("diff67")
-        for s in range(2, len(STEPS)):
-            make_at(s, later_ats[s - 2])
-            make_diff(s, later_diffs[s - 2])
+        def finish_on_gpsimd(s, gated):
+            nc.gpsimd.tensor_tensor(gated, gated, ats[s], ALU.add)
+            result = result_of(s)
+            nc.gpsimd.tensor_tensor(result[:], gated, weight[:, items_of(STEPS[s][1])], ALU.mult)
+            place(s, result)
 
-        place(0)
-        make_gated(2)
-        make_gated(3)
-        place(1)
-        make_gated(4)
-        make_gated(5)
-        for s in (2, 3, 4):
-            place(s)
-        open_window(3, 4, "gated1")
-        place(5)
-        make_gated(6)
-        make_gated(7)
-        place(6)
-        place(7)
+        def finish_by_transposes(s, gated):
+            h = STEPS[s][1]
+            summed = psum.tile([P, BLOCKS, P], F32, name="summed%d" % s, tag="bank%d" % s)
+            for c in range(BLOCKS):
+                cols = slice(P * c, P * (c + 1))
+                nc.tensor.matmul(summed[:, c, :], lhsT=ats[s][:, cols], rhs=ident[:], is_transpose=True, start=True, stop=False)
+                nc.tensor.matmul(summed[:, c, :], lhsT=gated[:, cols], rhs=ident[:], is_transpose=True, start=False, stop=True)
+            weighted = [held([P, P], F32, "weighted%d_%d" % (s, c), over=last_blocks[c] if s == 4 else "") for c in range(BLOCKS)]
+            for c in range(BLOCKS):
+                col = BLOCKS * h + c
+                nc.scalar.activation(weighted[c][:], summed[:, c, :], ACT.Copy, scale=weight_cols[:, col : col + 1])
+            turned = psum.tile([P, BLOCKS, P], F32, name="turned%d" % s, tag="bank%d" % (s - 1))
+            for c in range(BLOCKS):
+                nc.tensor.transpose(turned[:, c, :], weighted[c][:], ident[:])
+            result = result_of(s)
+            nc.scalar.copy(result[:], turned[:].rearrange("p c j -> p (c j)"))
+            place(s, result)
 
-        pair01 = held([P, 2, T], BF16, "pair01", tag="weighted3")
-        woven_tags = ("raw_wv", "raw_zv", "grouped_zt0_0", "raw_zt1", "")
-        woven = [held([P, c.stop - c.start, PACK], BF16, "woven%d" % i, tag=woven_tags[i]) for i, c in enumerate(PIECES)]
+        reserve("room_first", 12 * KIB)
+        first = held([P, HALF], F32, "first", over="room_first")
+        second = held([P, HALF], F32, "second")
+        nc.vector.tensor_tensor(first[:], diffs[0], gates[0][:], ALU.mult)
+        nc.vector.tensor_tensor(second[:], diffs[1], gates[1][:], ALU.mult)
+        nc.vector.tensor_tensor(first[:], first[:], ats[0], ALU.add)
+        result = result_of(0)
+        nc.vector.tensor_tensor(result[:], first[:], weight[:, items_of(0)], ALU.mult)
+        place(0, result)
+        finish_by_transposes(1, second)
+        gated = held([P, 6, HALF], F32, "gated", over="room_first")
+        for s in range(2, 5):
+            nc.gpsimd.tensor_tensor(gated[:, s - 2, :], diffs[s], gates[s][:], ALU.mult)
+            finish_by_transposes(s, gated[:, s - 2, :])
+        open_window(3, nc.gpsimd, 4, "room3")
+        for s in range(5, 8):
+            nc.gpsimd.tensor_tensor(gated[:, s - 2, :], diffs[s], gates[s][:], ALU.mult)
+            finish_on_gpsimd(s, gated[:, s - 2, :])
+
+        pair01 = held([P, 2, T], BF16, "pair01", over="raw_zt0")
+        woven = [held([P, c.stop - c.start, PACK], BF16, "woven%d" % i, over="raw_wv", shift=8 * c.start) for i, c in enumerate(PIECES)]
         for t in range(2):
             for u in range(2):
                 cols = slice(T // 2 * u, T // 2 * (u + 1))
                 nc.scalar.copy(pair01[:, t, cols], windows[t][:, cols])
         for i, c in enumerate(PIECES):
             nc.scalar.copy(woven[i][:, :, 0:2], pair01[:, :, c].rearrange("p e c -> p c e"))
-        pairs23 = held([P, 4, 2, QUARTER], BF16, "pairs23", tag="gated3")
-        pair23 = [pairs23[:, c.start // QUARTER, :, c.start % QUARTER : c.start % QUARTER + c.stop - c.start] for c in PIECES]
-        nc.gpsimd.tensor_scalar(pairs23[:, :, 0, :], windows[2][:].rearrange("p (q c) -> p q c", q=4), 1.0, -0.0, ALU.mult, ALU.add)
+        pair23 = [held([P, 2, c.stop - c.start], BF16, "pair23_%d" % i, over="pair01", shift=4 * c.start) for i, c in enumerate(SHARES)]
+        for i, c in enumerate(SHARES):
+            nc.scalar.copy(pair23[i][:, 0, :], windows[2][:, c])
 
         out_scales = held([P, T], U8, "out_scales")
-        for i, c in enumerate(PIECES):
-            copy = nc.vector.tensor_copy if i < VECTOR_PIECES else nc.scalar.copy
+        for i, c in enumerate(SHARES):
+            copy = nc.vector.tensor_copy if i < VECTOR_SHARES else nc.scalar.copy
             copy(pair23[i][:, 1, :], windows[3][:, c])
-            copy(woven[i][:, :, 2:4], pair23[i].rearrange("p e c -> p c e"))
-        codes_tags = ("v_words", "v2_words", "picked2_both", "wt_raw", "")
+            piece = max(k for k, whole in enumerate(PIECES) if whole.start <= c.start)
+            first_col = c.start - PIECES[piece].start
+            copy(woven[piece][:, first_col : first_col + c.stop - c.start, 2:4], pair23[i][:].rearrange("p e c -> p c e"))
         for i, c in enumerate(PIECES):
-            out_codes = held([P, c.stop - c.start], U32, "out_codes%d" % i, tag=codes_tags[i])
+            out_codes = held([P, c.stop - c.start], U32, "out_codes%d" % i, over="v_words", shift=4 * c.start)
             nc.vector.quantize_mx(out=out_codes[:].bitcast(FP8X4), scales=out_scales[:, c], in_=woven[i][:].rearrange("p c t -> p (c t)"))
             nc.sync.dma_start(words_view(out_1)[:, c], out_codes[:].bitcast(I32))
         for q in range(4):

@@ -62,36 +62,33 @@ def tile_list_gmu_relu_scatP_kernel(
 
         list1 = lists.tile([P, J // 16], U16, name="list1")
         list2 = lists.tile([P, J // 16], U16, name="list2")
-        reserve("room12", 16 * KIB)
+        for t in range(3):
+            reserve("room%d" % t, 8 * KIB)
         reserve("room_late", 10 * KIB)
         reserve("room3", 8 * KIB)
         v_words = held([P, T], U32, "v_words")
         v2_words = held([P, T], U32, "v2_words")
-        v_scales = held([P, T], U8, "v_scales")
-        v2_scales = held([P, T], U8, "v2_scales")
+        v_scales = held([P, T], U8, "v_scales", over="room2")
+        v2_scales = held([P, T], U8, "v2_scales", over="room0")
         wt_raw = held([P, 2, N], I32, "wt_raw")
-        wt_scales_raw = held([P, 2 * N], U8, "wt_scales_raw")
+        wt_scales_raw = held([P, 2 * N], U8, "wt_scales_raw", over="room1")
         picked2_scales = held([P, J], U8, "picked2_scales")
         planes2 = [held([P, J], U8, "planes2_%d" % a) for a in range(2)]
         raw = {name: held([P, PACK, N], F32, "raw_" + name) for name in ("wv", "zv", "zt0", "zt1")}
         bias = held([P, PACK], F32, "bias")
         weight = held([P, J], F32, "weight")
-        weight_rows = held([P, P], F32, "weight_rows")
         weight_cols = held([P, J // P], F32, "weight_cols")
-        ident = held([P, P], F32, "ident")
 
         warm = held([P, 2], F32, "warm")
         nc.gpsimd.memset(warm[:, 0:1], 0.0)
         nc.scalar.activation(warm[:, 1:2], warm[:, 0:1], ACT.Sigmoid)
 
         for q in range(4):
-            nc.vector.memset(v2_scales[QUADRANT * q : QUADRANT * q + LOADED_ROW, :].bitcast(I32), 0)
+            (nc.gpsimd, nc.vector)[q % 2].memset(v2_scales[QUADRANT * q : QUADRANT * q + LOADED_ROW, :].bitcast(I32), 0)
         nc.vector.memset(wt_scales_raw[:].bitcast(I32), 0)
         nc.vector.memset(v_scales[:].bitcast(I32), 0)
         for plane in planes2:
             nc.gpsimd.memset(plane[:].bitcast(I32), 0)
-        nc.gpsimd.memset(weight_rows[:], 0.0)
-        make_identity(nc, ident[:])
 
         windows = {}
 
@@ -99,8 +96,6 @@ def tile_list_gmu_relu_scatP_kernel(
             windows[t] = held([P, T], F32, "window%d" % t, over=over, shift=shift)
             for i in range(parts):
                 engine.memset(windows[t][:, T // parts * i : T // parts * (i + 1)], 0.0)
-
-        open_window(0, nc.vector, 1)
 
         def words_view(words):
             return words[0].rearrange("p t i -> p (t i)").bitcast(I32)
@@ -135,21 +130,26 @@ def tile_list_gmu_relu_scatP_kernel(
         load_weight("zt0", zt[0:512, :])
         load_weight("zt1", zt[512:1024, :])
         nc.sync.dma_start(weight[:], wgo)
-        nc.sync.dma_start(weight_rows[0 : J // P, :], wgo[0].rearrange("(c p) -> c p", p=P))
 
         both = held([P, J], U32, "picked2_both")
         nc.vector.tensor_copy(both[:], v2_words[:].indirect(list2[:]))
         parted = held([P, 2, 2 * J], U8, "picked2_words")
         nc.vector.tensor_copy(parted[:].bitcast(U16), both[:].bitcast(U16).rearrange("p (j d) -> p d j", d=2))
 
+        weight_rows = held([P, P], F32, "weight_rows", over="v2_words")
+        ident = held([P, P], F32, "ident", over="v2_words", shift=KIB)
+        nc.gpsimd.memset(weight_rows[:], 0.0)
+        nc.sync.dma_start(weight_rows[0 : J // P, :], wgo[0].rearrange("(c p) -> c p", p=P))
+        make_identity(nc, ident[:])
+
         wt_codes, wt_planes = [], []
         for u in range(2):
             wt_codes.append(held([P, 2, 2, P], I32, "wt_codes%d" % u))
             wt_planes.append(held([P, 2, 2, P], U8, "wt_planes%d" % u))
-            nc.gpsimd.tensor_copy(
+            nc.vector.tensor_copy(
                 wt_codes[u][:].rearrange("p a t m -> p a m t"), wt_raw[:].rearrange("p a (m t) -> p a m t", t=PACK)[:, :, :, 2 * u : 2 * u + 2]
             )
-            nc.gpsimd.tensor_copy(wt_planes[u][:], wt_scales_raw[:].rearrange("p (a m t) -> p a t m", a=2, t=PACK)[:, :, 2 * u : 2 * u + 2, :])
+            nc.vector.tensor_copy(wt_planes[u][:], wt_scales_raw[:].rearrange("p (a m t) -> p a t m", a=2, t=PACK)[:, :, 2 * u : 2 * u + 2, :])
         picked_scales = held([P, J], U8, "picked_scales")
         nc.vector.tensor_copy(picked_scales[:], v_scales[:].indirect(list1[:]))
 
@@ -198,7 +198,7 @@ def tile_list_gmu_relu_scatP_kernel(
         quantise_weight("wv", 0, nc.scalar.copy)
         picked_words = held([P, J], U32, "picked_words")
         nc.vector.tensor_copy(picked_words[:], v_words[:].indirect(list1[:]))
-        quantise_weight("wv", 1, nc.scalar.copy, over="room12", shift=7 * KIB)
+        quantise_weight("wv", 1, nc.scalar.copy)
 
         def v_side(h):
             return picked_words[:, items_of(h)].bitcast(FP8X4), picked_scales[:, items_of(h)]
@@ -229,8 +229,8 @@ def tile_list_gmu_relu_scatP_kernel(
         quantise_weight("zt1", 0, nc.scalar.copy, over="room_late")
         for s in range(2, 4):
             make_diff(s, early_diffs[s])
-        open_window(1, nc.gpsimd, 4, "room12")
-        open_window(2, nc.gpsimd, 4, "room12", 8 * KIB)
+        for t in range(3):
+            open_window(t, nc.gpsimd, 4, "room%d" % t)
         make_gate(0)
         make_gate(1)
         late_diffs = held([P, 4, HALF], F32, "diff4567", over="room_late", shift=2 * KIB - 64)

@@ -30,8 +30,8 @@ BLOCKS = HALF // P
 
 STEPS = [(0, 0), (1, 0), (0, 1), (1, 1), (2, 0), (3, 0), (2, 1), (3, 1)]
 PIECES = [slice(0, 512), slice(512, 1024), slice(1024, 1536), slice(1536, 1792), slice(1792, 2048)]
-SHARES = [slice(0, 512), slice(512, 1024), slice(1024, 1152), slice(1152, 1536), slice(1536, 1792), slice(1792, 2048)]
-VECTOR_SHARES = 3
+VECTOR_SHARES = [slice(0, 512), slice(512, 896)]
+SCALAR_SHARES = [slice(896, 1024), slice(1024, 1536), slice(1536, 1792), slice(1792, 2048)]
 
 
 def tile_list_gmu_relu_scatP_kernel(
@@ -62,16 +62,15 @@ def tile_list_gmu_relu_scatP_kernel(
 
         list1 = lists.tile([P, J // 16], U16, name="list1")
         list2 = lists.tile([P, J // 16], U16, name="list2")
-        for t in range(3):
-            reserve("room%d" % t, 8 * KIB)
+        reserve("room2", 8 * KIB)
         reserve("room_late", 10 * KIB)
-        reserve("room3", 8 * KIB)
+        reserve("room3", 12 * KIB)
         v_words = held([P, T], U32, "v_words")
         v2_words = held([P, T], U32, "v2_words")
-        v_scales = held([P, T], U8, "v_scales", over="room2")
-        v2_scales = held([P, T], U8, "v2_scales", over="room0")
+        v_scales = held([P, T], U8, "v_scales")
+        v2_scales = held([P, T], U8, "v2_scales")
         wt_raw = held([P, 2, N], I32, "wt_raw")
-        wt_scales_raw = held([P, 2 * N], U8, "wt_scales_raw", over="room1")
+        wt_scales_raw = held([P, 2 * N], U8, "wt_scales_raw", over="room2")
         picked2_scales = held([P, J], U8, "picked2_scales")
         planes2 = [held([P, J], U8, "planes2_%d" % a) for a in range(2)]
         raw = {name: held([P, PACK, N], F32, "raw_" + name) for name in ("wv", "zv", "zt0", "zt1")}
@@ -136,20 +135,12 @@ def tile_list_gmu_relu_scatP_kernel(
         parted = held([P, 2, 2 * J], U8, "picked2_words")
         nc.vector.tensor_copy(parted[:].bitcast(U16), both[:].bitcast(U16).rearrange("p (j d) -> p d j", d=2))
 
-        weight_rows = held([P, P], F32, "weight_rows", over="v2_words")
-        ident = held([P, P], F32, "ident", over="v2_words", shift=KIB)
-        nc.gpsimd.memset(weight_rows[:], 0.0)
-        nc.sync.dma_start(weight_rows[0 : J // P, :], wgo[0].rearrange("(c p) -> c p", p=P))
-        make_identity(nc, ident[:])
-
         wt_codes, wt_planes = [], []
         for u in range(2):
             wt_codes.append(held([P, 2, 2, P], I32, "wt_codes%d" % u))
             wt_planes.append(held([P, 2, 2, P], U8, "wt_planes%d" % u))
-            nc.vector.tensor_copy(
-                wt_codes[u][:].rearrange("p a t m -> p a m t"), wt_raw[:].rearrange("p a (m t) -> p a m t", t=PACK)[:, :, :, 2 * u : 2 * u + 2]
-            )
-            nc.vector.tensor_copy(wt_planes[u][:], wt_scales_raw[:].rearrange("p (a m t) -> p a t m", a=2, t=PACK)[:, :, 2 * u : 2 * u + 2, :])
+            nc.gpsimd.tensor_copy(wt_codes[u][:], wt_raw[:].rearrange("p a (m t) -> p a t m", t=PACK)[:, :, 2 * u : 2 * u + 2, :])
+            nc.gpsimd.tensor_copy(wt_planes[u][:], wt_scales_raw[:].rearrange("p (a m t) -> p a t m", a=2, t=PACK)[:, :, 2 * u : 2 * u + 2, :])
         picked_scales = held([P, J], U8, "picked_scales")
         nc.vector.tensor_copy(picked_scales[:], v_scales[:].indirect(list1[:]))
 
@@ -219,32 +210,35 @@ def tile_list_gmu_relu_scatP_kernel(
             make_at(s)
         quantise_weight("zv", 0, nc.scalar.copy)
         quantise_weight("zt0", 0, nc.scalar.copy)
-        early_diffs = two("diff01", over="room3") + two("diff23")
+        early_diffs = two("diff01", over="room3", shift=8 * KIB - 64) + two("diff23")
         make_at(4)
         make_at(5)
         make_diff(0, early_diffs[0])
         make_diff(1, early_diffs[1])
         make_at(6)
         make_at(7)
-        quantise_weight("zt1", 0, nc.scalar.copy, over="room_late")
+        quantise_weight("zt1", 0, nc.vector.tensor_copy, over="room_late")
         for s in range(2, 4):
             make_diff(s, early_diffs[s])
         for t in range(3):
-            open_window(t, nc.gpsimd, 4, "room%d" % t)
+            open_window(t, nc.gpsimd, 4, "room2" if t == 2 else "")
+        weight_rows = held([P, P], F32, "weight_rows")
+        ident = held([P, P], F32, "ident", over="wt_raw")
+        nc.gpsimd.memset(weight_rows[:], 0.0)
+        nc.sync.dma_start(weight_rows[0 : J // P, :], wgo[0].rearrange("(c p) -> c p", p=P))
+        make_identity(nc, ident[:])
+
         make_gate(0)
         make_gate(1)
         late_diffs = held([P, 4, HALF], F32, "diff4567", over="room_late", shift=2 * KIB - 64)
-        for s in range(4, 8):
+        for s in range(4, 6):
             make_diff(s, late_diffs[:, s - 4, :])
         make_gate(2)
         make_gate(3)
         turned_weight = psum.tile([P, P], F32, name="turned_weight", tag="bank0")
         nc.tensor.transpose(turned_weight[:], weight_rows[:], ident[:])
         nc.scalar.copy(weight_cols[:], turned_weight[:, 0 : J // P])
-        for name in ("zv", "zt0", "zt1"):
-            quantise_weight(name, 1, nc.scalar.copy)
-        for s in range(4, 8):
-            make_gate(s)
+        quantise_weight("zv", 1, nc.scalar.copy)
 
         rows_of = out_0.rearrange("(p t) c -> t p c", t=PACK)
 
@@ -260,7 +254,7 @@ def tile_list_gmu_relu_scatP_kernel(
         reserve("room_result5", 2 * KIB)
         reserve("room_result6", 2 * KIB)
         result_rooms = {5: ("room_result5", 0), 6: ("room_result6", 0)}
-        last_blocks = ("", "room_result6", "room_result5", "raw_zt0")
+        last_blocks = (("", 0), ("room_result6", 0), ("room_result5", 0), ("raw_zt0", 4 * KIB - 256))
 
         def result_of(s):
             over, shift = result_rooms.get(s, ("gate%d" % s, 0))
@@ -279,11 +273,11 @@ def tile_list_gmu_relu_scatP_kernel(
                 cols = slice(P * c, P * (c + 1))
                 nc.tensor.matmul(summed[:, c, :], lhsT=ats[s][:, cols], rhs=ident[:], is_transpose=True, start=True, stop=False)
                 nc.tensor.matmul(summed[:, c, :], lhsT=gated[:, cols], rhs=ident[:], is_transpose=True, start=False, stop=True)
-            weighted = [held([P, P], F32, "weighted%d_%d" % (s, c), over=last_blocks[c] if s == 4 else "") for c in range(BLOCKS)]
+            weighted = [held([P, P], F32, "weighted%d_%d" % (s, c), over=last_blocks[c][0] if s == 4 else "", shift=last_blocks[c][1]) for c in range(BLOCKS)]
             for c in range(BLOCKS):
                 col = BLOCKS * h + c
                 nc.scalar.activation(weighted[c][:], summed[:, c, :], ACT.Copy, scale=weight_cols[:, col : col + 1])
-            turned = psum.tile([P, BLOCKS, P], F32, name="turned%d" % s, tag="bank%d" % (s - 1))
+            turned = psum.tile([P, BLOCKS, P], F32, name="turned%d" % s, tag="bank%d" % (s + 3))
             for c in range(BLOCKS):
                 nc.tensor.transpose(turned[:, c, :], weighted[c][:], ident[:])
             result = result_of(s)
@@ -298,36 +292,47 @@ def tile_list_gmu_relu_scatP_kernel(
         nc.vector.tensor_tensor(first[:], first[:], ats[0], ALU.add)
         result = result_of(0)
         nc.vector.tensor_tensor(result[:], first[:], weight[:, items_of(0)], ALU.mult)
+        for s in range(6, 8):
+            make_diff(s, late_diffs[:, s - 4, :])
         place(0, result)
         finish_by_transposes(1, second)
+        quantise_weight("zt0", 1, nc.scalar.copy, over="room3", shift=8 * KIB)
+        quantise_weight("zt1", 1, nc.scalar.copy, over="room3", shift=10 * KIB)
         gated = held([P, 6, HALF], F32, "gated", over="room_first")
         for s in range(2, 5):
+            make_gate(s + 2)
             nc.gpsimd.tensor_tensor(gated[:, s - 2, :], diffs[s], gates[s][:], ALU.mult)
             finish_by_transposes(s, gated[:, s - 2, :])
+        make_gate(7)
         open_window(3, nc.gpsimd, 4, "room3")
         for s in range(5, 8):
             nc.gpsimd.tensor_tensor(gated[:, s - 2, :], diffs[s], gates[s][:], ALU.mult)
             finish_on_gpsimd(s, gated[:, s - 2, :])
 
-        pair01 = held([P, 2, T], BF16, "pair01", over="raw_zt0")
+        pair01 = [held([P, 2, T // 2], BF16, "pair01_%d" % u, over="raw_zt0", shift=4 * KIB * u) for u in range(2)]
         woven = [held([P, c.stop - c.start, PACK], BF16, "woven%d" % i, over="raw_wv", shift=8 * c.start) for i, c in enumerate(PIECES)]
+
+        def woven_cols(c, first, last):
+            piece = max(k for k, whole in enumerate(PIECES) if whole.start <= c.start)
+            start = c.start - PIECES[piece].start
+            return woven[piece][:, start : start + c.stop - c.start, first:last]
+
         for t in range(2):
             for u in range(2):
-                cols = slice(T // 2 * u, T // 2 * (u + 1))
-                nc.scalar.copy(pair01[:, t, cols], windows[t][:, cols])
-        for i, c in enumerate(PIECES):
-            nc.scalar.copy(woven[i][:, :, 0:2], pair01[:, :, c].rearrange("p e c -> p c e"))
-        pair23 = [held([P, 2, c.stop - c.start], BF16, "pair23_%d" % i, over="pair01", shift=4 * c.start) for i, c in enumerate(SHARES)]
-        for i, c in enumerate(SHARES):
-            nc.scalar.copy(pair23[i][:, 0, :], windows[2][:, c])
+                nc.scalar.copy(pair01[u][:, t, :], windows[t][:, T // 2 * u : T // 2 * (u + 1)])
+        for c in PIECES:
+            u, start = divmod(c.start, T // 2)
+            nc.scalar.copy(woven_cols(c, 0, 2), pair01[u][:, :, start : start + c.stop - c.start].rearrange("p e c -> p c e"))
+        for t in (2, 3):
+            for c in SCALAR_SHARES:
+                nc.scalar.copy(woven_cols(c, t, t + 1), windows[t][:, c].unsqueeze(2))
+        for i, c in enumerate(VECTOR_SHARES):
+            pair23 = held([P, 2, c.stop - c.start], BF16, "pair23_%d" % i, over="gated", shift=2 * KIB * i)
+            nc.gpsimd.tensor_scalar(pair23[:, 0, :], windows[2][:, c], 1.0, -0.0, ALU.mult, ALU.add)
+            nc.vector.tensor_copy(pair23[:, 1, :], windows[3][:, c])
+            nc.vector.tensor_copy(woven_cols(c, 2, 4), pair23[:].rearrange("p e c -> p c e"))
 
         out_scales = held([P, T], U8, "out_scales")
-        for i, c in enumerate(SHARES):
-            copy = nc.vector.tensor_copy if i < VECTOR_SHARES else nc.scalar.copy
-            copy(pair23[i][:, 1, :], windows[3][:, c])
-            piece = max(k for k, whole in enumerate(PIECES) if whole.start <= c.start)
-            first_col = c.start - PIECES[piece].start
-            copy(woven[piece][:, first_col : first_col + c.stop - c.start, 2:4], pair23[i][:].rearrange("p e c -> p c e"))
         for i, c in enumerate(PIECES):
             out_codes = held([P, c.stop - c.start], U32, "out_codes%d" % i, over="v_words", shift=4 * c.start)
             nc.vector.quantize_mx(out=out_codes[:].bitcast(FP8X4), scales=out_scales[:, c], in_=woven[i][:].rearrange("p c t -> p (c t)"))

@@ -30,8 +30,8 @@ BLOCKS = HALF // P
 
 STEPS = [(0, 0), (1, 0), (0, 1), (1, 1), (2, 0), (3, 0), (2, 1), (3, 1)]
 PIECES = [slice(0, 512), slice(512, 1024), slice(1024, 1536), slice(1536, 1792), slice(1792, 2048)]
-VECTOR_SHARES = [slice(0, 512), slice(512, 896)]
-SCALAR_SHARES = [slice(896, 1024), slice(1024, 1536), slice(1536, 1792), slice(1792, 2048)]
+SHARES = [slice(0, 512), slice(512, 1024), slice(1024, 1152), slice(1152, 1536), slice(1536, 1792), slice(1792, 2048)]
+VECTOR_SHARES = 3
 
 
 def tile_list_gmu_relu_scatP_kernel(
@@ -238,23 +238,30 @@ def tile_list_gmu_relu_scatP_kernel(
         turned_weight = psum.tile([P, P], F32, name="turned_weight", tag="bank0")
         nc.tensor.transpose(turned_weight[:], weight_rows[:], ident[:])
         nc.scalar.copy(weight_cols[:], turned_weight[:, 0 : J // P])
-        quantise_weight("zv", 1, nc.scalar.copy)
+        for name in ("zv", "zt0", "zt1"):
+            quantise_weight(name, 1, nc.scalar.copy)
+        make_gate(4)
 
         rows_of = out_0.rearrange("(p t) c -> t p c", t=PACK)
 
         def offsets_of(h):
             return list1[:, LIST_COLS * h : LIST_COLS * (h + 1)]
 
+        joined = [held([P, 2, T // 2], F32, "joined%d" % u, over="raw_zt%d" % u) for u in range(2)]
+
         def place(s, result):
             t, h = STEPS[s]
             nc.vector.tensor_copy(windows[t][:].indirect(offsets_of(h)), result[:])
+            if h == 1 and t < 2:
+                for u in range(2):
+                    nc.sync.dma_start(joined[u][:, t, :], windows[t][:, T // 2 * u : T // 2 * (u + 1)])
             if h == 1:
                 nc.sync.dma_start(rows_of[t], windows[t][:])
 
         reserve("room_result5", 2 * KIB)
         reserve("room_result6", 2 * KIB)
         result_rooms = {5: ("room_result5", 0), 6: ("room_result6", 0)}
-        last_blocks = (("", 0), ("room_result6", 0), ("room_result5", 0), ("raw_zt0", 4 * KIB - 256))
+        last_blocks = (("", 0), ("room_result6", 0), ("room_result5", 0), ("", 0))
 
         def result_of(s):
             over, shift = result_rooms.get(s, ("gate%d" % s, 0))
@@ -277,7 +284,7 @@ def tile_list_gmu_relu_scatP_kernel(
             for c in range(BLOCKS):
                 col = BLOCKS * h + c
                 nc.scalar.activation(weighted[c][:], summed[:, c, :], ACT.Copy, scale=weight_cols[:, col : col + 1])
-            turned = psum.tile([P, BLOCKS, P], F32, name="turned%d" % s, tag="bank%d" % (s + 3))
+            turned = psum.tile([P, BLOCKS, P], F32, name="turned%d" % s, tag="bank%d" % (s - 1))
             for c in range(BLOCKS):
                 nc.tensor.transpose(turned[:, c, :], weighted[c][:], ident[:])
             result = result_of(s)
@@ -296,20 +303,17 @@ def tile_list_gmu_relu_scatP_kernel(
             make_diff(s, late_diffs[:, s - 4, :])
         place(0, result)
         finish_by_transposes(1, second)
-        quantise_weight("zt0", 1, nc.scalar.copy, over="room3", shift=8 * KIB)
-        quantise_weight("zt1", 1, nc.scalar.copy, over="room3", shift=10 * KIB)
+        for s in range(5, 8):
+            make_gate(s)
         gated = held([P, 6, HALF], F32, "gated", over="room_first")
         for s in range(2, 5):
-            make_gate(s + 2)
             nc.gpsimd.tensor_tensor(gated[:, s - 2, :], diffs[s], gates[s][:], ALU.mult)
             finish_by_transposes(s, gated[:, s - 2, :])
-        make_gate(7)
         open_window(3, nc.gpsimd, 4, "room3")
         for s in range(5, 8):
             nc.gpsimd.tensor_tensor(gated[:, s - 2, :], diffs[s], gates[s][:], ALU.mult)
             finish_on_gpsimd(s, gated[:, s - 2, :])
 
-        pair01 = [held([P, 2, T // 2], BF16, "pair01_%d" % u, over="raw_zt0", shift=4 * KIB * u) for u in range(2)]
         woven = [held([P, c.stop - c.start, PACK], BF16, "woven%d" % i, over="raw_wv", shift=8 * c.start) for i, c in enumerate(PIECES)]
 
         def woven_cols(c, first, last):
@@ -317,20 +321,18 @@ def tile_list_gmu_relu_scatP_kernel(
             start = c.start - PIECES[piece].start
             return woven[piece][:, start : start + c.stop - c.start, first:last]
 
-        for t in range(2):
-            for u in range(2):
-                nc.scalar.copy(pair01[u][:, t, :], windows[t][:, T // 2 * u : T // 2 * (u + 1)])
         for c in PIECES:
             u, start = divmod(c.start, T // 2)
-            nc.scalar.copy(woven_cols(c, 0, 2), pair01[u][:, :, start : start + c.stop - c.start].rearrange("p e c -> p c e"))
-        for t in (2, 3):
-            for c in SCALAR_SHARES:
-                nc.scalar.copy(woven_cols(c, t, t + 1), windows[t][:, c].unsqueeze(2))
-        for i, c in enumerate(VECTOR_SHARES):
-            pair23 = held([P, 2, c.stop - c.start], BF16, "pair23_%d" % i, over="gated", shift=2 * KIB * i)
-            nc.gpsimd.tensor_scalar(pair23[:, 0, :], windows[2][:, c], 1.0, -0.0, ALU.mult, ALU.add)
-            nc.vector.tensor_copy(pair23[:, 1, :], windows[3][:, c])
-            nc.vector.tensor_copy(woven_cols(c, 2, 4), pair23[:].rearrange("p e c -> p c e"))
+            nc.scalar.copy(woven_cols(c, 0, 2), joined[u][:, :, start : start + c.stop - c.start].rearrange("p e c -> p c e"))
+        for i, c in enumerate(SHARES):
+            copy = nc.vector.tensor_copy if i < VECTOR_SHARES else nc.scalar.copy
+            pair23 = held([P, 2, c.stop - c.start], BF16, "pair23_%d" % i, over="gated" if i < VECTOR_SHARES else "joined1", shift=4 * c.start)
+            if i < VECTOR_SHARES:
+                nc.gpsimd.tensor_scalar(pair23[:, 0, :], windows[2][:, c], 1.0, -0.0, ALU.mult, ALU.add)
+            else:
+                nc.scalar.copy(pair23[:, 0, :], windows[2][:, c])
+            copy(pair23[:, 1, :], windows[3][:, c])
+            copy(woven_cols(c, 2, 4), pair23[:].rearrange("p e c -> p c e"))
 
         out_scales = held([P, T], U8, "out_scales")
         for i, c in enumerate(PIECES):

@@ -62,15 +62,15 @@ def tile_list_gmu_relu_scatP_kernel(
 
         list1 = lists.tile([P, J // 16], U16, name="list1")
         list2 = lists.tile([P, J // 16], U16, name="list2")
-        reserve("room2", 8 * KIB)
+        for t in range(4):
+            reserve("room%d" % t, 8 * KIB)
         reserve("room_late", 10 * KIB)
-        reserve("room3", 12 * KIB)
         v_words = held([P, T], U32, "v_words")
         v2_words = held([P, T], U32, "v2_words")
         v_scales = held([P, T], U8, "v_scales")
-        v2_scales = held([P, T], U8, "v2_scales")
+        v2_scales = held([P, T], U8, "v2_scales", over="room0")
         wt_raw = held([P, 2, N], I32, "wt_raw")
-        wt_scales_raw = held([P, 2 * N], U8, "wt_scales_raw", over="room2")
+        wt_scales_raw = held([P, 2 * N], U8, "wt_scales_raw", over="room1")
         picked2_scales = held([P, J], U8, "picked2_scales")
         planes2 = [held([P, J], U8, "planes2_%d" % a) for a in range(2)]
         raw = {name: held([P, PACK, N], F32, "raw_" + name) for name in ("wv", "zv", "zt0", "zt1")}
@@ -87,7 +87,12 @@ def tile_list_gmu_relu_scatP_kernel(
         nc.vector.memset(wt_scales_raw[:].bitcast(I32), 0)
         nc.vector.memset(v_scales[:].bitcast(I32), 0)
         for plane in planes2:
-            nc.gpsimd.memset(plane[:].bitcast(I32), 0)
+            nc.vector.memset(plane[:].bitcast(I32), 0)
+
+        weight_rows = held([P, P], F32, "weight_rows")
+        ident = held([P, P], F32, "ident")
+        nc.gpsimd.memset(weight_rows[:], 0.0)
+        make_identity(nc, ident[:])
 
         windows = {}
 
@@ -129,6 +134,7 @@ def tile_list_gmu_relu_scatP_kernel(
         load_weight("zt0", zt[0:512, :])
         load_weight("zt1", zt[512:1024, :])
         nc.sync.dma_start(weight[:], wgo)
+        nc.sync.dma_start(weight_rows[0 : J // P, :], wgo[0].rearrange("(c p) -> c p", p=P))
 
         both = held([P, J], U32, "picked2_both")
         nc.vector.tensor_copy(both[:], v2_words[:].indirect(list2[:]))
@@ -139,8 +145,10 @@ def tile_list_gmu_relu_scatP_kernel(
         for u in range(2):
             wt_codes.append(held([P, 2, 2, P], I32, "wt_codes%d" % u))
             wt_planes.append(held([P, 2, 2, P], U8, "wt_planes%d" % u))
-            nc.gpsimd.tensor_copy(wt_codes[u][:], wt_raw[:].rearrange("p a (m t) -> p a t m", t=PACK)[:, :, 2 * u : 2 * u + 2, :])
-            nc.gpsimd.tensor_copy(wt_planes[u][:], wt_scales_raw[:].rearrange("p (a m t) -> p a t m", a=2, t=PACK)[:, :, 2 * u : 2 * u + 2, :])
+            nc.vector.tensor_copy(
+                wt_codes[u][:].rearrange("p a t m -> p a m t"), wt_raw[:].rearrange("p a (m t) -> p a m t", t=PACK)[:, :, :, 2 * u : 2 * u + 2]
+            )
+            nc.vector.tensor_copy(wt_planes[u][:], wt_scales_raw[:].rearrange("p (a m t) -> p a t m", a=2, t=PACK)[:, :, 2 * u : 2 * u + 2, :])
         picked_scales = held([P, J], U8, "picked_scales")
         nc.vector.tensor_copy(picked_scales[:], v_scales[:].indirect(list1[:]))
 
@@ -186,7 +194,7 @@ def tile_list_gmu_relu_scatP_kernel(
             ht = product(s, "ht", [(wt_side(t, a), v2_side(h, a)) for a in range(2)])
             nc.scalar.activation(ats[s], ht[:], ACT.Relu)
 
-        quantise_weight("wv", 0, nc.scalar.copy)
+        quantise_weight("wv", 0, nc.scalar.copy, over="room2")
         picked_words = held([P, J], U32, "picked_words")
         nc.vector.tensor_copy(picked_words[:], v_words[:].indirect(list1[:]))
         quantise_weight("wv", 1, nc.scalar.copy)
@@ -210,7 +218,7 @@ def tile_list_gmu_relu_scatP_kernel(
             make_at(s)
         quantise_weight("zv", 0, nc.scalar.copy)
         quantise_weight("zt0", 0, nc.scalar.copy)
-        early_diffs = two("diff01", over="room3", shift=8 * KIB - 64) + two("diff23")
+        early_diffs = two("diff01") + two("diff23")
         make_at(4)
         make_at(5)
         make_diff(0, early_diffs[0])
@@ -221,13 +229,7 @@ def tile_list_gmu_relu_scatP_kernel(
         for s in range(2, 4):
             make_diff(s, early_diffs[s])
         for t in range(3):
-            open_window(t, nc.gpsimd, 4, "room2" if t == 2 else "")
-        weight_rows = held([P, P], F32, "weight_rows")
-        ident = held([P, P], F32, "ident", over="wt_raw")
-        nc.gpsimd.memset(weight_rows[:], 0.0)
-        nc.sync.dma_start(weight_rows[0 : J // P, :], wgo[0].rearrange("(c p) -> c p", p=P))
-        make_identity(nc, ident[:])
-
+            open_window(t, nc.gpsimd, 1, "room%d" % t)
         make_gate(0)
         make_gate(1)
         late_diffs = held([P, 4, HALF], F32, "diff4567", over="room_late", shift=2 * KIB - 64)
@@ -239,7 +241,8 @@ def tile_list_gmu_relu_scatP_kernel(
         nc.tensor.transpose(turned_weight[:], weight_rows[:], ident[:])
         nc.scalar.copy(weight_cols[:], turned_weight[:, 0 : J // P])
         for name in ("zv", "zt0", "zt1"):
-            quantise_weight(name, 1, nc.scalar.copy)
+            quantise_weight(name, 1, nc.scalar.copy, over="room3" if name == "zt1" else "")
+        open_window(3, nc.gpsimd, 1, "room3")
         make_gate(4)
 
         rows_of = out_0.rearrange("(p t) c -> t p c", t=PACK)
@@ -309,7 +312,6 @@ def tile_list_gmu_relu_scatP_kernel(
         for s in range(2, 5):
             nc.gpsimd.tensor_tensor(gated[:, s - 2, :], diffs[s], gates[s][:], ALU.mult)
             finish_by_transposes(s, gated[:, s - 2, :])
-        open_window(3, nc.gpsimd, 4, "room3")
         for s in range(5, 8):
             nc.gpsimd.tensor_tensor(gated[:, s - 2, :], diffs[s], gates[s][:], ALU.mult)
             finish_on_gpsimd(s, gated[:, s - 2, :])

@@ -78,10 +78,6 @@ def tile_list_gmu_relu_scatP_kernel(
         weight = held([P, J], F32, "weight")
         weight_cols = held([P, J // P], F32, "weight_cols")
 
-        warm = held([P, 2], F32, "warm")
-        nc.gpsimd.memset(warm[:, 0:1], 0.0)
-        nc.scalar.activation(warm[:, 1:2], warm[:, 0:1], ACT.Sigmoid)
-
         for q in range(4):
             (nc.gpsimd, nc.vector)[q % 2].memset(v2_scales[QUADRANT * q : QUADRANT * q + LOADED_ROW, :].bitcast(I32), 0)
         nc.vector.memset(wt_scales_raw[:].bitcast(I32), 0)

@@ -21,17 +21,17 @@ P = 128
 PACK = 4
 HALF = 512
 QUADRANT = 32
-QUARTER = T // 4
 LIST_COLS = HALF // 16
 LOADED_ROW = QUADRANT - 8
 MOVED_ROWS = 3 * QUADRANT + 4
-KIB = 1024
+SLABS = N // P
+MATS = 4
+GROUPS = 4
 BLOCKS = HALF // P
-
-STEPS = [(0, 0), (1, 0), (0, 1), (1, 1), (2, 0), (3, 0), (2, 1), (3, 1)]
-PIECES = [slice(0, 512), slice(512, 1024), slice(1024, 1536), slice(1536, 1792), slice(1792, 2048)]
-SHARES = [slice(0, 512), slice(512, 1024), slice(1024, 1152), slice(1152, 1536), slice(1536, 1792), slice(1792, 2048)]
-VECTOR_SHARES = 3
+ZT0, ZT1, ZV, WV = range(MATS)
+HT_BANKS = ((0, 1), (2, 0), (1, 3), (2, 0))
+HV_BANKS = ((0, 3), (2, 0), (1, 3), (4, 5))
+Z_BANKS = ((2, 1), (4, 5), (2, 0), (1, 3))
 
 
 def tile_list_gmu_relu_scatP_kernel(
@@ -48,54 +48,36 @@ def tile_list_gmu_relu_scatP_kernel(
 
         def reserve(name, size):
             places[name] = places["free"]
-            places["free"] = places["free"] + size
+            places["free"] = places["free"] + (size + 63) // 64 * 64
 
         def held(shape, dtype, name, over="", shift=0):
-            if not over:
+            if over:
+                places[name] = places[over] + shift
+            else:
                 size = sizes[dtype]
                 for count in shape[1:]:
                     size = size * count
-                reserve(name, (size + 63) // 64 * 64)
-            else:
-                places[name] = places[over] + shift
+                reserve(name, size)
             return keep.tile(shape, dtype, name=name, align_bytes=64, offset=places[name])
+
+        def bank(shape, name, number):
+            return psum.tile(shape, F32, name=name, tag="bank%d" % number)
 
         list1 = lists.tile([P, J // 16], U16, name="list1")
         list2 = lists.tile([P, J // 16], U16, name="list2")
-        for t in range(4):
-            reserve("room%d" % t, 8 * KIB)
-        reserve("room_late", 10 * KIB)
         v_words = held([P, T], U32, "v_words")
         v2_words = held([P, T], U32, "v2_words")
         v_scales = held([P, T], U8, "v_scales")
-        v2_scales = held([P, T], U8, "v2_scales", over="room0")
-        wt_raw = held([P, 2, N], I32, "wt_raw")
-        wt_scales_raw = held([P, 2 * N], U8, "wt_scales_raw", over="room1")
-        picked2_scales = held([P, J], U8, "picked2_scales")
+        v2_scales = held([P, T], U8, "v2_scales")
+        wt_codes = [held([P, 2, 2 * P], I32, "wt_codes%d" % u) for u in range(2)]
+        wt_planes = held([P, 2 * N], U8, "wt_planes")
         planes2 = [held([P, J], U8, "planes2_%d" % a) for a in range(2)]
-        raw = {name: held([P, PACK, N], F32, "raw_" + name) for name in ("wv", "zv", "zt0", "zt1")}
-        bias = held([P, PACK], F32, "bias")
+        raw = [held([P, MATS, PACK, 2 * P], F32, "raw%d" % u) for u in range(2)]
+        bias = held([P, SLABS], F32, "bias")
         weight = held([P, J], F32, "weight")
-        weight_cols = held([P, J // P], F32, "weight_cols")
-
-        for q in range(4):
-            (nc.gpsimd, nc.vector)[q % 2].memset(v2_scales[QUADRANT * q : QUADRANT * q + LOADED_ROW, :].bitcast(I32), 0)
-        nc.vector.memset(wt_scales_raw[:].bitcast(I32), 0)
-        nc.vector.memset(v_scales[:].bitcast(I32), 0)
-        for plane in planes2:
-            nc.vector.memset(plane[:].bitcast(I32), 0)
-
-        weight_rows = held([P, P], F32, "weight_rows")
+        weight_cols = held([P, BLOCKS], F32, "weight_cols")
+        windows = [held([P, T], F32, "window0")]
         ident = held([P, P], F32, "ident")
-        nc.gpsimd.memset(weight_rows[:], 0.0)
-        make_identity(nc, ident[:])
-
-        windows = {}
-
-        def open_window(t, engine, parts, over="", shift=0):
-            windows[t] = held([P, T], F32, "window%d" % t, over=over, shift=shift)
-            for i in range(parts):
-                engine.memset(windows[t][:, T // parts * i : T // parts * (i + 1)], 0.0)
 
         def words_view(words):
             return words[0].rearrange("p t i -> p (t i)").bitcast(I32)
@@ -103,65 +85,104 @@ def tile_list_gmu_relu_scatP_kernel(
         def scale_rows(tile, q, first, count):
             return tile[QUADRANT * q + first : QUADRANT * q + first + count, :].bitcast(I32)
 
-        def load_weight(name, rows):
-            nc.sync.dma_start(raw[name][:], rows.rearrange("(p j) n -> p j n", j=PACK))
+        for plane in (v_scales, wt_planes):
+            nc.gpsimd.memset(plane[:].bitcast(I32), 0)
+        for q in range(4):
+            nc.vector.memset(v2_scales[QUADRANT * q : QUADRANT * q + LOADED_ROW, :].bitcast(I32), 0)
+        for q in range(4):
+            nc.gpsimd.dma_start(scale_rows(v_scales, q, 0, 4), tab_scales[0, 4 * q : 4 * q + 4, :].bitcast(I32))
+        for plane in planes2:
+            nc.gpsimd.memset(plane[:].bitcast(I32), 0)
+        nc.gpsimd.memset(windows[0][:], 0.0)
+        make_identity(nc, ident[:])
+
+        sources = [zt[0:512, :], zt[512:1024, :], zv, wv]
+
+        def load_weights(u, mats):
+            for m in mats:
+                nc.sync.dma_start(raw[u][:, m], sources[m].rearrange("(p j) n -> p j n", j=PACK)[:, :, 2 * P * u : 2 * P * (u + 1)])
+
+        def load_wt(u):
+            nc.sync.dma_start(wt_codes[u][:], wt_words.rearrange("a p n i -> p a (n i)").bitcast(I32)[:, :, 2 * P * u : 2 * P * (u + 1)])
 
         nc.sync.dma_start(list2[:], offs2)
         for q in range(4):
             nc.sync.dma_start(scale_rows(v2_scales, q, LOADED_ROW, 8), tab2_scales[:, 4 * q : 4 * q + 4, :].bitcast(I32))
         nc.sync.dma_start(v2_words[:].bitcast(I32), words_view(tab2_words))
-        nc.sync.dma_start(wt_raw[:], wt_words.rearrange("a p n i -> p a (n i)").bitcast(I32))
         nc.sync.dma_start(list1[:], offs)
+        nc.sync.dma_start(v_words[:].bitcast(I32), words_view(tab_words))
         for q in range(4):
             nc.sync.dma_start(
-                scale_rows(wt_scales_raw, q, 0, 4).rearrange("r (a n) -> r a n", a=2),
+                scale_rows(wt_planes, q, 0, 4).rearrange("r (a n) -> r a n", a=2),
                 wt_scales[:, 4 * q : 4 * q + 4, :].bitcast(I32).rearrange("a r n -> r a n"),
             )
-        load_weight("wv", wv)
+        load_weights(0, [ZT0, ZT1])
+        picked2_scales = held([P, J], U8, "picked2_scales")
         nc.vector.tensor_copy(picked2_scales[:], v2_scales[:].indirect(list2[:]))
         for a in range(2):
             first_row = LOADED_ROW + 4 * a
             nc.sync.dma_start(planes2[a][0:MOVED_ROWS, :].bitcast(I32), picked2_scales[first_row : first_row + MOVED_ROWS, :].bitcast(I32))
-        for q in range(4):
-            nc.sync.dma_start(scale_rows(v_scales, q, 0, 4), tab_scales[0, 4 * q : 4 * q + 4, :].bitcast(I32))
-        nc.sync.dma_start(v_words[:].bitcast(I32), words_view(tab_words))
-        load_weight("zv", zv)
-        nc.sync.dma_start(bias[:], b.rearrange("(p t) -> p t", t=PACK))
-        load_weight("zt0", zt[0:512, :])
-        load_weight("zt1", zt[512:1024, :])
-        nc.sync.dma_start(weight[:], wgo)
-        nc.sync.dma_start(weight_rows[0 : J // P, :], wgo[0].rearrange("(c p) -> c p", p=P))
+        load_weights(0, [ZV])
+        load_wt(0)
+        load_weights(0, [WV])
+        with nc.allow_non_contiguous_dma(reason="one value a partition and column"):
+            nc.sync.dma_start(bias[:], b.rearrange("(w p) -> p w", p=P))
+            nc.sync.dma_start(weight[:, 0:HALF], wgo[:, 0:HALF])
+            load_wt(1)
+            load_weights(1, [WV, ZV])
+            nc.sync.dma_start(weight[:, HALF:J], wgo[:, HALF:J])
+            load_weights(1, [ZT0, ZT1])
+            nc.sync.dma_start(weight_cols[:], wgo[0, HALF:J].rearrange("(c p) -> p c", p=P))
 
-        both = held([P, J], U32, "picked2_both")
-        nc.vector.tensor_copy(both[:], v2_words[:].indirect(list2[:]))
-        parted = held([P, 2, 2 * J], U8, "picked2_words")
-        nc.vector.tensor_copy(parted[:].bitcast(U16), both[:].bitcast(U16).rearrange("p (j d) -> p d j", d=2))
+        def items_of(h):
+            return slice(HALF * h, HALF * (h + 1))
 
-        wt_codes, wt_planes = [], []
-        for u in range(2):
-            wt_codes.append(held([P, 2, 2, P], I32, "wt_codes%d" % u))
-            wt_planes.append(held([P, 2, 2, P], U8, "wt_planes%d" % u))
-            nc.vector.tensor_copy(
-                wt_codes[u][:].rearrange("p a t m -> p a m t"), wt_raw[:].rearrange("p a (m t) -> p a m t", t=PACK)[:, :, :, 2 * u : 2 * u + 2]
+        def offsets_of(tile, h):
+            return tile[:, LIST_COLS * h : LIST_COLS * (h + 1)]
+
+        reserve("room_window1", 4 * T)
+        reserve("room_scales", J)
+        reserve("room_window2", 4 * T)
+
+        def open_window(i):
+            windows.append(held([P, T], F32, "window%d" % i, over="room_window%d" % i))
+            nc.gpsimd.memset(windows[i][:], 0.0)
+
+        codes = {w: held([P, MATS * P], U32, "codes%d" % w) for w in range(2)}
+        scales = [held([P, MATS * P], U8, "scales%d" % w) for w in range(SLABS)]
+
+        def rounded(name, count, over=""):
+            return held([P, count, P, PACK], BF16, name, over=over)
+
+        def round_weight(copy, grouped, i, w, m):
+            copy(
+                grouped[:, i].rearrange("p (c i) j -> p c j i", i=4),
+                raw[w // 2][:, m, :, P * (w % 2) : P * (w % 2 + 1)].rearrange("p j (c i) -> p c j i", i=4),
             )
-            nc.vector.tensor_copy(wt_planes[u][:], wt_scales_raw[:].rearrange("p (a m t) -> p a t m", a=2, t=PACK)[:, :, 2 * u : 2 * u + 2, :])
-        picked_scales = held([P, J], U8, "picked_scales")
-        nc.vector.tensor_copy(picked_scales[:], v_scales[:].indirect(list1[:]))
 
-        quantised = {}
+        def quantise(grouped, w, first, count):
+            cols = slice(P * first, P * (first + count))
+            nc.vector.quantize_mx(
+                out=codes[w][:, cols].bitcast(FP8X4), scales=scales[w][:, cols],
+                in_=grouped[:].rearrange("p a c j -> p (a c j)"),
+            )
 
-        def quantise_weight(name, u, copy, over="", shift=0):
-            grouped = held([P, 2, P, PACK], BF16, "grouped_%s_%d" % (name, u), over=over, shift=shift)
-            copy(grouped[:].rearrange("p t m j -> p m j t"), raw[name][:].rearrange("p j (m t) -> p m j t", t=PACK)[:, :, :, 2 * u : 2 * u + 2])
-            codes = held([P, 2 * P], U32, "codes_%s_%d" % (name, u))
-            scales = held([P, 2 * P], U8, "scales_%s_%d" % (name, u))
-            nc.vector.quantize_mx(out=codes[:].bitcast(FP8X4), scales=scales[:], in_=grouped[:].rearrange("p t m j -> p (t m j)"))
-            for i in range(2):
-                cols = slice(P * i, P * (i + 1))
-                quantised[name, 2 * u + i] = (codes[:, cols].bitcast(FP8X4), scales[:, cols])
+        def made_side(w, m):
+            cols = slice(P * m, P * (m + 1))
+            return codes[w][:, cols].bitcast(FP8X4), scales[w][:, cols]
 
-        def product(s, name, passes):
-            acc = psum.tile([P, HALF], F32, name="%s%d" % (name, s), tag="bank%d" % s)
+        def wt_side(w, a):
+            first = P * (w % 2)
+            return wt_codes[w // 2][:, a, first : first + P].bitcast(FP8X4), wt_planes[:, N * a + P * w : N * a + P * (w + 1)]
+
+        def v_side(h):
+            return picked_words[:, items_of(h)].bitcast(FP8X4), picked_scales[:, items_of(h)]
+
+        def v2_side(h, a):
+            return parted[:, a, 2 * HALF * h : 2 * HALF * (h + 1)].bitcast(FP4X4), planes2[a][:, items_of(h)]
+
+        def product(name, number, passes):
+            acc = bank([P, HALF], name, number)
             for i, (lhs, rhs) in enumerate(passes):
                 nc.tensor.matmul_mx(
                     out=acc[:], lhsT=lhs[0], lhsT_scale=lhs[1], rhs=rhs[0], rhs_scale=rhs[1],
@@ -169,173 +190,197 @@ def tile_list_gmu_relu_scatP_kernel(
                 )
             return acc
 
-        def items_of(h):
-            return slice(HALF * h, HALF * (h + 1))
+        both_ats = [held([P, J], F32, "ats%d" % w) for w in range(SLABS)]
+        ats = {(w, h): both_ats[w][:, items_of(h)] for w in range(SLABS) for h in range(2)}
+        gates = [held([P, J], F32, "gates%d" % w) for w in range(SLABS)]
+        gated = held([P, J], F32, "gated")
+        values = [held([P, J], F32, "values%d" % r) for r in range(SLABS)]
 
-        def v2_side(h, a):
-            return parted[:, a, 2 * HALF * h : 2 * HALF * (h + 1)].bitcast(FP4X4), planes2[a][:, items_of(h)]
+        def value_of(w, h):
+            return values[w][:, items_of(h)]
 
-        def wt_side(t, a):
-            return wt_codes[t // 2][:, a, t % 2, :].bitcast(FP8X4), wt_planes[t // 2][:, a, t % 2, :]
+        def make_gate(w, h):
+            z = product("z%d_%d" % (w, h), Z_BANKS[w][h], [(made_side(w, ZT0), v2_side(h, 0)), (made_side(w, ZT1), v2_side(h, 1)), (made_side(w, ZV), v_side(h))])
+            nc.scalar.activation(gates[w][:, items_of(h)], z[:], ACT.Sigmoid, bias=bias[:, w : w + 1], scale=1.0)
 
-        def two(name, over="", shift=0):
-            pair = held([P, 2, HALF], F32, name, over=over, shift=shift)
-            return pair[:, 0, :], pair[:, 1, :]
+        def make_ht(w, h):
+            return product("ht%d_%d" % (w, h), HT_BANKS[w][h], [(wt_side(w, a), v2_side(h, a)) for a in range(2)])
 
-        ats = two("at01") + two("at23") + two("at45") + two("at67")
-        diffs, gates = {}, {}
+        def make_at(w, h):
+            nc.scalar.activation(ats[w, h], make_ht(w, h)[:], ACT.Relu)
 
-        def make_at(s):
-            t, h = STEPS[s]
-            ht = product(s, "ht", [(wt_side(t, a), v2_side(h, a)) for a in range(2)])
-            nc.scalar.activation(ats[s], ht[:], ACT.Relu)
+        def make_diff(w, h):
+            hv = product("hv%d_%d" % (w, h), HV_BANKS[w][h], [(made_side(w, WV), v_side(h))])
+            nc.vector.scalar_tensor_tensor(value_of(w, h), hv[:], 0.0, ats[w, h], ALU.max, ALU.subtract)
 
-        quantise_weight("wv", 0, nc.scalar.copy, over="room2")
-        picked_words = held([P, J], U32, "picked_words")
-        nc.vector.tensor_copy(picked_words[:], v_words[:].indirect(list1[:]))
-        quantise_weight("wv", 1, nc.scalar.copy)
+        def finish(engine, working, result, w, h):
+            engine.tensor_tensor(working, working, ats[w, h], ALU.add)
+            engine.tensor_tensor(result, working, weight[:, items_of(h)], ALU.mult)
 
-        def v_side(h):
-            return picked_words[:, items_of(h)].bitcast(FP8X4), picked_scales[:, items_of(h)]
+        def block_banks(name, numbers):
+            tiles = {number: bank([P, BLOCKS, P], "%s_%d" % (name, number), number) for number in sorted(set(numbers))}
+            return [tiles[numbers[c]] for c in range(BLOCKS)]
 
-        def make_diff(s, diff):
-            t, h = STEPS[s]
-            hv = product(s, "hv", [(quantised["wv", t], v_side(h))])
-            nc.vector.scalar_tensor_tensor(diff, hv[:], 0.0, ats[s], ALU.max, ALU.subtract)
-            diffs[s] = diff
-
-        def make_gate(s):
-            t, h = STEPS[s]
-            z = product(s, "z", [(quantised["zv", t], v_side(h)), (quantised["zt0", t], v2_side(h, 0)), (quantised["zt1", t], v2_side(h, 1))])
-            gates[s] = held([P, HALF], F32, "gate%d" % s)
-            nc.scalar.activation(gates[s][:], z[:], ACT.Sigmoid, bias=bias[:, t : t + 1], scale=1.0)
-
-        for s in range(4):
-            make_at(s)
-        quantise_weight("zv", 0, nc.scalar.copy)
-        quantise_weight("zt0", 0, nc.scalar.copy)
-        early_diffs = two("diff01") + two("diff23")
-        make_at(4)
-        make_at(5)
-        make_diff(0, early_diffs[0])
-        make_diff(1, early_diffs[1])
-        make_at(6)
-        make_at(7)
-        quantise_weight("zt1", 0, nc.vector.tensor_copy, over="room_late")
-        for s in range(2, 4):
-            make_diff(s, early_diffs[s])
-        for t in range(3):
-            open_window(t, nc.gpsimd, 1, "room%d" % t)
-        make_gate(0)
-        make_gate(1)
-        late_diffs = held([P, 4, HALF], F32, "diff4567", over="room_late", shift=2 * KIB - 64)
-        for s in range(4, 6):
-            make_diff(s, late_diffs[:, s - 4, :])
-        make_gate(2)
-        make_gate(3)
-        turned_weight = psum.tile([P, P], F32, name="turned_weight", tag="bank0")
-        nc.tensor.transpose(turned_weight[:], weight_rows[:], ident[:])
-        nc.scalar.copy(weight_cols[:], turned_weight[:, 0 : J // P])
-        for name in ("zv", "zt0", "zt1"):
-            quantise_weight(name, 1, nc.scalar.copy, over="room3" if name == "zt1" else "")
-        open_window(3, nc.gpsimd, 1, "room3")
-        make_gate(4)
-
-        rows_of = out_0.rearrange("(p t) c -> t p c", t=PACK)
-
-        def offsets_of(h):
-            return list1[:, LIST_COLS * h : LIST_COLS * (h + 1)]
-
-        joined = [held([P, 2, T // 2], F32, "joined%d" % u, over="raw_zt%d" % u) for u in range(2)]
-
-        def place(s, result):
-            t, h = STEPS[s]
-            nc.vector.tensor_copy(windows[t][:].indirect(offsets_of(h)), result[:])
-            if h == 1 and t < 2:
-                for u in range(2):
-                    nc.sync.dma_start(joined[u][:, t, :], windows[t][:, T // 2 * u : T // 2 * (u + 1)])
-            if h == 1:
-                nc.sync.dma_start(rows_of[t], windows[t][:])
-
-        reserve("room_result5", 2 * KIB)
-        reserve("room_result6", 2 * KIB)
-        result_rooms = {5: ("room_result5", 0), 6: ("room_result6", 0)}
-        last_blocks = (("", 0), ("room_result6", 0), ("room_result5", 0), ("", 0))
-
-        def result_of(s):
-            over, shift = result_rooms.get(s, ("gate%d" % s, 0))
-            return held([P, HALF], F32, "result%d" % s, over=over, shift=shift)
-
-        def finish_on_gpsimd(s, gated):
-            nc.gpsimd.tensor_tensor(gated, gated, ats[s], ALU.add)
-            result = result_of(s)
-            nc.gpsimd.tensor_tensor(result[:], gated, weight[:, items_of(STEPS[s][1])], ALU.mult)
-            place(s, result)
-
-        def finish_by_transposes(s, gated):
-            h = STEPS[s][1]
-            summed = psum.tile([P, BLOCKS, P], F32, name="summed%d" % s, tag="bank%d" % s)
+        def sum_by_transposes(w, product_rows, numbers):
+            summed = block_banks("summed%d" % w, numbers)
             for c in range(BLOCKS):
                 cols = slice(P * c, P * (c + 1))
-                nc.tensor.matmul(summed[:, c, :], lhsT=ats[s][:, cols], rhs=ident[:], is_transpose=True, start=True, stop=False)
-                nc.tensor.matmul(summed[:, c, :], lhsT=gated[:, cols], rhs=ident[:], is_transpose=True, start=False, stop=True)
-            weighted = [held([P, P], F32, "weighted%d_%d" % (s, c), over=last_blocks[c][0] if s == 4 else "", shift=last_blocks[c][1]) for c in range(BLOCKS)]
+                nc.tensor.matmul(summed[c][:, c, :], lhsT=ats[w, 1][:, cols], rhs=ident[:], is_transpose=True, start=True, stop=False)
+                nc.tensor.matmul(summed[c][:, c, :], lhsT=product_rows[:, cols], rhs=ident[:], is_transpose=True, start=False, stop=True)
+            return summed
+
+        def finish_by_transposes(summed, w, result, numbers):
+            weighted = held([P, BLOCKS, P], F32, "weighted%d" % w)
             for c in range(BLOCKS):
-                col = BLOCKS * h + c
-                nc.scalar.activation(weighted[c][:], summed[:, c, :], ACT.Copy, scale=weight_cols[:, col : col + 1])
-            turned = psum.tile([P, BLOCKS, P], F32, name="turned%d" % s, tag="bank%d" % (s - 1))
+                nc.scalar.activation(weighted[:, c, :], summed[c][:, c, :], ACT.Copy, scale=weight_cols[:, c : c + 1])
+            upright = block_banks("upright%d" % w, numbers)
             for c in range(BLOCKS):
-                nc.tensor.transpose(turned[:, c, :], weighted[c][:], ident[:])
-            result = result_of(s)
-            nc.scalar.copy(result[:], turned[:].rearrange("p c j -> p (c j)"))
-            place(s, result)
+                nc.tensor.transpose(upright[c][:, c, :], weighted[:, c, :], ident[:])
+            count = BLOCKS // len(set(numbers))
+            for c in range(0, BLOCKS, count):
+                nc.scalar.copy(result[:, P * c : P * (c + count)], upright[c][:, c : c + count, :].rearrange("p c j -> p (c j)"))
 
-        reserve("room_first", 12 * KIB)
-        first = held([P, HALF], F32, "first", over="room_first")
-        second = held([P, HALF], F32, "second")
-        nc.vector.tensor_tensor(first[:], diffs[0], gates[0][:], ALU.mult)
-        nc.vector.tensor_tensor(second[:], diffs[1], gates[1][:], ALU.mult)
-        nc.vector.tensor_tensor(first[:], first[:], ats[0], ALU.add)
-        result = result_of(0)
-        nc.vector.tensor_tensor(result[:], first[:], weight[:, items_of(0)], ALU.mult)
-        for s in range(6, 8):
-            make_diff(s, late_diffs[:, s - 4, :])
-        place(0, result)
-        finish_by_transposes(1, second)
-        for s in range(5, 8):
-            make_gate(s)
-        gated = held([P, 6, HALF], F32, "gated", over="room_first")
-        for s in range(2, 5):
-            nc.gpsimd.tensor_tensor(gated[:, s - 2, :], diffs[s], gates[s][:], ALU.mult)
-            finish_by_transposes(s, gated[:, s - 2, :])
-        for s in range(5, 8):
-            nc.gpsimd.tensor_tensor(gated[:, s - 2, :], diffs[s], gates[s][:], ALU.mult)
-            finish_on_gpsimd(s, gated[:, s - 2, :])
+        def open_blend(w):
+            nc.gpsimd.tensor_tensor(gated[:], values[w][:], gates[w][:], ALU.mult)
 
-        woven = [held([P, c.stop - c.start, PACK], BF16, "woven%d" % i, over="raw_wv", shift=8 * c.start) for i, c in enumerate(PIECES)]
+        def close_blend(w, result):
+            finish(nc.gpsimd, gated[:, items_of(0)], result[:, items_of(0)], w, 0)
 
-        def woven_cols(c, first, last):
-            piece = max(k for k, whole in enumerate(PIECES) if whole.start <= c.start)
-            start = c.start - PIECES[piece].start
-            return woven[piece][:, start : start + c.stop - c.start, first:last]
+        woven = {}
+        out_scales = held([P, SLABS, HALF], U8, "out_scales")
 
-        for c in PIECES:
-            u, start = divmod(c.start, T // 2)
-            nc.scalar.copy(woven_cols(c, 0, 2), joined[u][:, :, start : start + c.stop - c.start].rearrange("p e c -> p c e"))
-        for i, c in enumerate(SHARES):
-            copy = nc.vector.tensor_copy if i < VECTOR_SHARES else nc.scalar.copy
-            pair23 = held([P, 2, c.stop - c.start], BF16, "pair23_%d" % i, over="gated" if i < VECTOR_SHARES else "joined1", shift=4 * c.start)
-            if i < VECTOR_SHARES:
-                nc.gpsimd.tensor_scalar(pair23[:, 0, :], windows[2][:, c], 1.0, -0.0, ALU.mult, ALU.add)
-            else:
-                nc.scalar.copy(pair23[:, 0, :], windows[2][:, c])
-            copy(pair23[:, 1, :], windows[3][:, c])
-            copy(woven_cols(c, 2, 4), pair23[:].rearrange("p e c -> p c e"))
+        def scatter(w, h, result):
+            nc.vector.tensor_copy(windows[w % 3][:].indirect(offsets_of(list1, h)), result)
 
-        out_scales = held([P, T], U8, "out_scales")
-        for i, c in enumerate(PIECES):
-            out_codes = held([P, c.stop - c.start], U32, "out_codes%d" % i, over="v_words", shift=4 * c.start)
-            nc.vector.quantize_mx(out=out_codes[:].bitcast(FP8X4), scales=out_scales[:, c], in_=woven[i][:].rearrange("p c t -> p (c t)"))
-            nc.sync.dma_start(words_view(out_1)[:, c], out_codes[:].bitcast(I32))
-        for q in range(4):
-            nc.scalar.dma_start(out_2[0, 4 * q : 4 * q + 4, :].bitcast(I32), scale_rows(out_scales, q, 0, 4))
+        def store(w):
+            nc.sync.dma_start(out_0[P * w : P * (w + 1), :], windows[w % 3][:])
+
+        def regroup_by_transposes(w, other_copy, turn_banks, back_banks):
+            window = windows[w % 3]
+            woven[w] = held([P, HALF, PACK], BF16, "woven%d" % w)
+            woven_words = woven[w][:].rearrange("p c i -> p (c i)").bitcast(F32).rearrange("p (g c u) -> p g c u", g=GROUPS, u=2)
+            pairs = []
+            for g in range(GROUPS):
+                turned = bank([P, 4, P], "turned%d_%d" % (w, g), turn_banks[g])
+                for chunk in range(4):
+                    first = HALF * chunk + P * g
+                    nc.tensor.transpose(turned[:, chunk, :], window[:, first : first + P], ident[:])
+                pair = held([P, 2, P, 2], BF16, "pair%d_%d" % (w, g))
+                nc.scalar.copy(pair[:], turned[:].rearrange("p c (q u e) -> p u (c q) e", u=2, e=2))
+                pairs.append(pair)
+            for number, groups in back_banks:
+                back = bank([P, len(groups), 2, P], "back%d_%d" % (w, groups[0]), number)
+                for i, g in enumerate(groups):
+                    words = pairs[g][:].rearrange("p u m e -> p (u m e)").bitcast(F32)
+                    for u in range(2):
+                        nc.tensor.transpose(back[:, i, u, :], words[:, P * u : P * (u + 1)], ident[:])
+                other_copy(woven_words[:, groups.start : groups.stop : groups.step], back[:].rearrange("p g u c -> p g c u"))
+
+        def hand_on(name, slabs, over, other_queue):
+            out_codes = held([P, len(slabs), HALF], U32, name, over=over)
+            for i, w in enumerate(slabs):
+                nc.vector.quantize_mx(
+                    out=out_codes[:, i, :].bitcast(FP8X4), scales=out_scales[:, w, :],
+                    in_=woven[w][:].rearrange("p c i -> p (c i)"),
+                )
+            rows = words_view(out_1).rearrange("(w q) t -> q w t", q=QUADRANT)
+            for chunk in (0, 2, 1, 3):
+                (nc.sync if chunk < 2 else other_queue).dma_start(
+                    rows[:, slabs[0] : slabs[-1] + 1, HALF * chunk : HALF * (chunk + 1)],
+                    out_codes[QUADRANT * chunk : QUADRANT * (chunk + 1)].bitcast(I32),
+                )
+
+        both = held([P, J], U32, "picked2_both", over="room_window1")
+        nc.vector.tensor_copy(both[:], v2_words[:].indirect(list2[:]))
+        parted = held([P, 2, 2 * J], U8, "picked2_words")
+        nc.vector.tensor_copy(parted[:].bitcast(U16), both[:].bitcast(U16).rearrange("p (j d) -> p d j", d=2))
+        open_window(1)
+        picked_words = held([P, J], U32, "picked_words")
+        nc.vector.tensor_copy(picked_words[:], v_words[:].indirect(list1[:]))
+
+        first_zt = rounded("first_zt", 2, over="room_scales")
+        first_zv = rounded("first_zv", 1)
+        first_wv = rounded("first_wv", 1)
+        second = rounded("second", MATS)
+        for m in (ZT0, ZT1):
+            round_weight(nc.scalar.copy, first_zt, m, 0, m)
+            round_weight(nc.scalar.copy, second, m, 1, m)
+        quantise(first_zt, 0, ZT0, 2)
+        open_window(2)
+        picked_scales = held([P, J], U8, "picked_scales", over="room_scales")
+        nc.vector.tensor_copy(picked_scales[:], v_scales[:].indirect(list1[:]))
+        round_weight(nc.scalar.copy, first_zv, 0, 0, ZV)
+        round_weight(nc.scalar.copy, second, ZV, 1, ZV)
+        quantise(first_zv, 0, ZV, 1)
+        make_at(0, 0)
+        ht_second = make_ht(0, 1)
+        make_gate(0, 0)
+        round_weight(nc.vector.tensor_copy, first_wv, 0, 0, WV)
+        quantise(first_wv, 0, WV, 1)
+        round_weight(nc.vector.tensor_copy, second, WV, 1, WV)
+        quantise(second, 1, 0, MATS)
+        make_diff(0, 0)
+        nc.scalar.activation(ats[0, 1], ht_second[:], ACT.Relu)
+        make_diff(0, 1)
+        make_gate(0, 1)
+        nc.vector.tensor_tensor(gated[:, items_of(0)], value_of(0, 0), gates[0][:, items_of(0)], ALU.mult)
+        finish(nc.vector, gated[:, items_of(0)], value_of(0, 0), 0, 0)
+        nc.gpsimd.tensor_tensor(gated[:, items_of(0)], value_of(0, 1), gates[0][:, items_of(1)], ALU.mult)
+        finish(nc.gpsimd, gated[:, items_of(0)], value_of(0, 1), 0, 1)
+        for h in (1, 0):
+            make_at(1, h)
+        for h in (1, 0):
+            make_diff(1, h)
+        for h in (1, 0):
+            make_gate(1, h)
+        third = rounded("third", MATS)
+        fourth = rounded("fourth", MATS)
+        for m in (WV, ZV, ZT0, ZT1):
+            round_weight(nc.scalar.copy, third, m, 2, m)
+            round_weight(nc.scalar.copy, fourth, m, 3, m)
+        open_blend(1)
+        nc.gpsimd.tensor_tensor(gated[:, items_of(0)], gated[:, items_of(0)], ats[1, 0], ALU.add)
+        for h in range(2):
+            scatter(0, h, value_of(0, h))
+        store(0)
+        for w in (2, 3):
+            for h in (1, 0):
+                make_at(w, h)
+        late_codes = held([P, 2, MATS * P], U32, "late_codes", over="values0")
+        codes[2], codes[3] = late_codes[:, 0, :], late_codes[:, 1, :]
+        quantise(third, 2, 0, MATS)
+        quantise(fourth, 3, 0, MATS)
+        held_back = [held([P, HALF], F32, "held_back%d" % h, over="fourth", shift=4 * HALF * h) for h in range(2)]
+        nc.gpsimd.tensor_tensor(held_back[0][:], gated[:, items_of(0)], weight[:, items_of(0)], ALU.mult)
+        nc.gpsimd.tensor_tensor(held_back[1][:], gated[:, items_of(1)], ats[1, 1], ALU.add)
+        nc.gpsimd.tensor_tensor(value_of(1, 1), held_back[1][:], weight[:, items_of(1)], ALU.mult)
+        results = {(w, h): value_of(w, h) for w in range(SLABS) for h in range(2)}
+        results[1, 0] = held_back[0][:]
+        for w in (2, 3):
+            for h in (1, 0):
+                make_diff(w, h)
+        for w in (2, 3):
+            for h in (1, 0):
+                make_gate(w, h)
+        for w in (2, 3):
+            open_blend(w)
+            close_blend(w, values[w])
+            summed = sum_by_transposes(w, gated[:, items_of(1)], (6, 6, 6, 6))
+            finish_by_transposes(summed, w, value_of(w, 1), (7, 7, 7, 7))
+        for w in range(1, SLABS):
+            for h in range(2):
+                scatter(w, h, results[w, h])
+            store(w)
+            if w == 1:
+                for early in range(2):
+                    regroup_by_transposes(early, nc.scalar.copy, (1, 3, 1, 3), [(0, range(0, 2)), (2, range(2, 4))])
+            if w == 2:
+                regroup_by_transposes(w, nc.scalar.copy, (7, 3, 0, 2), [(3, range(1, 3)), (7, range(0, 4, 3))])
+        hand_on("early_codes", [0, 1, 2], "values2", nc.gpsimd)
+        regroup_by_transposes(SLABS - 1, nc.vector.tensor_copy, (2, 3, 7, 2), [(number, range(g, g + 1)) for g, number in enumerate((1, 4, 5, 6))])
+        hand_on("last_codes", [3], "", nc.scalar)
+        for chunk in range(4):
+            (nc.sync if chunk < 2 else nc.scalar).dma_start(
+                out_2[0].rearrange("(w r) t -> r w t", r=4)[:, :, HALF * chunk : HALF * (chunk + 1)].bitcast(I32),
+                out_scales[QUADRANT * chunk : QUADRANT * chunk + 4].bitcast(I32),
+            )

@@ -68,7 +68,8 @@ def tile_list_gmu_relu_scatP_kernel(
         v_words = held([P, T], U32, "v_words")
         v2_words = held([P, T], U32, "v2_words")
         v_scales = held([P, T], U8, "v_scales")
-        v2_scales = held([P, T], U8, "v2_scales")
+        reserve("room_window0", 4 * T)
+        v2_scales = held([P, T], U8, "v2_scales", over="room_window0")
         wt_codes = [held([P, 2, 2 * P], I32, "wt_codes%d" % u) for u in range(2)]
         wt_planes = held([P, 2 * N], U8, "wt_planes")
         planes2 = [held([P, J], U8, "planes2_%d" % a) for a in range(2)]
@@ -76,7 +77,7 @@ def tile_list_gmu_relu_scatP_kernel(
         bias = held([P, SLABS], F32, "bias")
         weight = held([P, J], F32, "weight")
         weight_cols = held([P, BLOCKS], F32, "weight_cols")
-        windows = [held([P, T], F32, "window0")]
+        windows = [held([P, T], F32, "window0", over="room_window0")]
         ident = held([P, P], F32, "ident")
 
         def words_view(words):
@@ -89,11 +90,8 @@ def tile_list_gmu_relu_scatP_kernel(
             nc.gpsimd.memset(plane[:].bitcast(I32), 0)
         for q in range(4):
             nc.vector.memset(v2_scales[QUADRANT * q : QUADRANT * q + LOADED_ROW, :].bitcast(I32), 0)
-        for q in range(4):
-            nc.gpsimd.dma_start(scale_rows(v_scales, q, 0, 4), tab_scales[0, 4 * q : 4 * q + 4, :].bitcast(I32))
         for plane in planes2:
             nc.gpsimd.memset(plane[:].bitcast(I32), 0)
-        nc.gpsimd.memset(windows[0][:], 0.0)
         make_identity(nc, ident[:])
 
         sources = [zt[0:512, :], zt[512:1024, :], zv, wv]
@@ -105,6 +103,12 @@ def tile_list_gmu_relu_scatP_kernel(
         def load_wt(u):
             nc.sync.dma_start(wt_codes[u][:], wt_words.rearrange("a p n i -> p a (n i)").bitcast(I32)[:, :, 2 * P * u : 2 * P * (u + 1)])
 
+        def load_wt_scales(q):
+            nc.scalar.dma_start(
+                scale_rows(wt_planes, q, 0, 4).rearrange("r (a n) -> r a n", a=2),
+                wt_scales[:, 4 * q : 4 * q + 4, :].bitcast(I32).rearrange("a r n -> r a n"),
+            )
+
         nc.sync.dma_start(list2[:], offs2)
         for q in range(4):
             nc.sync.dma_start(scale_rows(v2_scales, q, LOADED_ROW, 8), tab2_scales[:, 4 * q : 4 * q + 4, :].bitcast(I32))
@@ -112,13 +116,14 @@ def tile_list_gmu_relu_scatP_kernel(
         nc.sync.dma_start(list1[:], offs)
         nc.sync.dma_start(v_words[:].bitcast(I32), words_view(tab_words))
         for q in range(4):
-            nc.sync.dma_start(
-                scale_rows(wt_planes, q, 0, 4).rearrange("r (a n) -> r a n", a=2),
-                wt_scales[:, 4 * q : 4 * q + 4, :].bitcast(I32).rearrange("a r n -> r a n"),
-            )
-        load_weights(0, [ZT0, ZT1])
+            nc.sync.dma_start(scale_rows(v_scales, q, 0, 4), tab_scales[0, 4 * q : 4 * q + 4, :].bitcast(I32))
+        load_weights(0, [ZT0])
+        for q in range(4):
+            load_wt_scales(q)
+        load_weights(0, [ZT1])
         picked2_scales = held([P, J], U8, "picked2_scales")
         nc.vector.tensor_copy(picked2_scales[:], v2_scales[:].indirect(list2[:]))
+        nc.gpsimd.memset(windows[0][:], 0.0)
         for a in range(2):
             first_row = LOADED_ROW + 4 * a
             nc.sync.dma_start(planes2[a][0:MOVED_ROWS, :].bitcast(I32), picked2_scales[first_row : first_row + MOVED_ROWS, :].bitcast(I32))
@@ -324,7 +329,8 @@ def tile_list_gmu_relu_scatP_kernel(
         make_diff(0, 1)
         make_gate(0, 1)
         nc.vector.tensor_tensor(gated[:, items_of(0)], value_of(0, 0), gates[0][:, items_of(0)], ALU.mult)
-        finish(nc.vector, gated[:, items_of(0)], value_of(0, 0), 0, 0)
+        first_result = held([P, HALF], F32, "first_result", over="second")
+        finish(nc.vector, gated[:, items_of(0)], first_result[:], 0, 0)
         nc.gpsimd.tensor_tensor(gated[:, items_of(0)], value_of(0, 1), gates[0][:, items_of(1)], ALU.mult)
         finish(nc.gpsimd, gated[:, items_of(0)], value_of(0, 1), 0, 1)
         for h in (1, 0):
@@ -340,8 +346,8 @@ def tile_list_gmu_relu_scatP_kernel(
             round_weight(nc.scalar.copy, fourth, m, 3, m)
         open_blend(1)
         nc.gpsimd.tensor_tensor(gated[:, items_of(0)], gated[:, items_of(0)], ats[1, 0], ALU.add)
-        for h in range(2):
-            scatter(0, h, value_of(0, h))
+        scatter(0, 0, first_result[:])
+        scatter(0, 1, value_of(0, 1))
         store(0)
         for w in (2, 3):
             for h in (1, 0):

@@ -78,7 +78,6 @@ def tile_list_gmu_relu_scatP_kernel(
         weight = held([P, J], F32, "weight")
         weight_cols = held([P, BLOCKS], F32, "weight_cols")
         windows = [held([P, T], F32, "window0", over="room_window0")]
-        ident = held([P, P], F32, "ident")
 
         def words_view(words):
             return words[0].rearrange("p t i -> p (t i)").bitcast(I32)
@@ -86,13 +85,11 @@ def tile_list_gmu_relu_scatP_kernel(
         def scale_rows(tile, q, first, count):
             return tile[QUADRANT * q + first : QUADRANT * q + first + count, :].bitcast(I32)
 
-        for plane in (v_scales, wt_planes):
-            nc.gpsimd.memset(plane[:].bitcast(I32), 0)
+        nc.vector.memset(wt_planes[:].bitcast(I32), 0)
         for q in range(4):
-            nc.vector.memset(v2_scales[QUADRANT * q : QUADRANT * q + LOADED_ROW, :].bitcast(I32), 0)
-        for plane in planes2:
-            nc.gpsimd.memset(plane[:].bitcast(I32), 0)
-        make_identity(nc, ident[:])
+            (nc.vector if q else nc.gpsimd).memset(v2_scales[QUADRANT * q : QUADRANT * q + LOADED_ROW, :].bitcast(I32), 0)
+        for plane in planes2 + [v_scales]:
+            nc.vector.memset(plane[:].bitcast(I32), 0)
 
         sources = [zt[0:512, :], zt[512:1024, :], zv, wv]
 
@@ -104,7 +101,7 @@ def tile_list_gmu_relu_scatP_kernel(
             nc.sync.dma_start(wt_codes[u][:], wt_words.rearrange("a p n i -> p a (n i)").bitcast(I32)[:, :, 2 * P * u : 2 * P * (u + 1)])
 
         def load_wt_scales(q):
-            nc.scalar.dma_start(
+            nc.sync.dma_start(
                 scale_rows(wt_planes, q, 0, 4).rearrange("r (a n) -> r a n", a=2),
                 wt_scales[:, 4 * q : 4 * q + 4, :].bitcast(I32).rearrange("a r n -> r a n"),
             )
@@ -115,19 +112,19 @@ def tile_list_gmu_relu_scatP_kernel(
         nc.sync.dma_start(v2_words[:].bitcast(I32), words_view(tab2_words))
         nc.sync.dma_start(list1[:], offs)
         nc.sync.dma_start(v_words[:].bitcast(I32), words_view(tab_words))
-        for q in range(4):
-            nc.sync.dma_start(scale_rows(v_scales, q, 0, 4), tab_scales[0, 4 * q : 4 * q + 4, :].bitcast(I32))
-        load_weights(0, [ZT0])
-        for q in range(4):
+        load_weights(0, [ZT0, ZT1])
+        for q in range(3):
             load_wt_scales(q)
-        load_weights(0, [ZT1])
         picked2_scales = held([P, J], U8, "picked2_scales")
         nc.vector.tensor_copy(picked2_scales[:], v2_scales[:].indirect(list2[:]))
         nc.gpsimd.memset(windows[0][:], 0.0)
         for a in range(2):
             first_row = LOADED_ROW + 4 * a
             nc.sync.dma_start(planes2[a][0:MOVED_ROWS, :].bitcast(I32), picked2_scales[first_row : first_row + MOVED_ROWS, :].bitcast(I32))
+        load_wt_scales(3)
         load_weights(0, [ZV])
+        for q in range(4):
+            nc.sync.dma_start(scale_rows(v_scales, q, 0, 4), tab_scales[0, 4 * q : 4 * q + 4, :].bitcast(I32))
         load_wt(0)
         load_weights(0, [WV])
         with nc.allow_non_contiguous_dma(reason="one value a partition and column"):
@@ -281,13 +278,15 @@ def tile_list_gmu_relu_scatP_kernel(
                         nc.tensor.transpose(back[:, i, u, :], words[:, P * u : P * (u + 1)], ident[:])
                 other_copy(woven_words[:, groups.start : groups.stop : groups.step], back[:].rearrange("p g u c -> p g c u"))
 
-        def hand_on(name, slabs, over, other_queue):
+        def hand_on(name, slabs, over, other_queue, parts=1):
             out_codes = held([P, len(slabs), HALF], U32, name, over=over)
             for i, w in enumerate(slabs):
-                nc.vector.quantize_mx(
-                    out=out_codes[:, i, :].bitcast(FP8X4), scales=out_scales[:, w, :],
-                    in_=woven[w][:].rearrange("p c i -> p (c i)"),
-                )
+                for part in range(parts):
+                    cols = slice(HALF // parts * part, HALF // parts * (part + 1))
+                    nc.vector.quantize_mx(
+                        out=out_codes[:, i, cols].bitcast(FP8X4), scales=out_scales[:, w, cols],
+                        in_=woven[w][:, cols, :].rearrange("p c i -> p (c i)"),
+                    )
             rows = words_view(out_1).rearrange("(w q) t -> q w t", q=QUADRANT)
             for chunk in (0, 2, 1, 3):
                 (nc.sync if chunk < 2 else other_queue).dma_start(
@@ -324,6 +323,8 @@ def tile_list_gmu_relu_scatP_kernel(
         quantise(first_wv, 0, WV, 1)
         round_weight(nc.vector.tensor_copy, second, WV, 1, WV)
         quantise(second, 1, 0, MATS)
+        ident = held([P, P], F32, "ident", over="second", shift=4 * HALF)
+        make_identity(nc, ident[:])
         make_diff(0, 0)
         nc.scalar.activation(ats[0, 1], ht_second[:], ACT.Relu)
         make_diff(0, 1)
@@ -382,9 +383,9 @@ def tile_list_gmu_relu_scatP_kernel(
                     regroup_by_transposes(early, nc.scalar.copy, (1, 3, 1, 3), [(0, range(0, 2)), (2, range(2, 4))])
             if w == 2:
                 regroup_by_transposes(w, nc.scalar.copy, (7, 3, 0, 2), [(3, range(1, 3)), (7, range(0, 4, 3))])
-        hand_on("early_codes", [0, 1, 2], "values2", nc.gpsimd)
+        hand_on("early_codes", [0, 1, 2], "values2", nc.scalar)
         regroup_by_transposes(SLABS - 1, nc.vector.tensor_copy, (2, 3, 7, 2), [(number, range(g, g + 1)) for g, number in enumerate((1, 4, 5, 6))])
-        hand_on("last_codes", [3], "", nc.scalar)
+        hand_on("last_codes", [3], "", nc.scalar, parts=2)
         for chunk in range(4):
             (nc.sync if chunk < 2 else nc.scalar).dma_start(
                 out_2[0].rearrange("(w r) t -> r w t", r=4)[:, :, HALF * chunk : HALF * (chunk + 1)].bitcast(I32),

@@ -192,8 +192,8 @@ def tile_list_gmu_relu_scatP_kernel(
                 )
             return acc
 
-        both_ats = [held([P, J], F32, "ats%d" % w) for w in range(SLABS)]
-        ats = {(w, h): both_ats[w][:, items_of(h)] for w in range(SLABS) for h in range(2)}
+        reserve("room_fourth", 4 * J)
+        ats = {(w, h): held([P, HALF], F32, "at%d_%d" % (w, h))[:] for w in (1, 0, 2, 3) for h in range(2)}
         gates = [held([P, J], F32, "gates%d" % w) for w in range(SLABS)]
         gated = held([P, J], F32, "gated")
         values = [held([P, J], F32, "values%d" % r) for r in range(SLABS)]
@@ -268,7 +268,7 @@ def tile_list_gmu_relu_scatP_kernel(
                     first = HALF * chunk + P * g
                     nc.tensor.transpose(turned[:, chunk, :], window[:, first : first + P], ident[:])
                 pair = held([P, 2, P, 2], BF16, "pair%d_%d" % (w, g))
-                nc.scalar.copy(pair[:], turned[:].rearrange("p c (q u e) -> p u (c q) e", u=2, e=2))
+                (other_copy if g == 2 else nc.scalar.copy)(pair[:], turned[:].rearrange("p c (q u e) -> p u (c q) e", u=2, e=2))
                 pairs.append(pair)
             for number, groups in back_banks:
                 back = bank([P, len(groups), 2, P], "back%d_%d" % (w, groups[0]), number)
@@ -303,8 +303,7 @@ def tile_list_gmu_relu_scatP_kernel(
         nc.vector.tensor_copy(picked_words[:], v_words[:].indirect(list1[:]))
 
         first_zt = rounded("first_zt", 2, over="room_scales")
-        first_zv = rounded("first_zv", 1)
-        first_wv = rounded("first_wv", 1)
+        first_v = rounded("first_v", 2)
         second = rounded("second", MATS)
         for m in (ZT0, ZT1):
             round_weight(nc.scalar.copy, first_zt, m, 0, m)
@@ -313,14 +312,13 @@ def tile_list_gmu_relu_scatP_kernel(
         open_window(2)
         picked_scales = held([P, J], U8, "picked_scales", over="room_scales")
         nc.vector.tensor_copy(picked_scales[:], v_scales[:].indirect(list1[:]))
-        round_weight(nc.scalar.copy, first_zv, 0, 0, ZV)
+        round_weight(nc.scalar.copy, first_v, 0, 0, ZV)
         round_weight(nc.scalar.copy, second, ZV, 1, ZV)
-        quantise(first_zv, 0, ZV, 1)
         make_at(0, 0)
         ht_second = make_ht(0, 1)
+        round_weight(nc.vector.tensor_copy, first_v, 1, 0, WV)
+        quantise(first_v, 0, ZV, 2)
         make_gate(0, 0)
-        round_weight(nc.vector.tensor_copy, first_wv, 0, 0, WV)
-        quantise(first_wv, 0, WV, 1)
         round_weight(nc.vector.tensor_copy, second, WV, 1, WV)
         quantise(second, 1, 0, MATS)
         ident = held([P, P], F32, "ident", over="second", shift=4 * HALF)
@@ -341,7 +339,7 @@ def tile_list_gmu_relu_scatP_kernel(
         for h in (1, 0):
             make_gate(1, h)
         third = rounded("third", MATS)
-        fourth = rounded("fourth", MATS)
+        fourth = rounded("fourth", MATS, over="room_fourth")
         for m in (WV, ZV, ZT0, ZT1):
             round_weight(nc.scalar.copy, third, m, 2, m)
             round_weight(nc.scalar.copy, fourth, m, 3, m)
@@ -357,7 +355,7 @@ def tile_list_gmu_relu_scatP_kernel(
         codes[2], codes[3] = late_codes[:, 0, :], late_codes[:, 1, :]
         quantise(third, 2, 0, MATS)
         quantise(fourth, 3, 0, MATS)
-        held_back = [held([P, HALF], F32, "held_back%d" % h, over="fourth", shift=4 * HALF * h) for h in range(2)]
+        held_back = [held([P, HALF], F32, "held_back%d" % h, over="fourth", shift=6 * HALF * h) for h in range(2)]
         nc.gpsimd.tensor_tensor(held_back[0][:], gated[:, items_of(0)], weight[:, items_of(0)], ALU.mult)
         nc.gpsimd.tensor_tensor(held_back[1][:], gated[:, items_of(1)], ats[1, 1], ALU.add)
         nc.gpsimd.tensor_tensor(value_of(1, 1), held_back[1][:], weight[:, items_of(1)], ALU.mult)
@@ -370,13 +368,20 @@ def tile_list_gmu_relu_scatP_kernel(
             for h in (1, 0):
                 make_gate(w, h)
         for w in (2, 3):
-            open_blend(w)
+            if w == 2:
+                open_blend(w)
+            else:
+                for h in (1, 0):
+                    nc.gpsimd.tensor_tensor(gated[:, items_of(h)], value_of(w, h), gates[w][:, items_of(h)], ALU.mult)
             close_blend(w, values[w])
             summed = sum_by_transposes(w, gated[:, items_of(1)], (6, 6, 6, 6))
             finish_by_transposes(summed, w, value_of(w, 1), (7, 7, 7, 7))
         for w in range(1, SLABS):
-            for h in range(2):
-                scatter(w, h, results[w, h])
+            if w == SLABS - 1:
+                nc.vector.tensor_copy(windows[0][:].indirect(list1[:]), values[w][:])
+            else:
+                for h in range(2):
+                    scatter(w, h, results[w, h])
             store(w)
             if w == 1:
                 for early in range(2):

@@ -29,7 +29,7 @@ MATS = 4
 GROUPS = 4
 BLOCKS = HALF // P
 ZT0, ZT1, ZV, WV = range(MATS)
-HT_BANKS = ((0, 1), (2, 0), (1, 3), (2, 0))
+HT_BANKS = ((0, 1), (2, 0), (2, 0), (2, 0))
 HV_BANKS = ((0, 3), (2, 0), (1, 3), (4, 5))
 Z_BANKS = ((2, 1), (4, 5), (2, 0), (1, 3))
 
@@ -70,7 +70,8 @@ def tile_list_gmu_relu_scatP_kernel(
         v_scales = held([P, T], U8, "v_scales")
         reserve("room_window0", 4 * T)
         v2_scales = held([P, T], U8, "v2_scales", over="room_window0")
-        wt_codes = [held([P, 2, 2 * P], I32, "wt_codes%d" % u) for u in range(2)]
+        values = [held([P, J], F32, "values0")]
+        wt_codes = {u: held([P, 2, 2 * P], I32, "wt_codes%d" % u) for u in (1, 0)}
         wt_planes = held([P, 2 * N], U8, "wt_planes")
         planes2 = [held([P, J], U8, "planes2_%d" % a) for a in range(2)]
         raw = [held([P, MATS, PACK, 2 * P], F32, "raw%d" % u) for u in range(2)]
@@ -85,10 +86,10 @@ def tile_list_gmu_relu_scatP_kernel(
         def scale_rows(tile, q, first, count):
             return tile[QUADRANT * q + first : QUADRANT * q + first + count, :].bitcast(I32)
 
-        nc.vector.memset(wt_planes[:].bitcast(I32), 0)
+        nc.vector.memset(v_scales[:].bitcast(I32), 0)
         for q in range(4):
             (nc.vector if q else nc.gpsimd).memset(v2_scales[QUADRANT * q : QUADRANT * q + LOADED_ROW, :].bitcast(I32), 0)
-        for plane in planes2 + [v_scales]:
+        for plane in planes2 + [wt_planes]:
             nc.vector.memset(plane[:].bitcast(I32), 0)
 
         sources = [zt[0:512, :], zt[512:1024, :], zv, wv]
@@ -99,6 +100,9 @@ def tile_list_gmu_relu_scatP_kernel(
 
         def load_wt(u):
             nc.sync.dma_start(wt_codes[u][:], wt_words.rearrange("a p n i -> p a (n i)").bitcast(I32)[:, :, 2 * P * u : 2 * P * (u + 1)])
+
+        def load_v_scales(q):
+            nc.sync.dma_start(scale_rows(v_scales, q, 0, 4), tab_scales[0, 4 * q : 4 * q + 4, :].bitcast(I32))
 
         def load_wt_scales(q):
             nc.sync.dma_start(
@@ -114,17 +118,17 @@ def tile_list_gmu_relu_scatP_kernel(
         nc.sync.dma_start(v_words[:].bitcast(I32), words_view(tab_words))
         load_weights(0, [ZT0, ZT1])
         for q in range(3):
-            load_wt_scales(q)
+            load_v_scales(q)
         picked2_scales = held([P, J], U8, "picked2_scales")
         nc.vector.tensor_copy(picked2_scales[:], v2_scales[:].indirect(list2[:]))
         nc.gpsimd.memset(windows[0][:], 0.0)
         for a in range(2):
             first_row = LOADED_ROW + 4 * a
             nc.sync.dma_start(planes2[a][0:MOVED_ROWS, :].bitcast(I32), picked2_scales[first_row : first_row + MOVED_ROWS, :].bitcast(I32))
-        load_wt_scales(3)
+        load_v_scales(3)
         load_weights(0, [ZV])
         for q in range(4):
-            nc.sync.dma_start(scale_rows(v_scales, q, 0, 4), tab_scales[0, 4 * q : 4 * q + 4, :].bitcast(I32))
+            load_wt_scales(q)
         load_wt(0)
         load_weights(0, [WV])
         with nc.allow_non_contiguous_dma(reason="one value a partition and column"):
@@ -196,7 +200,7 @@ def tile_list_gmu_relu_scatP_kernel(
         ats = {(w, h): held([P, HALF], F32, "at%d_%d" % (w, h))[:] for w in (1, 0, 2, 3) for h in range(2)}
         gates = [held([P, J], F32, "gates%d" % w) for w in range(SLABS)]
         gated = held([P, J], F32, "gated")
-        values = [held([P, J], F32, "values%d" % r) for r in range(SLABS)]
+        values += [held([P, J], F32, "values%d" % r) for r in range(1, SLABS)]
 
         def value_of(w, h):
             return values[w][:, items_of(h)]
@@ -227,8 +231,8 @@ def tile_list_gmu_relu_scatP_kernel(
             summed = block_banks("summed%d" % w, numbers)
             for c in range(BLOCKS):
                 cols = slice(P * c, P * (c + 1))
-                nc.tensor.matmul(summed[c][:, c, :], lhsT=ats[w, 1][:, cols], rhs=ident[:], is_transpose=True, start=True, stop=False)
-                nc.tensor.matmul(summed[c][:, c, :], lhsT=product_rows[:, cols], rhs=ident[:], is_transpose=True, start=False, stop=True)
+                nc.tensor.matmul(summed[c][:, c, :], lhsT=product_rows[:, cols], rhs=ident[:], is_transpose=True, start=True, stop=False)
+                nc.tensor.matmul(summed[c][:, c, :], lhsT=ats[w, 1][:, cols], rhs=ident[:], is_transpose=True, start=False, stop=True)
             return summed
 
         def finish_by_transposes(summed, w, result, numbers):
@@ -351,7 +355,7 @@ def tile_list_gmu_relu_scatP_kernel(
         for w in (2, 3):
             for h in (1, 0):
                 make_at(w, h)
-        late_codes = held([P, 2, MATS * P], U32, "late_codes", over="values0")
+        late_codes = held([P, 2, MATS * P], U32, "late_codes", over="values0", shift=4 * HALF)
         codes[2], codes[3] = late_codes[:, 0, :], late_codes[:, 1, :]
         quantise(third, 2, 0, MATS)
         quantise(fourth, 3, 0, MATS)

@@ -22,16 +22,18 @@ PACK = 4
 HALF = 512
 QUADRANT = 32
 LIST_COLS = HALF // 16
-LOADED_ROW = QUADRANT - 8
-MOVED_ROWS = 3 * QUADRANT + 4
+LOADED_ROW = 3 * QUADRANT
 SLABS = N // P
 MATS = 4
 GROUPS = 4
 BLOCKS = HALF // P
-ZT0, ZT1, ZV, WV = range(MATS)
-HT_BANKS = ((0, 1), (2, 0), (2, 0), (2, 0))
-HV_BANKS = ((0, 3), (2, 0), (1, 3), (4, 5))
-Z_BANKS = ((2, 1), (4, 5), (2, 0), (1, 3))
+BANK = 2048
+BY_PORT = (0, 2, 1, 3)
+WV, ZV, ZT0, ZT1 = range(MATS)
+HT_BANKS = ((0, 1), (2, 3), (0, 1), (0, 1))
+HV_BANKS = ((4, 5), (4, 5), (4, 5), (0, 1))
+Z_BANKS = ((2, 3), (0, 1), (6, 7), (4, 5))
+REGROUP_BANKS = ((4, 5, 0, 1), (2, 3, 6, 7))
 
 
 def tile_list_gmu_relu_scatP_kernel(
@@ -61,84 +63,13 @@ def tile_list_gmu_relu_scatP_kernel(
             return keep.tile(shape, dtype, name=name, align_bytes=64, offset=places[name])
 
         def bank(shape, name, number):
-            return psum.tile(shape, F32, name=name, tag="bank%d" % number)
-
-        list1 = lists.tile([P, J // 16], U16, name="list1")
-        list2 = lists.tile([P, J // 16], U16, name="list2")
-        v_words = held([P, T], U32, "v_words")
-        v2_words = held([P, T], U32, "v2_words")
-        v_scales = held([P, T], U8, "v_scales")
-        reserve("room_window0", 4 * T)
-        v2_scales = held([P, T], U8, "v2_scales", over="room_window0")
-        values = [held([P, J], F32, "values0")]
-        wt_codes = {u: held([P, 2, 2 * P], I32, "wt_codes%d" % u) for u in (1, 0)}
-        wt_planes = held([P, 2 * N], U8, "wt_planes")
-        planes2 = [held([P, J], U8, "planes2_%d" % a) for a in range(2)]
-        raw = [held([P, MATS, PACK, 2 * P], F32, "raw%d" % u) for u in range(2)]
-        bias = held([P, SLABS], F32, "bias")
-        weight = held([P, J], F32, "weight")
-        weight_cols = held([P, BLOCKS], F32, "weight_cols")
-        windows = [held([P, T], F32, "window0", over="room_window0")]
+            return psum.tile(shape, F32, name=name, offset=BANK * number)
 
         def words_view(words):
             return words[0].rearrange("p t i -> p (t i)").bitcast(I32)
 
-        def scale_rows(tile, q, first, count):
-            return tile[QUADRANT * q + first : QUADRANT * q + first + count, :].bitcast(I32)
-
-        nc.vector.memset(v_scales[:].bitcast(I32), 0)
-        for q in range(4):
-            (nc.vector if q else nc.gpsimd).memset(v2_scales[QUADRANT * q : QUADRANT * q + LOADED_ROW, :].bitcast(I32), 0)
-        for plane in planes2 + [wt_planes]:
-            nc.vector.memset(plane[:].bitcast(I32), 0)
-
-        sources = [zt[0:512, :], zt[512:1024, :], zv, wv]
-
-        def load_weights(u, mats):
-            for m in mats:
-                nc.sync.dma_start(raw[u][:, m], sources[m].rearrange("(p j) n -> p j n", j=PACK)[:, :, 2 * P * u : 2 * P * (u + 1)])
-
-        def load_wt(u):
-            nc.sync.dma_start(wt_codes[u][:], wt_words.rearrange("a p n i -> p a (n i)").bitcast(I32)[:, :, 2 * P * u : 2 * P * (u + 1)])
-
-        def load_v_scales(q):
-            nc.sync.dma_start(scale_rows(v_scales, q, 0, 4), tab_scales[0, 4 * q : 4 * q + 4, :].bitcast(I32))
-
-        def load_wt_scales(q):
-            nc.sync.dma_start(
-                scale_rows(wt_planes, q, 0, 4).rearrange("r (a n) -> r a n", a=2),
-                wt_scales[:, 4 * q : 4 * q + 4, :].bitcast(I32).rearrange("a r n -> r a n"),
-            )
-
-        nc.sync.dma_start(list2[:], offs2)
-        for q in range(4):
-            nc.sync.dma_start(scale_rows(v2_scales, q, LOADED_ROW, 8), tab2_scales[:, 4 * q : 4 * q + 4, :].bitcast(I32))
-        nc.sync.dma_start(v2_words[:].bitcast(I32), words_view(tab2_words))
-        nc.sync.dma_start(list1[:], offs)
-        nc.sync.dma_start(v_words[:].bitcast(I32), words_view(tab_words))
-        load_weights(0, [ZT0, ZT1])
-        for q in range(3):
-            load_v_scales(q)
-        picked2_scales = held([P, J], U8, "picked2_scales")
-        nc.vector.tensor_copy(picked2_scales[:], v2_scales[:].indirect(list2[:]))
-        nc.gpsimd.memset(windows[0][:], 0.0)
-        for a in range(2):
-            first_row = LOADED_ROW + 4 * a
-            nc.sync.dma_start(planes2[a][0:MOVED_ROWS, :].bitcast(I32), picked2_scales[first_row : first_row + MOVED_ROWS, :].bitcast(I32))
-        load_v_scales(3)
-        load_weights(0, [ZV])
-        for q in range(4):
-            load_wt_scales(q)
-        load_wt(0)
-        load_weights(0, [WV])
-        with nc.allow_non_contiguous_dma(reason="one value a partition and column"):
-            nc.sync.dma_start(bias[:], b.rearrange("(w p) -> p w", p=P))
-            nc.sync.dma_start(weight[:, 0:HALF], wgo[:, 0:HALF])
-            load_wt(1)
-            load_weights(1, [WV, ZV])
-            nc.sync.dma_start(weight[:, HALF:J], wgo[:, HALF:J])
-            load_weights(1, [ZT0, ZT1])
-            nc.sync.dma_start(weight_cols[:], wgo[0, HALF:J].rearrange("(c p) -> p c", p=P))
+        def scale_rows(tile, q):
+            return tile[QUADRANT * q : QUADRANT * q + 4, :].bitcast(I32)
 
         def items_of(h):
             return slice(HALF * h, HALF * (h + 1))
@@ -146,114 +77,159 @@ def tile_list_gmu_relu_scatP_kernel(
         def offsets_of(tile, h):
             return tile[:, LIST_COLS * h : LIST_COLS * (h + 1)]
 
+        list1 = lists.tile([P, J // 16], U16, name="list1")
+        list2 = lists.tile([P, J // 16], U16, name="list2")
+        reserve("room_window0", 4 * T)
+        v2_scales = held([P, T], U8, "v2_scales", over="room_window0", shift=4 * T - 64)
+        reserve("room_between", T - 128)
+        loaded = held([P, MATS * PACK * N + J + SLABS], F32, "loaded")
+        v_scales = held([P, T], U8, "v_scales")
+        planes2 = held([P, 2 * J], U8, "planes2")
+        wt_planes = held([P, 2 * N], U8, "wt_planes")
+        v2_words = held([P, T], U32, "v2_words")
+        v_words = held([P, T], U32, "v_words")
         reserve("room_window1", 4 * T)
-        reserve("room_scales", J)
-        reserve("room_window2", 4 * T)
+        both = held([P, J], U32, "picked2_both", over="room_window1", shift=4 * T - 2 * J)
+        wt_codes = {u: held([P, 2, 2 * P], I32, "wt_codes%d" % u) for u in (1, 0)}
+        weight = loaded[:, MATS * PACK * N : MATS * PACK * N + J]
+        bias = loaded[:, MATS * PACK * N + J :]
 
-        def open_window(i):
-            windows.append(held([P, T], F32, "window%d" % i, over="room_window%d" % i))
-            nc.gpsimd.memset(windows[i][:], 0.0)
+        nc.vector.memset(v2_scales[0:LOADED_ROW, :].bitcast(I32), 0)
+        for tile in (wt_planes, v_scales, planes2):
+            nc.vector.memset(tile[:].bitcast(I32), 0)
 
-        codes = {w: held([P, MATS * P], U32, "codes%d" % w) for w in range(2)}
-        scales = [held([P, MATS * P], U8, "scales%d" % w) for w in range(SLABS)]
+        ident = held([P, P], F32, "ident")
+        nc.vector.memset(ident[:], 0.0)
+        make_identity(nc, ident[:], nomemset=True)
 
-        def rounded(name, count, over=""):
-            return held([P, count, P, PACK], BF16, name, over=over)
+        sources = [wv, zv, zt[0:512, :], zt[512:1024, :]]
 
-        def round_weight(copy, grouped, i, w, m):
-            copy(
-                grouped[:, i].rearrange("p (c i) j -> p c j i", i=4),
-                raw[w // 2][:, m, :, P * (w % 2) : P * (w % 2 + 1)].rearrange("p j (c i) -> p c j i", i=4),
+        def raw(m, first, count):
+            start = PACK * (N * m + P * first)
+            return loaded[:, start : start + PACK * P * count].rearrange("p (j n) -> p j n", j=PACK)
+
+        def load_weight(m, first, count):
+            nc.sync.dma_start(raw(m, first, count), sources[m].rearrange("(p j) n -> p j n", j=PACK)[:, :, P * first : P * (first + count)])
+
+        def load_wt(u):
+            nc.sync.dma_start(wt_codes[u][:], wt_words.rearrange("a p n i -> p a (n i)").bitcast(I32)[:, :, 2 * P * u : 2 * P * (u + 1)])
+
+        def load_v_scales(q):
+            nc.sync.dma_start(scale_rows(v_scales, q), tab_scales[0, 4 * q : 4 * q + 4, :].bitcast(I32))
+
+        def load_wt_scales(q):
+            nc.sync.dma_start(
+                scale_rows(wt_planes, q).rearrange("r (a n) -> r a n", a=2),
+                wt_scales[:, 4 * q : 4 * q + 4, :].bitcast(I32).rearrange("a r n -> r a n"),
             )
 
-        def quantise(grouped, w, first, count):
-            cols = slice(P * first, P * (first + count))
-            nc.vector.quantize_mx(
-                out=codes[w][:, cols].bitcast(FP8X4), scales=scales[w][:, cols],
-                in_=grouped[:].rearrange("p a c j -> p (a c j)"),
+        nc.sync.dma_start(list2[:], offs2)
+        nc.sync.dma_start(v2_scales[LOADED_ROW:P, :].bitcast(I32), tab2_scales.bitcast(I32).rearrange("a r t -> r a t"))
+        nc.sync.dma_start(v2_words[:].bitcast(I32), words_view(tab2_words))
+        nc.sync.dma_start(list1[:], offs)
+        nc.sync.dma_start(v_words[:].bitcast(I32), words_view(tab_words))
+        load_wt(0)
+        for q in BY_PORT:
+            load_wt_scales(q)
+        picked2_scales = held([P, J], U8, "picked2_scales")
+        nc.vector.tensor_copy(picked2_scales[:], v2_scales[:].indirect(list2[:]))
+        nc.vector.tensor_copy(both[:], v2_words[:].indirect(list2[:]))
+        parted = held([P, 2, 2 * J], U8, "picked2_words")
+        nc.vector.tensor_copy(parted[:].bitcast(U16), both[:].bitcast(U16).rearrange("p (j d) -> p d j", d=2))
+        load_weight(WV, 0, 2)
+        for q in BY_PORT:
+            nc.sync.dma_start(scale_rows(planes2, q), picked2_scales[LOADED_ROW + 8 * q : LOADED_ROW + 8 * (q + 1), :].bitcast(I32))
+        load_weight(ZV, 0, 1)
+        for q in BY_PORT:
+            load_v_scales(q)
+        load_weight(ZT0, 0, 1)
+        load_weight(ZT1, 0, 1)
+        with nc.allow_non_contiguous_dma(reason="one value a partition and column"):
+            nc.sync.dma_start(bias, b.rearrange("(w p) -> p w", p=P))
+        for m in (ZV, ZT0, ZT1):
+            load_weight(m, 1, 1)
+        load_weight(WV, 2, 2)
+        nc.sync.dma_start(weight, wgo)
+        load_weight(ZV, 2, 2)
+        load_wt(1)
+        for m in (ZT0, ZT1):
+            load_weight(m, 2, 2)
+
+        windows = []
+
+        def open_window(over, shift):
+            windows.append(held([P, T], F32, "window%d" % len(windows), over=over, shift=shift))
+            nc.gpsimd.memset(windows[-1][:], 0.0)
+
+        made = {}
+
+        def round_weight(grouped, m, first, count):
+            nc.scalar.copy(
+                grouped.rearrange("p w (c i) j -> p w c j i", i=4),
+                raw(m, first, count).rearrange("p j (w c i) -> p w c j i", i=4, c=P // 4),
             )
+
+        def round_on_gpsimd(grouped, m, first, count):
+            nc.gpsimd.tensor_scalar(grouped, raw(m, first, count).rearrange("p j c -> p c j"), 1.0, 0.0, ALU.mult, ALU.add)
+
+        def quantise(grouped, parts, codes, over="", shift=0):
+            planes = held([P, len(parts) * P], U8, "planes_%d_%d" % parts[0], over=over, shift=shift)
+            nc.vector.quantize_mx(out=codes.bitcast(FP8X4), scales=planes[:], in_=grouped.rearrange("p a c j -> p (a c j)"))
+            for i, part in enumerate(parts):
+                made[part] = codes[:, P * i : P * (i + 1)].bitcast(FP8X4), planes[:, P * i : P * (i + 1)]
 
         def made_side(w, m):
-            cols = slice(P * m, P * (m + 1))
-            return codes[w][:, cols].bitcast(FP8X4), scales[w][:, cols]
+            return made[w, m]
 
         def wt_side(w, a):
             first = P * (w % 2)
             return wt_codes[w // 2][:, a, first : first + P].bitcast(FP8X4), wt_planes[:, N * a + P * w : N * a + P * (w + 1)]
 
         def v_side(h):
-            return picked_words[:, items_of(h)].bitcast(FP8X4), picked_scales[:, items_of(h)]
+            return picked_words[:, items_of(h)].bitcast(FP8X4), picked_scales[h][:]
 
         def v2_side(h, a):
-            return parted[:, a, 2 * HALF * h : 2 * HALF * (h + 1)].bitcast(FP4X4), planes2[a][:, items_of(h)]
+            return parted[:, a, 2 * HALF * h : 2 * HALF * (h + 1)].bitcast(FP4X4), planes2[:, J * a + HALF * h : J * a + HALF * (h + 1)]
 
-        def product(name, number, passes):
-            acc = bank([P, HALF], name, number)
+        def product(acc, passes):
             for i, (lhs, rhs) in enumerate(passes):
                 nc.tensor.matmul_mx(
-                    out=acc[:], lhsT=lhs[0], lhsT_scale=lhs[1], rhs=rhs[0], rhs_scale=rhs[1],
+                    out=acc, lhsT=lhs[0], lhsT_scale=lhs[1], rhs=rhs[0], rhs_scale=rhs[1],
                     start=(i == 0), stop=(i == len(passes) - 1),
                 )
             return acc
 
-        reserve("room_fourth", 4 * J)
-        ats = {(w, h): held([P, HALF], F32, "at%d_%d" % (w, h))[:] for w in (1, 0, 2, 3) for h in range(2)}
-        gates = [held([P, J], F32, "gates%d" % w) for w in range(SLABS)]
-        gated = held([P, J], F32, "gated")
-        values += [held([P, J], F32, "values%d" % r) for r in range(1, SLABS)]
-
-        def value_of(w, h):
-            return values[w][:, items_of(h)]
+        ats = {w: held([P, J], F32, "ats%d" % w) for w in (0, 3)}
+        at_of = {(w, h): ats[w][:, items_of(h)] for w in (0, 3) for h in range(2)}
+        for w in (1, 2):
+            for h in range(2):
+                at_of[w, h] = held([P, HALF], F32, "at%d_%d" % (w, h))[:]
+        gate_of = {}
+        for h in range(2):
+            reserve("room_gate%d" % h, 8 * HALF)
+            gate_of[0, h] = held([P, HALF], F32, "gate0_%d" % h, over="room_gate%d" % h)[:]
+        for w in range(1, SLABS):
+            slab_gates = held([P, J], F32, "gates%d" % w)
+            for h in range(2):
+                gate_of[w, h] = slab_gates[:, items_of(h)]
+        diffs = {}
 
         def make_gate(w, h):
-            z = product("z%d_%d" % (w, h), Z_BANKS[w][h], [(made_side(w, ZT0), v2_side(h, 0)), (made_side(w, ZT1), v2_side(h, 1)), (made_side(w, ZV), v_side(h))])
-            nc.scalar.activation(gates[w][:, items_of(h)], z[:], ACT.Sigmoid, bias=bias[:, w : w + 1], scale=1.0)
-
-        def make_ht(w, h):
-            return product("ht%d_%d" % (w, h), HT_BANKS[w][h], [(wt_side(w, a), v2_side(h, a)) for a in range(2)])
+            z = product(bank([P, HALF], "z%d_%d" % (w, h), Z_BANKS[w][h])[:], [(made_side(w, ZV), v_side(h)), (made_side(w, ZT0), v2_side(h, 0)), (made_side(w, ZT1), v2_side(h, 1))])
+            nc.scalar.activation(gate_of[w, h], z, ACT.Sigmoid, bias=bias_of[w], scale=1.0)
 
         def make_at(w, h):
-            nc.scalar.activation(ats[w, h], make_ht(w, h)[:], ACT.Relu)
+            ht = product(bank([P, HALF], "ht%d_%d" % (w, h), HT_BANKS[w][h])[:], [(wt_side(w, a), v2_side(h, a)) for a in range(2)])
+            nc.scalar.activation(at_of[w, h], ht, ACT.Relu)
+
+        def make_hv(w, h):
+            return product(bank([P, HALF], "hv%d_%d" % (w, h), HV_BANKS[w][h])[:], [(made_side(w, WV), v_side(h))])
+
+        def subtract_at(w, h, hv):
+            nc.vector.scalar_tensor_tensor(diffs[w, h], hv, 0.0, at_of[w, h], ALU.max, ALU.subtract)
 
         def make_diff(w, h):
-            hv = product("hv%d_%d" % (w, h), HV_BANKS[w][h], [(made_side(w, WV), v_side(h))])
-            nc.vector.scalar_tensor_tensor(value_of(w, h), hv[:], 0.0, ats[w, h], ALU.max, ALU.subtract)
-
-        def finish(engine, working, result, w, h):
-            engine.tensor_tensor(working, working, ats[w, h], ALU.add)
-            engine.tensor_tensor(result, working, weight[:, items_of(h)], ALU.mult)
-
-        def block_banks(name, numbers):
-            tiles = {number: bank([P, BLOCKS, P], "%s_%d" % (name, number), number) for number in sorted(set(numbers))}
-            return [tiles[numbers[c]] for c in range(BLOCKS)]
-
-        def sum_by_transposes(w, product_rows, numbers):
-            summed = block_banks("summed%d" % w, numbers)
-            for c in range(BLOCKS):
-                cols = slice(P * c, P * (c + 1))
-                nc.tensor.matmul(summed[c][:, c, :], lhsT=product_rows[:, cols], rhs=ident[:], is_transpose=True, start=True, stop=False)
-                nc.tensor.matmul(summed[c][:, c, :], lhsT=ats[w, 1][:, cols], rhs=ident[:], is_transpose=True, start=False, stop=True)
-            return summed
-
-        def finish_by_transposes(summed, w, result, numbers):
-            weighted = held([P, BLOCKS, P], F32, "weighted%d" % w)
-            for c in range(BLOCKS):
-                nc.scalar.activation(weighted[:, c, :], summed[c][:, c, :], ACT.Copy, scale=weight_cols[:, c : c + 1])
-            upright = block_banks("upright%d" % w, numbers)
-            for c in range(BLOCKS):
-                nc.tensor.transpose(upright[c][:, c, :], weighted[:, c, :], ident[:])
-            count = BLOCKS // len(set(numbers))
-            for c in range(0, BLOCKS, count):
-                nc.scalar.copy(result[:, P * c : P * (c + count)], upright[c][:, c : c + count, :].rearrange("p c j -> p (c j)"))
-
-        def open_blend(w):
-            nc.gpsimd.tensor_tensor(gated[:], values[w][:], gates[w][:], ALU.mult)
-
-        def close_blend(w, result):
-            finish(nc.gpsimd, gated[:, items_of(0)], result[:, items_of(0)], w, 0)
-
-        woven = {}
-        out_scales = held([P, SLABS, HALF], U8, "out_scales")
+            subtract_at(w, h, make_hv(w, h))
 
         def scatter(w, h, result):
             nc.vector.tensor_copy(windows[w % 3][:].indirect(offsets_of(list1, h)), result)
@@ -261,30 +237,157 @@ def tile_list_gmu_relu_scatP_kernel(
         def store(w):
             nc.sync.dma_start(out_0[P * w : P * (w + 1), :], windows[w % 3][:])
 
-        def regroup_by_transposes(w, other_copy, turn_banks, back_banks):
-            window = windows[w % 3]
-            woven[w] = held([P, HALF, PACK], BF16, "woven%d" % w)
-            woven_words = woven[w][:].rearrange("p c i -> p (c i)").bitcast(F32).rearrange("p (g c u) -> p g c u", g=GROUPS, u=2)
-            pairs = []
-            for g in range(GROUPS):
-                turned = bank([P, 4, P], "turned%d_%d" % (w, g), turn_banks[g])
-                for chunk in range(4):
-                    first = HALF * chunk + P * g
-                    nc.tensor.transpose(turned[:, chunk, :], window[:, first : first + P], ident[:])
-                pair = held([P, 2, P, 2], BF16, "pair%d_%d" % (w, g))
-                (other_copy if g == 2 else nc.scalar.copy)(pair[:], turned[:].rearrange("p c (q u e) -> p u (c q) e", u=2, e=2))
-                pairs.append(pair)
-            for number, groups in back_banks:
-                back = bank([P, len(groups), 2, P], "back%d_%d" % (w, groups[0]), number)
-                for i, g in enumerate(groups):
-                    words = pairs[g][:].rearrange("p u m e -> p (u m e)").bitcast(F32)
-                    for u in range(2):
-                        nc.tensor.transpose(back[:, i, u, :], words[:, P * u : P * (u + 1)], ident[:])
-                other_copy(woven_words[:, groups.start : groups.stop : groups.step], back[:].rearrange("p g u c -> p g c u"))
+        open_window("room_window0", 0)
+        open_window("room_window1", 0)
+        picked_words = held([P, J], U32, "picked_words")
+        nc.vector.tensor_copy(picked_words[:], v_words[:].indirect(list1[:]))
 
-        def hand_on(name, slabs, over, other_queue, parts=1):
-            out_codes = held([P, len(slabs), HALF], U32, name, over=over)
+        reserve("room_scales", J - 64)
+        reserve("room_early_wv", 2 * J - 64)
+        reserve("room_first", 3 * J - 64)
+        reserve("room_window2", 4 * T)
+        early_wv = held([P, 2, P, PACK], BF16, "early_wv", over="room_early_wv")
+        round_weight(early_wv[:], WV, 0, 2)
+        quantise(early_wv[:], [(0, WV), (1, WV)], held([P, 2 * P], U32, "codes_wv")[:])
+        picked_scales = [held([P, HALF], U8, "picked_scales%d" % h, over="room_scales", shift=HALF * h) for h in range(2)]
+        for h in range(2):
+            nc.vector.tensor_copy(picked_scales[h][:], v_scales[:].indirect(offsets_of(list1, h)))
+        for h in range(2):
+            make_at(0, h)
+        reserve("room_diffs3", 4 * HALF)
+        reserve("room_late_zt", 8 * HALF)
+        second_bias = held([P, 1], F32, "second_bias", over="room_late_zt")
+        nc.scalar.copy(second_bias[:], bias[:, 1:2])
+        bias_of = [bias[:, 0:1], second_bias[:], bias[:, 2:3], bias[:, 3:4]]
+        gate_codes = held([P, 3 * P], U32, "gate_codes0")
+        first = held([P, 3, P, PACK], BF16, "first", over="room_first")
+        for i, m in enumerate((ZV, ZT0)):
+            round_on_gpsimd(first[:, i], m, 0, 1)
+        round_weight(first[:, 2:3], ZT1, 0, 1)
+        quantise(first[:, 0:2], [(0, ZV), (0, ZT0)], gate_codes[:, 0 : 2 * P])
+        quantise(first[:, 2:3], [(0, ZT1)], gate_codes[:, 2 * P : 3 * P])
+        open_window("room_window2", 0)
+        whole_diffs = {0: held([P, J], F32, "diffs0", over="room_early_wv", shift=64)}
+        for w in (1, 2):
+            whole_diffs[w] = held([P, J], F32, "diffs%d" % w)
+        for w in range(3):
+            for h in range(2):
+                diffs[w, h] = whole_diffs[w][:, items_of(h)]
+        for h in range(2):
+            make_diff(0, h)
+            make_gate(0, h)
+
+        work0 = held([P, J], F32, "work0")
+        for h in range(2):
+            nc.vector.tensor_tensor(work0[:, items_of(h)], diffs[0, h], gate_of[0, h], ALU.mult)
+        nc.vector.tensor_tensor(work0[:], work0[:], ats[0][:], ALU.add)
+        second = held([P, 3, P, PACK], BF16, "second", over="room_gate0")
+        for i, m in enumerate((ZV, ZT0, ZT1)):
+            round_weight(second[:, i : i + 1], m, 1, 1)
+        quantise(second[:], [(1, ZV), (1, ZT0), (1, ZT1)], held([P, 3 * P], U32, "gate_codes1", over="room_gate1")[:])
+        for h in range(2):
+            make_at(1, h)
+        results0 = held([P, J], F32, "results0")
+        make_diff(1, 0)
+        nc.vector.tensor_tensor(results0[:], work0[:], weight, ALU.mult)
+        make_diff(1, 1)
+        nc.vector.tensor_copy(windows[0][:].indirect(list1[:]), results0[:])
+        store(0)
+
+        late_zv = held([P, 2, P, PACK], BF16, "late_zv", over="work0")
+        round_on_gpsimd(late_zv[:].rearrange("p w c j -> p (w c) j"), ZV, 2, 2)
+        for h in range(2):
+            make_gate(1, h)
+        work1 = [held([P, HALF], F32, "work1_%d" % h) for h in range(2)]
+        for h in range(2):
+            nc.gpsimd.tensor_tensor(work1[h][:], diffs[1, h], gate_of[1, h], ALU.mult)
+        for h in range(2):
+            nc.gpsimd.tensor_tensor(work1[h][:], work1[h][:], at_of[1, h], ALU.add)
+
+        late_wv = held([P, 2, P, PACK], BF16, "late_wv", over="ats0")
+        round_weight(late_wv[:], WV, 2, 2)
+        late_zt = held([P, 2, 2, P, PACK], BF16, "late_zt", over="room_late_zt")
+        for i, m in enumerate((ZT0, ZT1)):
+            round_weight(late_zt[:, :, i], m, 2, 2)
+        for w in (2, 3):
+            for h in range(2):
+                make_at(w, h)
+        late_codes = held([P, 8 * P], U32, "late_codes")
+        late_parts = (
+            (late_wv[:], [(2, WV), (3, WV)]),
+            (late_zv[:], [(2, ZV), (3, ZV)]),
+            (late_zt[:, 0], [(2, ZT0), (2, ZT1)]),
+            (late_zt[:, 1], [(3, ZT0), (3, ZT1)]),
+        )
+        for i, (grouped, parts) in enumerate(late_parts):
+            quantise(grouped, parts, late_codes[:, 2 * P * i : 2 * P * (i + 1)], "wt_codes1", 2 * P * i)
+        result10 = held([P, HALF], F32, "result10", over="late_zt")
+        nc.gpsimd.tensor_tensor(result10[:], work1[0][:], weight[:, items_of(0)], ALU.mult)
+        result11 = held([P, HALF], F32, "result11", over="late_zt", shift=4 * HALF)
+        nc.gpsimd.tensor_tensor(result11[:], work1[1][:], weight[:, items_of(1)], ALU.mult)
+        for h in range(2):
+            make_diff(2, h)
+        for h in range(2):
+            make_gate(2, h)
+        last_hv = [make_hv(3, h) for h in range(2)]
+        for h in range(2):
+            make_gate(3, h)
+        scatter(1, 0, result10[:])
+        whole_diffs[3] = held([P, J], F32, "diffs3", over="room_diffs3")
+        for h in range(2):
+            diffs[3, h] = whole_diffs[3][:, items_of(h)]
+            subtract_at(3, h, last_hv[h])
+        scatter(1, 1, result11[:])
+        store(1)
+
+        for h in range(2):
+            part = held([P, HALF], F32, "work2_%d" % h, over=("work1_1", "at2_0")[h])[:]
+            nc.gpsimd.tensor_tensor(part, diffs[2, h], gate_of[2, h], ALU.mult)
+            nc.gpsimd.tensor_tensor(part, part, at_of[2, h], ALU.add)
+            nc.gpsimd.tensor_tensor(diffs[2, h], part, weight[:, items_of(h)], ALU.mult)
+        work3 = held([P, J], F32, "work3", over="at2_0")
+        nc.gpsimd.tensor_tensor(work3[:], whole_diffs[3][:], slab_gates[:], ALU.mult)
+        nc.gpsimd.tensor_tensor(work3[:], work3[:], ats[3][:], ALU.add)
+
+        woven = {}
+        out_scales = held([P, SLABS, HALF], U8, "out_scales")
+
+        def turn(w, g, turned, copy):
+            for chunk in range(4):
+                first = HALF * chunk + P * g
+                nc.tensor.transpose(turned[:, chunk, :], windows[w % 3][:, first : first + P], ident[:])
+            pair = held([P, 2, P, 2], BF16, "pair%d_%d" % (w, g))
+            copy(pair[:], turned.rearrange("p c (q u e) -> p u (c q) e", u=2, e=2))
+            return pair
+
+        def turn_back(w, pair, g, number, copy):
+            woven_words = woven[w][:].rearrange("p c i -> p (c i)").bitcast(F32).rearrange("p (g c u) -> p g c u", g=GROUPS, u=2)
+            back = bank([P, 2, P], "back%d_%d" % (w, g), number)
+            words = pair[:].rearrange("p u m e -> p (u m e)").bitcast(F32)
+            for u in range(2):
+                nc.tensor.transpose(back[:, u, :], words[:, P * u : P * (u + 1)], ident[:])
+            copy(woven_words[:, g], back[:].rearrange("p u c -> p c u"))
+
+        def regroup(w, turn_copies, back_copies):
+            woven[w] = held([P, HALF, PACK], BF16, "woven%d" % w)
+            pairs = [turn(w, g, bank([P, 4, P], "turned%d_%d" % (w, g), REGROUP_BANKS[w % 2][g])[:], turn_copies[g]) for g in range(GROUPS)]
+            for g in range(GROUPS):
+                turn_back(w, pairs[g], g, REGROUP_BANKS[1 - w % 2][g], back_copies[g])
+
+        on_scalar = [nc.scalar.copy] * GROUPS
+        regroup(0, on_scalar, on_scalar)
+        regroup(1, on_scalar, on_scalar)
+        for h in range(2):
+            scatter(2, h, diffs[2, h])
+        store(2)
+        regroup(2, on_scalar, on_scalar)
+        nc.vector.tensor_tensor(windows[0][:].indirect(list1[:]), work3[:], weight, ALU.mult)
+        store(3)
+
+        def hand_on(name, slabs, over, shift, other_queue):
+            out_codes = held([P, len(slabs), HALF], U32, name, over=over, shift=shift)
             for i, w in enumerate(slabs):
+                parts = GROUPS if w == SLABS - 1 else 1
                 for part in range(parts):
                     cols = slice(HALF // parts * part, HALF // parts * (part + 1))
                     nc.vector.quantize_mx(
@@ -298,103 +401,10 @@ def tile_list_gmu_relu_scatP_kernel(
                     out_codes[QUADRANT * chunk : QUADRANT * (chunk + 1)].bitcast(I32),
                 )
 
-        both = held([P, J], U32, "picked2_both", over="room_window1")
-        nc.vector.tensor_copy(both[:], v2_words[:].indirect(list2[:]))
-        parted = held([P, 2, 2 * J], U8, "picked2_words")
-        nc.vector.tensor_copy(parted[:].bitcast(U16), both[:].bitcast(U16).rearrange("p (j d) -> p d j", d=2))
-        open_window(1)
-        picked_words = held([P, J], U32, "picked_words")
-        nc.vector.tensor_copy(picked_words[:], v_words[:].indirect(list1[:]))
-
-        first_zt = rounded("first_zt", 2, over="room_scales")
-        first_v = rounded("first_v", 2)
-        second = rounded("second", MATS)
-        for m in (ZT0, ZT1):
-            round_weight(nc.scalar.copy, first_zt, m, 0, m)
-            round_weight(nc.scalar.copy, second, m, 1, m)
-        quantise(first_zt, 0, ZT0, 2)
-        open_window(2)
-        picked_scales = held([P, J], U8, "picked_scales", over="room_scales")
-        nc.vector.tensor_copy(picked_scales[:], v_scales[:].indirect(list1[:]))
-        round_weight(nc.scalar.copy, first_v, 0, 0, ZV)
-        round_weight(nc.scalar.copy, second, ZV, 1, ZV)
-        make_at(0, 0)
-        ht_second = make_ht(0, 1)
-        round_weight(nc.vector.tensor_copy, first_v, 1, 0, WV)
-        quantise(first_v, 0, ZV, 2)
-        make_gate(0, 0)
-        round_weight(nc.vector.tensor_copy, second, WV, 1, WV)
-        quantise(second, 1, 0, MATS)
-        ident = held([P, P], F32, "ident", over="second", shift=4 * HALF)
-        make_identity(nc, ident[:])
-        make_diff(0, 0)
-        nc.scalar.activation(ats[0, 1], ht_second[:], ACT.Relu)
-        make_diff(0, 1)
-        make_gate(0, 1)
-        nc.vector.tensor_tensor(gated[:, items_of(0)], value_of(0, 0), gates[0][:, items_of(0)], ALU.mult)
-        first_result = held([P, HALF], F32, "first_result", over="second")
-        finish(nc.vector, gated[:, items_of(0)], first_result[:], 0, 0)
-        nc.gpsimd.tensor_tensor(gated[:, items_of(0)], value_of(0, 1), gates[0][:, items_of(1)], ALU.mult)
-        finish(nc.gpsimd, gated[:, items_of(0)], value_of(0, 1), 0, 1)
-        for h in (1, 0):
-            make_at(1, h)
-        for h in (1, 0):
-            make_diff(1, h)
-        for h in (1, 0):
-            make_gate(1, h)
-        third = rounded("third", MATS)
-        fourth = rounded("fourth", MATS, over="room_fourth")
-        for m in (WV, ZV, ZT0, ZT1):
-            round_weight(nc.scalar.copy, third, m, 2, m)
-            round_weight(nc.scalar.copy, fourth, m, 3, m)
-        open_blend(1)
-        nc.gpsimd.tensor_tensor(gated[:, items_of(0)], gated[:, items_of(0)], ats[1, 0], ALU.add)
-        scatter(0, 0, first_result[:])
-        scatter(0, 1, value_of(0, 1))
-        store(0)
-        for w in (2, 3):
-            for h in (1, 0):
-                make_at(w, h)
-        late_codes = held([P, 2, MATS * P], U32, "late_codes", over="values0", shift=4 * HALF)
-        codes[2], codes[3] = late_codes[:, 0, :], late_codes[:, 1, :]
-        quantise(third, 2, 0, MATS)
-        quantise(fourth, 3, 0, MATS)
-        held_back = [held([P, HALF], F32, "held_back%d" % h, over="fourth", shift=6 * HALF * h) for h in range(2)]
-        nc.gpsimd.tensor_tensor(held_back[0][:], gated[:, items_of(0)], weight[:, items_of(0)], ALU.mult)
-        nc.gpsimd.tensor_tensor(held_back[1][:], gated[:, items_of(1)], ats[1, 1], ALU.add)
-        nc.gpsimd.tensor_tensor(value_of(1, 1), held_back[1][:], weight[:, items_of(1)], ALU.mult)
-        results = {(w, h): value_of(w, h) for w in range(SLABS) for h in range(2)}
-        results[1, 0] = held_back[0][:]
-        for w in (2, 3):
-            for h in (1, 0):
-                make_diff(w, h)
-        for w in (2, 3):
-            for h in (1, 0):
-                make_gate(w, h)
-        for w in (2, 3):
-            if w == 2:
-                open_blend(w)
-            else:
-                for h in (1, 0):
-                    nc.gpsimd.tensor_tensor(gated[:, items_of(h)], value_of(w, h), gates[w][:, items_of(h)], ALU.mult)
-            close_blend(w, values[w])
-            summed = sum_by_transposes(w, gated[:, items_of(1)], (6, 6, 6, 6))
-            finish_by_transposes(summed, w, value_of(w, 1), (7, 7, 7, 7))
-        for w in range(1, SLABS):
-            if w == SLABS - 1:
-                nc.vector.tensor_copy(windows[0][:].indirect(list1[:]), values[w][:])
-            else:
-                for h in range(2):
-                    scatter(w, h, results[w, h])
-            store(w)
-            if w == 1:
-                for early in range(2):
-                    regroup_by_transposes(early, nc.scalar.copy, (1, 3, 1, 3), [(0, range(0, 2)), (2, range(2, 4))])
-            if w == 2:
-                regroup_by_transposes(w, nc.scalar.copy, (7, 3, 0, 2), [(3, range(1, 3)), (7, range(0, 4, 3))])
-        hand_on("early_codes", [0, 1, 2], "values2", nc.scalar)
-        regroup_by_transposes(SLABS - 1, nc.vector.tensor_copy, (2, 3, 7, 2), [(number, range(g, g + 1)) for g, number in enumerate((1, 4, 5, 6))])
-        hand_on("last_codes", [3], "", nc.scalar, parts=2)
+        hand_on("early_codes", [0, 1, 2], "work3", 0, nc.scalar)
+        last = SLABS - 1
+        regroup(last, on_scalar[:3] + [nc.vector.tensor_copy], on_scalar[:2] + [nc.vector.tensor_copy] * 2)
+        hand_on("last_codes", [last], "", 0, nc.scalar)
         for chunk in range(4):
             (nc.sync if chunk < 2 else nc.scalar).dma_start(
                 out_2[0].rearrange("(w r) t -> r w t", r=4)[:, :, HALF * chunk : HALF * (chunk + 1)].bitcast(I32),

@@ -30,10 +30,12 @@ BLOCKS = HALF // P
 BANK = 2048
 BY_PORT = (0, 2, 1, 3)
 WV, ZV, ZT0, ZT1 = range(MATS)
-HT_BANKS = ((0, 1), (2, 3), (0, 1), (0, 1))
-HV_BANKS = ((4, 5), (4, 5), (4, 5), (0, 1))
-Z_BANKS = ((2, 3), (0, 1), (6, 7), (4, 5))
-REGROUP_BANKS = ((4, 5, 0, 1), (2, 3, 6, 7))
+HT_BANKS = ((0, 1), (6, 7), (2, 3), (4, 5))
+HV_BANKS = ((4, 5), (4, 5), (0, 1), (2, 3))
+Z_BANKS = ((2, 3), (6, 7), (6, 7), (0, 1))
+SUM_BANKS = (0, 2)
+REGROUP_BANKS = ((0, 2, 6, 7), (4, 1, 3, 5))
+FIRST_TURN_BANKS = (2, 0, 2, 0)
 
 
 def tile_list_gmu_relu_scatP_kernel(
@@ -82,7 +84,7 @@ def tile_list_gmu_relu_scatP_kernel(
         reserve("room_window0", 4 * T)
         v2_scales = held([P, T], U8, "v2_scales", over="room_window0", shift=4 * T - 64)
         reserve("room_between", T - 128)
-        loaded = held([P, MATS * PACK * N + J + SLABS], F32, "loaded")
+        loaded = held([P, MATS * PACK * N + J + SLABS + BLOCKS], F32, "loaded")
         v_scales = held([P, T], U8, "v_scales")
         planes2 = held([P, 2 * J], U8, "planes2")
         wt_planes = held([P, 2 * N], U8, "wt_planes")
@@ -92,7 +94,8 @@ def tile_list_gmu_relu_scatP_kernel(
         both = held([P, J], U32, "picked2_both", over="room_window1", shift=4 * T - 2 * J)
         wt_codes = {u: held([P, 2, 2 * P], I32, "wt_codes%d" % u) for u in (1, 0)}
         weight = loaded[:, MATS * PACK * N : MATS * PACK * N + J]
-        bias = loaded[:, MATS * PACK * N + J :]
+        bias = loaded[:, MATS * PACK * N + J : MATS * PACK * N + J + SLABS]
+        weight_cols = loaded[:, MATS * PACK * N + J + SLABS :]
 
         nc.vector.memset(v2_scales[0:LOADED_ROW, :].bitcast(I32), 0)
         for tile in (wt_planes, v_scales, planes2):
@@ -108,8 +111,8 @@ def tile_list_gmu_relu_scatP_kernel(
             start = PACK * (N * m + P * first)
             return loaded[:, start : start + PACK * P * count].rearrange("p (j n) -> p j n", j=PACK)
 
-        def load_weight(m, first, count):
-            nc.sync.dma_start(raw(m, first, count), sources[m].rearrange("(p j) n -> p j n", j=PACK)[:, :, P * first : P * (first + count)])
+        def load_weight(m, first, count, tile=None):
+            nc.sync.dma_start(raw(m, first, count) if tile is None else tile, sources[m].rearrange("(p j) n -> p j n", j=PACK)[:, :, P * first : P * (first + count)])
 
         def load_wt(u):
             nc.sync.dma_start(wt_codes[u][:], wt_words.rearrange("a p n i -> p a (n i)").bitcast(I32)[:, :, 2 * P * u : 2 * P * (u + 1)])
@@ -143,17 +146,21 @@ def tile_list_gmu_relu_scatP_kernel(
         for q in BY_PORT:
             load_v_scales(q)
         load_weight(ZT0, 0, 1)
-        load_weight(ZT1, 0, 1)
+        last_first = held([P, PACK, P], F32, "last_first", over="v2_words", shift=J)
+        load_weight(ZT1, 0, 1, last_first[:])
         with nc.allow_non_contiguous_dma(reason="one value a partition and column"):
             nc.sync.dma_start(bias, b.rearrange("(w p) -> p w", p=P))
         for m in (ZV, ZT0, ZT1):
             load_weight(m, 1, 1)
-        load_weight(WV, 2, 2)
-        nc.sync.dma_start(weight, wgo)
-        load_weight(ZV, 2, 2)
         load_wt(1)
-        for m in (ZT0, ZT1):
-            load_weight(m, 2, 2)
+        nc.sync.dma_start(weight, wgo)
+        load_weight(WV, 2, 2)
+        load_weight(ZV, 2, 2)
+        load_weight(ZT0, 2, 2)
+        last_late = held([P, PACK, 2 * P], F32, "last_late", over="v2_words", shift=4 * J)
+        load_weight(ZT1, 2, 2, last_late[:])
+        with nc.allow_non_contiguous_dma(reason="one value a partition and column"):
+            nc.sync.dma_start(weight_cols, wgo[0, 0:HALF].rearrange("(c p) -> p c", p=P))
 
         windows = []
 
@@ -163,10 +170,10 @@ def tile_list_gmu_relu_scatP_kernel(
 
         made = {}
 
-        def round_weight(grouped, m, first, count):
+        def round_weight(grouped, rows):
             nc.scalar.copy(
                 grouped.rearrange("p w (c i) j -> p w c j i", i=4),
-                raw(m, first, count).rearrange("p j (w c i) -> p w c j i", i=4, c=P // 4),
+                rows.rearrange("p j (w c i) -> p w c j i", i=4, c=P // 4),
             )
 
         def round_on_gpsimd(grouped, m, first, count):
@@ -199,19 +206,15 @@ def tile_list_gmu_relu_scatP_kernel(
                 )
             return acc
 
-        ats = {w: held([P, J], F32, "ats%d" % w) for w in (0, 3)}
-        at_of = {(w, h): ats[w][:, items_of(h)] for w in (0, 3) for h in range(2)}
-        for w in (1, 2):
-            for h in range(2):
-                at_of[w, h] = held([P, HALF], F32, "at%d_%d" % (w, h))[:]
+        ats = {0: held([P, J], F32, "ats0")}
+        at_of = {(0, h): ats[0][:, items_of(h)] for h in range(2)}
         gate_of = {}
         for h in range(2):
             reserve("room_gate%d" % h, 8 * HALF)
             gate_of[0, h] = held([P, HALF], F32, "gate0_%d" % h, over="room_gate%d" % h)[:]
         for w in range(1, SLABS):
-            slab_gates = held([P, J], F32, "gates%d" % w)
             for h in range(2):
-                gate_of[w, h] = slab_gates[:, items_of(h)]
+                gate_of[w, h] = held([P, HALF], F32, "gate%d_%d" % (w, h))[:]
         diffs = {}
 
         def make_gate(w, h):
@@ -247,50 +250,55 @@ def tile_list_gmu_relu_scatP_kernel(
         reserve("room_first", 3 * J - 64)
         reserve("room_window2", 4 * T)
         early_wv = held([P, 2, P, PACK], BF16, "early_wv", over="room_early_wv")
-        round_weight(early_wv[:], WV, 0, 2)
+        round_weight(early_wv[:], raw(WV, 0, 2))
         quantise(early_wv[:], [(0, WV), (1, WV)], held([P, 2 * P], U32, "codes_wv")[:])
         picked_scales = [held([P, HALF], U8, "picked_scales%d" % h, over="room_scales", shift=HALF * h) for h in range(2)]
         for h in range(2):
             nc.vector.tensor_copy(picked_scales[h][:], v_scales[:].indirect(offsets_of(list1, h)))
         for h in range(2):
             make_at(0, h)
-        reserve("room_diffs3", 4 * HALF)
+        reserve("room_ats3", 4 * J)
         reserve("room_late_zt", 8 * HALF)
-        second_bias = held([P, 1], F32, "second_bias", over="room_late_zt")
-        nc.scalar.copy(second_bias[:], bias[:, 1:2])
-        bias_of = [bias[:, 0:1], second_bias[:], bias[:, 2:3], bias[:, 3:4]]
+        second_bias = held([P, 32], F32, "second_bias", over="room_late_zt", shift=-64)
+        nc.gpsimd.tensor_copy(second_bias[:, 0:1], bias[:, 1:2])
+        bias_of = [bias[:, 0:1], second_bias[:, 0:1], bias[:, 2:3], bias[:, 3:4]]
         gate_codes = held([P, 3 * P], U32, "gate_codes0")
         first = held([P, 3, P, PACK], BF16, "first", over="room_first")
         for i, m in enumerate((ZV, ZT0)):
             round_on_gpsimd(first[:, i], m, 0, 1)
-        round_weight(first[:, 2:3], ZT1, 0, 1)
+        round_weight(first[:, 2:3], last_first[:])
         quantise(first[:, 0:2], [(0, ZV), (0, ZT0)], gate_codes[:, 0 : 2 * P])
         quantise(first[:, 2:3], [(0, ZT1)], gate_codes[:, 2 * P : 3 * P])
         open_window("room_window2", 0)
+        for h in range(2):
+            at_of[1, h] = held([P, HALF], F32, "at1_%d" % h, over="v2_words", shift=4 * HALF * h)[:]
+            make_at(1, h)
         whole_diffs = {0: held([P, J], F32, "diffs0", over="room_early_wv", shift=64)}
         for w in (1, 2):
             whole_diffs[w] = held([P, J], F32, "diffs%d" % w)
         for w in range(3):
             for h in range(2):
                 diffs[w, h] = whole_diffs[w][:, items_of(h)]
-        for h in range(2):
-            make_diff(0, h)
-            make_gate(0, h)
+        make_diff(0, 0)
+        make_gate(0, 0)
+        make_diff(0, 1)
+        make_diff(1, 0)
+        make_gate(0, 1)
 
         work0 = held([P, J], F32, "work0")
-        for h in range(2):
-            nc.vector.tensor_tensor(work0[:, items_of(h)], diffs[0, h], gate_of[0, h], ALU.mult)
+        nc.vector.tensor_tensor(work0[:, items_of(0)], diffs[0, 0], gate_of[0, 0], ALU.mult)
+        make_diff(1, 1)
+        nc.vector.tensor_tensor(work0[:, items_of(1)], diffs[0, 1], gate_of[0, 1], ALU.mult)
         nc.vector.tensor_tensor(work0[:], work0[:], ats[0][:], ALU.add)
         second = held([P, 3, P, PACK], BF16, "second", over="room_gate0")
         for i, m in enumerate((ZV, ZT0, ZT1)):
-            round_weight(second[:, i : i + 1], m, 1, 1)
+            round_weight(second[:, i : i + 1], raw(m, 1, 1))
         quantise(second[:], [(1, ZV), (1, ZT0), (1, ZT1)], held([P, 3 * P], U32, "gate_codes1", over="room_gate1")[:])
         for h in range(2):
-            make_at(1, h)
+            at_of[2, h] = held([P, HALF], F32, "at2_%d" % h, over="second", shift=4 * HALF * h)[:]
+            make_at(2, h)
         results0 = held([P, J], F32, "results0")
-        make_diff(1, 0)
         nc.vector.tensor_tensor(results0[:], work0[:], weight, ALU.mult)
-        make_diff(1, 1)
         nc.vector.tensor_copy(windows[0][:].indirect(list1[:]), results0[:])
         store(0)
 
@@ -304,14 +312,15 @@ def tile_list_gmu_relu_scatP_kernel(
         for h in range(2):
             nc.gpsimd.tensor_tensor(work1[h][:], work1[h][:], at_of[1, h], ALU.add)
 
-        late_wv = held([P, 2, P, PACK], BF16, "late_wv", over="ats0")
-        round_weight(late_wv[:], WV, 2, 2)
+        late_wv = held([P, 2, P, PACK], BF16, "late_wv", over="diffs0")
+        round_weight(late_wv[:], raw(WV, 2, 2))
         late_zt = held([P, 2, 2, P, PACK], BF16, "late_zt", over="room_late_zt")
-        for i, m in enumerate((ZT0, ZT1)):
-            round_weight(late_zt[:, :, i], m, 2, 2)
-        for w in (2, 3):
-            for h in range(2):
-                make_at(w, h)
+        for i, rows in enumerate((raw(ZT0, 2, 2), last_late[:])):
+            round_weight(late_zt[:, :, i], rows)
+        ats[3] = held([P, J], F32, "ats3", over="room_ats3")
+        for h in range(2):
+            at_of[3, h] = ats[3][:, items_of(h)]
+            make_at(3, h)
         late_codes = held([P, 8 * P], U32, "late_codes")
         late_parts = (
             (late_wv[:], [(2, WV), (3, WV)]),
@@ -320,36 +329,49 @@ def tile_list_gmu_relu_scatP_kernel(
             (late_zt[:, 1], [(3, ZT0), (3, ZT1)]),
         )
         for i, (grouped, parts) in enumerate(late_parts):
-            quantise(grouped, parts, late_codes[:, 2 * P * i : 2 * P * (i + 1)], "wt_codes1", 2 * P * i)
+            quantise(grouped, parts, late_codes[:, 2 * P * i : 2 * P * (i + 1)], "last_late", 2 * P * i)
         result10 = held([P, HALF], F32, "result10", over="late_zt")
         nc.gpsimd.tensor_tensor(result10[:], work1[0][:], weight[:, items_of(0)], ALU.mult)
         result11 = held([P, HALF], F32, "result11", over="late_zt", shift=4 * HALF)
         nc.gpsimd.tensor_tensor(result11[:], work1[1][:], weight[:, items_of(1)], ALU.mult)
-        for h in range(2):
-            make_diff(2, h)
+        diffs[3, 0] = held([P, HALF], F32, "diff3_0")[:]
+        for w, h in ((2, 0), (2, 1), (3, 0)):
+            make_diff(w, h)
+        last_hv = make_hv(3, 1)
         for h in range(2):
             make_gate(2, h)
-        last_hv = [make_hv(3, h) for h in range(2)]
         for h in range(2):
             make_gate(3, h)
         scatter(1, 0, result10[:])
-        whole_diffs[3] = held([P, J], F32, "diffs3", over="room_diffs3")
-        for h in range(2):
-            diffs[3, h] = whole_diffs[3][:, items_of(h)]
-            subtract_at(3, h, last_hv[h])
+        diffs[3, 1] = held([P, HALF], F32, "diff3_1", over="work1_0")[:]
+        subtract_at(3, 1, last_hv)
         scatter(1, 1, result11[:])
         store(1)
 
+        work2 = [held([P, HALF], F32, "work2_%d" % h, over=("at1_0", "gate2_0")[h]) for h in range(2)]
         for h in range(2):
-            part = held([P, HALF], F32, "work2_%d" % h, over=("work1_1", "at2_0")[h])[:]
-            nc.gpsimd.tensor_tensor(part, diffs[2, h], gate_of[2, h], ALU.mult)
-            nc.gpsimd.tensor_tensor(part, part, at_of[2, h], ALU.add)
-            nc.gpsimd.tensor_tensor(diffs[2, h], part, weight[:, items_of(h)], ALU.mult)
-        work3 = held([P, J], F32, "work3", over="at2_0")
-        nc.gpsimd.tensor_tensor(work3[:], whole_diffs[3][:], slab_gates[:], ALU.mult)
+            nc.gpsimd.tensor_tensor(work2[h][:], diffs[2, h], gate_of[2, h], ALU.mult)
+        nc.gpsimd.tensor_tensor(work2[1][:], work2[1][:], at_of[2, 1], ALU.add)
+        nc.gpsimd.tensor_tensor(diffs[2, 1], work2[1][:], weight[:, items_of(1)], ALU.mult)
+        summed = bank([P, BLOCKS, P], "summed", SUM_BANKS[0])
+        for c in range(BLOCKS):
+            cols = slice(P * c, P * (c + 1))
+            nc.tensor.matmul(summed[:, c, :], lhsT=work2[0][:, cols], rhs=ident[:], is_transpose=True, start=True, stop=False)
+            nc.tensor.matmul(summed[:, c, :], lhsT=at_of[2, 0][:, cols], rhs=ident[:], is_transpose=True, start=False, stop=True)
+        weighted = held([P, BLOCKS, P], F32, "weighted")
+        for c in range(BLOCKS):
+            nc.scalar.activation(weighted[:, c, :], summed[:, c, :], ACT.Copy, scale=weight_cols[:, c : c + 1])
+        upright = bank([P, BLOCKS, P], "upright", SUM_BANKS[1])
+        for c in range(BLOCKS):
+            nc.tensor.transpose(upright[:, c, :], weighted[:, c, :], ident[:])
+        nc.scalar.copy(diffs[2, 0], upright[:].rearrange("p c j -> p (c j)"))
+        work3 = held([P, J], F32, "work3", over="gate2_0")
+        for h in range(2):
+            nc.gpsimd.tensor_tensor(work3[:, items_of(h)], diffs[3, h], gate_of[3, h], ALU.mult)
         nc.gpsimd.tensor_tensor(work3[:], work3[:], ats[3][:], ALU.add)
 
         woven = {}
+        whole_woven = {}
         out_scales = held([P, SLABS, HALF], U8, "out_scales")
 
         def turn(w, g, turned, copy):
@@ -361,16 +383,20 @@ def tile_list_gmu_relu_scatP_kernel(
             return pair
 
         def turn_back(w, pair, g, number, copy):
-            woven_words = woven[w][:].rearrange("p c i -> p (c i)").bitcast(F32).rearrange("p (g c u) -> p g c u", g=GROUPS, u=2)
             back = bank([P, 2, P], "back%d_%d" % (w, g), number)
             words = pair[:].rearrange("p u m e -> p (u m e)").bitcast(F32)
             for u in range(2):
                 nc.tensor.transpose(back[:, u, :], words[:, P * u : P * (u + 1)], ident[:])
-            copy(woven_words[:, g], back[:].rearrange("p u c -> p c u"))
+            copy(woven[w][g].bitcast(F32).rearrange("p (c u) -> p c u", u=2), back[:].rearrange("p u c -> p c u"))
 
         def regroup(w, turn_copies, back_copies):
-            woven[w] = held([P, HALF, PACK], BF16, "woven%d" % w)
-            pairs = [turn(w, g, bank([P, 4, P], "turned%d_%d" % (w, g), REGROUP_BANKS[w % 2][g])[:], turn_copies[g]) for g in range(GROUPS)]
+            if w < SLABS - 1:
+                whole_woven[w] = held([P, HALF * PACK], BF16, "woven%d" % w)
+                woven[w] = [whole_woven[w][:, P * PACK * g : P * PACK * (g + 1)] for g in range(GROUPS)]
+            else:
+                woven[w] = [held([P, P * PACK], BF16, "woven%d_%d" % (w, g))[:] for g in range(GROUPS)]
+            turn_banks = REGROUP_BANKS[w % 2] if w else FIRST_TURN_BANKS
+            pairs = [turn(w, g, bank([P, 4, P], "turned%d_%d" % (w, g), turn_banks[g])[:], turn_copies[g]) for g in range(GROUPS)]
             for g in range(GROUPS):
                 turn_back(w, pairs[g], g, REGROUP_BANKS[1 - w % 2][g], back_copies[g])
 
@@ -387,13 +413,10 @@ def tile_list_gmu_relu_scatP_kernel(
         def hand_on(name, slabs, over, shift, other_queue):
             out_codes = held([P, len(slabs), HALF], U32, name, over=over, shift=shift)
             for i, w in enumerate(slabs):
-                parts = GROUPS if w == SLABS - 1 else 1
-                for part in range(parts):
-                    cols = slice(HALF // parts * part, HALF // parts * (part + 1))
-                    nc.vector.quantize_mx(
-                        out=out_codes[:, i, cols].bitcast(FP8X4), scales=out_scales[:, w, cols],
-                        in_=woven[w][:, cols, :].rearrange("p c i -> p (c i)"),
-                    )
+                parts = woven[w] if w == SLABS - 1 else [whole_woven[w][:]]
+                for part, rounded in enumerate(parts):
+                    cols = slice(HALF // len(parts) * part, HALF // len(parts) * (part + 1))
+                    nc.vector.quantize_mx(out=out_codes[:, i, cols].bitcast(FP8X4), scales=out_scales[:, w, cols], in_=rounded)
             rows = words_view(out_1).rearrange("(w q) t -> q w t", q=QUADRANT)
             for chunk in (0, 2, 1, 3):
                 (nc.sync if chunk < 2 else other_queue).dma_start(
@@ -401,7 +424,7 @@ def tile_list_gmu_relu_scatP_kernel(
                     out_codes[QUADRANT * chunk : QUADRANT * (chunk + 1)].bitcast(I32),
                 )
 
-        hand_on("early_codes", [0, 1, 2], "work3", 0, nc.scalar)
+        hand_on("early_codes", [0, 1, 2], "work3", -4 * HALF, nc.scalar)
         last = SLABS - 1
         regroup(last, on_scalar[:3] + [nc.vector.tensor_copy], on_scalar[:2] + [nc.vector.tensor_copy] * 2)
         hand_on("last_codes", [last], "", 0, nc.scalar)

@@ -105,6 +105,9 @@ def tile_list_gmu_relu_scatP_kernel(
         nc.vector.memset(ident[:], 0.0)
         make_identity(nc, ident[:], nomemset=True)
 
+        unread = held([P, 1], F32, "unread")
+        nc.scalar.activation(unread[:], ident[:, 0:1], ACT.Sigmoid)
+
         sources = [wv, zv, zt[0:512, :], zt[512:1024, :]]
 
         def raw(m, first, count):

@@ -1,7 +1,6 @@
 from contextlib import ExitStack
 
 import concourse.mybir as mybir
-from concourse.masks import make_identity
 
 K, L, N, T, J = 512, 1024, 512, 2048, 1024
 FLOPS = 2 * N * J * (K + L) * 2
@@ -82,16 +81,16 @@ def tile_list_gmu_relu_scatP_kernel(
         list1 = lists.tile([P, J // 16], U16, name="list1")
         list2 = lists.tile([P, J // 16], U16, name="list2")
         reserve("room_window0", 4 * T)
-        v2_scales = held([P, T], U8, "v2_scales", over="room_window0", shift=4 * T - 64)
-        reserve("room_between", T - 128)
+        reserve("room_v2_scales", T - 64)
+        v2_scales = held([P, T], U8, "v2_scales", over="room_v2_scales")
         loaded = held([P, MATS * PACK * N + J + SLABS + BLOCKS], F32, "loaded")
         v_scales = held([P, T], U8, "v_scales")
         planes2 = held([P, 2 * J], U8, "planes2")
         wt_planes = held([P, 2 * N], U8, "wt_planes")
         v2_words = held([P, T], U32, "v2_words")
         v_words = held([P, T], U32, "v_words")
-        reserve("room_window1", 4 * T)
-        both = held([P, J], U32, "picked2_both", over="room_window1", shift=4 * T - 2 * J)
+        reserve("room_both", 2 * J)
+        both = held([P, J], U32, "picked2_both", over="room_both")
         wt_codes = {u: held([P, 2, 2 * P], I32, "wt_codes%d" % u) for u in (1, 0)}
         weight = loaded[:, MATS * PACK * N : MATS * PACK * N + J]
         bias = loaded[:, MATS * PACK * N + J : MATS * PACK * N + J + SLABS]
@@ -101,9 +100,12 @@ def tile_list_gmu_relu_scatP_kernel(
         for tile in (wt_planes, v_scales, planes2):
             nc.vector.memset(tile[:].bitcast(I32), 0)
 
+        zeros = held([P, P], F32, "zeros", over="room_window0")
+        nc.vector.memset(zeros[:], 0.0)
         ident = held([P, P], F32, "ident")
-        nc.vector.memset(ident[:], 0.0)
-        make_identity(nc, ident[:], nomemset=True)
+        nc.gpsimd.affine_select(
+            out=ident[:], in_=zeros[:], compare_op=ALU.not_equal, fill=1.0, base=0, pattern=[[-1, P]], channel_multiplier=1
+        )
 
         unread = held([P, 1], F32, "unread")
         nc.scalar.activation(unread[:], ident[:, 0:1], ACT.Sigmoid)
@@ -139,9 +141,11 @@ def tile_list_gmu_relu_scatP_kernel(
             load_wt_scales(q)
         picked2_scales = held([P, J], U8, "picked2_scales")
         nc.vector.tensor_copy(picked2_scales[:], v2_scales[:].indirect(list2[:]))
-        nc.vector.tensor_copy(both[:], v2_words[:].indirect(list2[:]))
-        parted = held([P, 2, 2 * J], U8, "picked2_words")
-        nc.vector.tensor_copy(parted[:].bitcast(U16), both[:].bitcast(U16).rearrange("p (j d) -> p d j", d=2))
+        for h in range(2):
+            nc.vector.tensor_copy(both[:, items_of(h)], v2_words[:].indirect(offsets_of(list2, h)))
+        parted = [held([P, 2, 2 * HALF], U8, "picked2_words%d" % h) for h in range(2)]
+        for h in range(2):
+            nc.vector.tensor_copy(parted[h][:].bitcast(U16), both[:, items_of(h)].bitcast(U16).rearrange("p (j d) -> p d j", d=2))
         load_weight(WV, 0, 2)
         for q in BY_PORT:
             nc.sync.dma_start(scale_rows(planes2, q), picked2_scales[LOADED_ROW + 8 * q : LOADED_ROW + 8 * (q + 1), :].bitcast(I32))
@@ -199,7 +203,7 @@ def tile_list_gmu_relu_scatP_kernel(
             return picked_words[:, items_of(h)].bitcast(FP8X4), picked_scales[h][:]
 
         def v2_side(h, a):
-            return parted[:, a, 2 * HALF * h : 2 * HALF * (h + 1)].bitcast(FP4X4), planes2[:, J * a + HALF * h : J * a + HALF * (h + 1)]
+            return parted[h][:, a].bitcast(FP4X4), planes2[:, J * a + HALF * h : J * a + HALF * (h + 1)]
 
         def product(acc, passes):
             for i, (lhs, rhs) in enumerate(passes):
@@ -244,14 +248,14 @@ def tile_list_gmu_relu_scatP_kernel(
             nc.sync.dma_start(out_0[P * w : P * (w + 1), :], windows[w % 3][:])
 
         open_window("room_window0", 0)
-        open_window("room_window1", 0)
         picked_words = held([P, J], U32, "picked_words")
         nc.vector.tensor_copy(picked_words[:], v_words[:].indirect(list1[:]))
 
         reserve("room_scales", J - 64)
         reserve("room_early_wv", 2 * J - 64)
         reserve("room_first", 3 * J - 64)
-        reserve("room_window2", 4 * T)
+        reserve("room_window1", 4 * T)
+        reserve("room_window2", 4 * T - 64)
         early_wv = held([P, 2, P, PACK], BF16, "early_wv", over="room_early_wv")
         round_weight(early_wv[:], raw(WV, 0, 2))
         quantise(early_wv[:], [(0, WV), (1, WV)], held([P, 2 * P], U32, "codes_wv")[:])
@@ -261,9 +265,9 @@ def tile_list_gmu_relu_scatP_kernel(
         for h in range(2):
             make_at(0, h)
         reserve("room_ats3", 4 * J)
-        reserve("room_late_zt", 8 * HALF)
+        reserve("room_late_zt", 12 * HALF)
         second_bias = held([P, 32], F32, "second_bias", over="room_late_zt", shift=-64)
-        nc.gpsimd.tensor_copy(second_bias[:, 0:1], bias[:, 1:2])
+        nc.vector.tensor_copy(second_bias[:, 0:1], bias[:, 1:2])
         bias_of = [bias[:, 0:1], second_bias[:, 0:1], bias[:, 2:3], bias[:, 3:4]]
         gate_codes = held([P, 3 * P], U32, "gate_codes0")
         first = held([P, 3, P, PACK], BF16, "first", over="room_first")
@@ -272,7 +276,7 @@ def tile_list_gmu_relu_scatP_kernel(
         round_weight(first[:, 2:3], last_first[:])
         quantise(first[:, 0:2], [(0, ZV), (0, ZT0)], gate_codes[:, 0 : 2 * P])
         quantise(first[:, 2:3], [(0, ZT1)], gate_codes[:, 2 * P : 3 * P])
-        open_window("room_window2", 0)
+        open_window("room_window1", 0)
         for h in range(2):
             at_of[1, h] = held([P, HALF], F32, "at1_%d" % h, over="v2_words", shift=4 * HALF * h)[:]
             make_at(1, h)
@@ -291,8 +295,10 @@ def tile_list_gmu_relu_scatP_kernel(
         work0 = held([P, J], F32, "work0")
         nc.vector.tensor_tensor(work0[:, items_of(0)], diffs[0, 0], gate_of[0, 0], ALU.mult)
         make_diff(1, 1)
+        open_window("room_window2", 0)
         nc.vector.tensor_tensor(work0[:, items_of(1)], diffs[0, 1], gate_of[0, 1], ALU.mult)
-        nc.vector.tensor_tensor(work0[:], work0[:], ats[0][:], ALU.add)
+        for h in range(2):
+            nc.vector.tensor_tensor(work0[:, items_of(h)], work0[:, items_of(h)], at_of[0, h], ALU.add)
         second = held([P, 3, P, PACK], BF16, "second", over="room_gate0")
         for i, m in enumerate((ZV, ZT0, ZT1)):
             round_weight(second[:, i : i + 1], raw(m, 1, 1))
@@ -305,8 +311,6 @@ def tile_list_gmu_relu_scatP_kernel(
         nc.vector.tensor_copy(windows[0][:].indirect(list1[:]), results0[:])
         store(0)
 
-        late_zv = held([P, 2, P, PACK], BF16, "late_zv", over="work0")
-        round_on_gpsimd(late_zv[:].rearrange("p w c j -> p (w c) j"), ZV, 2, 2)
         for h in range(2):
             make_gate(1, h)
         work1 = [held([P, HALF], F32, "work1_%d" % h) for h in range(2)]
@@ -317,22 +321,18 @@ def tile_list_gmu_relu_scatP_kernel(
 
         late_wv = held([P, 2, P, PACK], BF16, "late_wv", over="diffs0")
         round_weight(late_wv[:], raw(WV, 2, 2))
-        late_zt = held([P, 2, 2, P, PACK], BF16, "late_zt", over="room_late_zt")
-        for i, rows in enumerate((raw(ZT0, 2, 2), last_late[:])):
+        late_zt = held([P, 2, 3, P, PACK], BF16, "late_zt", over="room_late_zt")
+        for i, rows in enumerate((raw(ZV, 2, 2), raw(ZT0, 2, 2), last_late[:])):
             round_weight(late_zt[:, :, i], rows)
         ats[3] = held([P, J], F32, "ats3", over="room_ats3")
         for h in range(2):
             at_of[3, h] = ats[3][:, items_of(h)]
             make_at(3, h)
         late_codes = held([P, 8 * P], U32, "late_codes")
-        late_parts = (
-            (late_wv[:], [(2, WV), (3, WV)]),
-            (late_zv[:], [(2, ZV), (3, ZV)]),
-            (late_zt[:, 0], [(2, ZT0), (2, ZT1)]),
-            (late_zt[:, 1], [(3, ZT0), (3, ZT1)]),
-        )
-        for i, (grouped, parts) in enumerate(late_parts):
-            quantise(grouped, parts, late_codes[:, 2 * P * i : 2 * P * (i + 1)], "last_late", 2 * P * i)
+        quantise(late_wv[:], [(2, WV), (3, WV)], late_codes[:, 0 : 2 * P], "last_late", 0)
+        for i in range(2):
+            parts = [(2 + i, m) for m in (ZV, ZT0, ZT1)]
+            quantise(late_zt[:, i], parts, late_codes[:, (2 + 3 * i) * P : (5 + 3 * i) * P], "last_late", (2 + 3 * i) * P)
         result10 = held([P, HALF], F32, "result10", over="late_zt")
         nc.gpsimd.tensor_tensor(result10[:], work1[0][:], weight[:, items_of(0)], ALU.mult)
         result11 = held([P, HALF], F32, "result11", over="late_zt", shift=4 * HALF)

@@ -80,7 +80,8 @@ def tile_list_gmu_relu_scatP_kernel(
 
         list1 = lists.tile([P, J // 16], U16, name="list1")
         list2 = lists.tile([P, J // 16], U16, name="list2")
-        reserve("room_window0", 4 * T)
+        for i in range(2):
+            reserve("room_window%d" % i, 4 * T)
         reserve("room_v2_scales", T - 64)
         v2_scales = held([P, T], U8, "v2_scales", over="room_v2_scales")
         loaded = held([P, MATS * PACK * N + J + SLABS + BLOCKS], F32, "loaded")
@@ -89,19 +90,18 @@ def tile_list_gmu_relu_scatP_kernel(
         wt_planes = held([P, 2 * N], U8, "wt_planes")
         v2_words = held([P, T], U32, "v2_words")
         v_words = held([P, T], U32, "v_words")
-        reserve("room_both", 2 * J)
-        both = held([P, J], U32, "picked2_both", over="room_both")
-        wt_codes = {u: held([P, 2, 2 * P], I32, "wt_codes%d" % u) for u in (1, 0)}
+        both = [held([P, HALF], U32, "picked2_both%d" % h) for h in range(2)]
+        wt_codes = {1: held([P, 2, 2 * P], I32, "wt_codes1", over="picked2_both1"), 0: held([P, 2, 2 * P], I32, "wt_codes0")}
         weight = loaded[:, MATS * PACK * N : MATS * PACK * N + J]
         bias = loaded[:, MATS * PACK * N + J : MATS * PACK * N + J + SLABS]
         weight_cols = loaded[:, MATS * PACK * N + J + SLABS :]
 
-        nc.vector.memset(v2_scales[0:LOADED_ROW, :].bitcast(I32), 0)
         for tile in (wt_planes, v_scales, planes2):
             nc.vector.memset(tile[:].bitcast(I32), 0)
 
-        zeros = held([P, P], F32, "zeros", over="room_window0")
+        zeros = held([P, P], F32, "zeros", over="room_window1", shift=-2 * P)
         nc.vector.memset(zeros[:], 0.0)
+        nc.vector.memset(v2_scales[0:LOADED_ROW, :].bitcast(I32), 0)
         ident = held([P, P], F32, "ident")
         nc.gpsimd.affine_select(
             out=ident[:], in_=zeros[:], compare_op=ALU.not_equal, fill=1.0, base=0, pattern=[[-1, P]], channel_multiplier=1
@@ -142,10 +142,10 @@ def tile_list_gmu_relu_scatP_kernel(
         picked2_scales = held([P, J], U8, "picked2_scales")
         nc.vector.tensor_copy(picked2_scales[:], v2_scales[:].indirect(list2[:]))
         for h in range(2):
-            nc.vector.tensor_copy(both[:, items_of(h)], v2_words[:].indirect(offsets_of(list2, h)))
+            nc.vector.tensor_copy(both[h][:], v2_words[:].indirect(offsets_of(list2, h)))
         parted = [held([P, 2, 2 * HALF], U8, "picked2_words%d" % h) for h in range(2)]
         for h in range(2):
-            nc.vector.tensor_copy(parted[h][:].bitcast(U16), both[:, items_of(h)].bitcast(U16).rearrange("p (j d) -> p d j", d=2))
+            nc.vector.tensor_copy(parted[h][:].bitcast(U16), both[h][:].bitcast(U16).rearrange("p (j d) -> p d j", d=2))
         load_weight(WV, 0, 2)
         for q in BY_PORT:
             nc.sync.dma_start(scale_rows(planes2, q), picked2_scales[LOADED_ROW + 8 * q : LOADED_ROW + 8 * (q + 1), :].bitcast(I32))
@@ -247,15 +247,15 @@ def tile_list_gmu_relu_scatP_kernel(
         def store(w):
             nc.sync.dma_start(out_0[P * w : P * (w + 1), :], windows[w % 3][:])
 
-        open_window("room_window0", 0)
+        for i in range(2):
+            open_window("room_window%d" % i, 0)
         picked_words = held([P, J], U32, "picked_words")
         nc.vector.tensor_copy(picked_words[:], v_words[:].indirect(list1[:]))
 
         reserve("room_scales", J - 64)
         reserve("room_early_wv", 2 * J - 64)
-        reserve("room_first", 3 * J - 64)
-        reserve("room_window1", 4 * T)
-        reserve("room_window2", 4 * T - 64)
+        reserve("room_first", 3 * J + 256 - 64)
+        reserve("room_window2", 4 * T)
         early_wv = held([P, 2, P, PACK], BF16, "early_wv", over="room_early_wv")
         round_weight(early_wv[:], raw(WV, 0, 2))
         quantise(early_wv[:], [(0, WV), (1, WV)], held([P, 2 * P], U32, "codes_wv")[:])
@@ -265,63 +265,70 @@ def tile_list_gmu_relu_scatP_kernel(
         for h in range(2):
             make_at(0, h)
         reserve("room_ats3", 4 * J)
-        reserve("room_late_zt", 12 * HALF)
+        reserve("room_late_zt", 16 * HALF)
         second_bias = held([P, 32], F32, "second_bias", over="room_late_zt", shift=-64)
         nc.vector.tensor_copy(second_bias[:, 0:1], bias[:, 1:2])
         bias_of = [bias[:, 0:1], second_bias[:, 0:1], bias[:, 2:3], bias[:, 3:4]]
         gate_codes = held([P, 3 * P], U32, "gate_codes0")
-        first = held([P, 3, P, PACK], BF16, "first", over="room_first")
+        first = held([P, 3 * P * PACK + P], BF16, "first", over="room_first")[:, 0 : 3 * P * PACK].rearrange("p (m c j) -> p m c j", m=3, j=PACK)
         for i, m in enumerate((ZV, ZT0)):
             round_on_gpsimd(first[:, i], m, 0, 1)
         round_weight(first[:, 2:3], last_first[:])
         quantise(first[:, 0:2], [(0, ZV), (0, ZT0)], gate_codes[:, 0 : 2 * P])
         quantise(first[:, 2:3], [(0, ZT1)], gate_codes[:, 2 * P : 3 * P])
-        open_window("room_window1", 0)
+        open_window("room_window2", 0)
         for h in range(2):
             at_of[1, h] = held([P, HALF], F32, "at1_%d" % h, over="v2_words", shift=4 * HALF * h)[:]
             make_at(1, h)
-        whole_diffs = {0: held([P, J], F32, "diffs0", over="room_early_wv", shift=64)}
+        diffs[0, 1] = held([P, HALF], F32, "diff0_1", over="room_first", shift=128 - 4 * HALF)[:]
+        diffs[0, 0] = held([P, HALF], F32, "diff0_0", over="room_first", shift=128)[:]
         for w in (1, 2):
-            whole_diffs[w] = held([P, J], F32, "diffs%d" % w)
-        for w in range(3):
+            slab_diffs = held([P, J], F32, "diffs%d" % w)
             for h in range(2):
-                diffs[w, h] = whole_diffs[w][:, items_of(h)]
+                diffs[w, h] = slab_diffs[:, items_of(h)]
+        second_codes = held([P, 3 * P], U32, "gate_codes1")
+
+        def second_part(i, m, over, shift):
+            grouped = held([P, 1, P, PACK], BF16, "second%d" % i, over=over, shift=shift)
+            round_weight(grouped[:], raw(m, 1, 1))
+            quantise(grouped[:], [(1, m)], second_codes[:, P * i : P * (i + 1)], "codes_wv", P * i)
+
         make_diff(0, 0)
         make_gate(0, 0)
+        second_part(0, ZV, "room_first", 128 + 4 * HALF)
         make_diff(0, 1)
         make_diff(1, 0)
         make_gate(0, 1)
+        second_part(1, ZT0, "gate_codes0", 0)
 
         work0 = held([P, J], F32, "work0")
         nc.vector.tensor_tensor(work0[:, items_of(0)], diffs[0, 0], gate_of[0, 0], ALU.mult)
         make_diff(1, 1)
-        open_window("room_window2", 0)
         nc.vector.tensor_tensor(work0[:, items_of(1)], diffs[0, 1], gate_of[0, 1], ALU.mult)
+        second_part(2, ZT1, "room_gate0", 4 * HALF - HALF)
         for h in range(2):
             nc.vector.tensor_tensor(work0[:, items_of(h)], work0[:, items_of(h)], at_of[0, h], ALU.add)
-        second = held([P, 3, P, PACK], BF16, "second", over="room_gate0")
-        for i, m in enumerate((ZV, ZT0, ZT1)):
-            round_weight(second[:, i : i + 1], raw(m, 1, 1))
-        quantise(second[:], [(1, ZV), (1, ZT0), (1, ZT1)], held([P, 3 * P], U32, "gate_codes1", over="room_gate1")[:])
         for h in range(2):
-            at_of[2, h] = held([P, HALF], F32, "at2_%d" % h, over="second", shift=4 * HALF * h)[:]
+            at_of[2, h] = held([P, HALF], F32, "at2_%d" % h, over="room_gate0", shift=4 * HALF * h)[:]
             make_at(2, h)
         results0 = held([P, J], F32, "results0")
-        nc.vector.tensor_tensor(results0[:], work0[:], weight, ALU.mult)
+        for h in range(2):
+            nc.vector.tensor_tensor(results0[:, items_of(h)], work0[:, items_of(h)], weight[:, items_of(h)], ALU.mult)
         nc.vector.tensor_copy(windows[0][:].indirect(list1[:]), results0[:])
         store(0)
 
         for h in range(2):
             make_gate(1, h)
-        work1 = [held([P, HALF], F32, "work1_%d" % h) for h in range(2)]
+        work1 = [held([P, HALF], F32, "work1_%d" % h, over="work0", shift=4 * HALF * h) for h in range(2)]
         for h in range(2):
             nc.gpsimd.tensor_tensor(work1[h][:], diffs[1, h], gate_of[1, h], ALU.mult)
         for h in range(2):
             nc.gpsimd.tensor_tensor(work1[h][:], work1[h][:], at_of[1, h], ALU.add)
 
-        late_wv = held([P, 2, P, PACK], BF16, "late_wv", over="diffs0")
-        round_weight(late_wv[:], raw(WV, 2, 2))
-        late_zt = held([P, 2, 3, P, PACK], BF16, "late_zt", over="room_late_zt")
+        late = held([P, 2 * MATS, P, PACK], BF16, "late_zt", over="room_late_zt")
+        late_wv = late[:, 0:2]
+        late_zt = late[:, 2:].rearrange("p (w m) c j -> p w m c j", w=2)
+        round_weight(late_wv, raw(WV, 2, 2))
         for i, rows in enumerate((raw(ZV, 2, 2), raw(ZT0, 2, 2), last_late[:])):
             round_weight(late_zt[:, :, i], rows)
         ats[3] = held([P, J], F32, "ats3", over="room_ats3")
@@ -329,7 +336,7 @@ def tile_list_gmu_relu_scatP_kernel(
             at_of[3, h] = ats[3][:, items_of(h)]
             make_at(3, h)
         late_codes = held([P, 8 * P], U32, "late_codes")
-        quantise(late_wv[:], [(2, WV), (3, WV)], late_codes[:, 0 : 2 * P], "last_late", 0)
+        quantise(late_wv, [(2, WV), (3, WV)], late_codes[:, 0 : 2 * P], "last_late", 0)
         for i in range(2):
             parts = [(2 + i, m) for m in (ZV, ZT0, ZT1)]
             quantise(late_zt[:, i], parts, late_codes[:, (2 + 3 * i) * P : (5 + 3 * i) * P], "last_late", (2 + 3 * i) * P)
@@ -377,13 +384,12 @@ def tile_list_gmu_relu_scatP_kernel(
         whole_woven = {}
         out_scales = held([P, SLABS, HALF], U8, "out_scales")
 
-        def turn(w, g, turned, copy):
-            for chunk in range(4):
+        def turn(w, g, pair, chunks, number, copy):
+            turned = bank([P, len(chunks), P], "turned%d_%d_%d" % (w, g, chunks[0]), number)
+            for i, chunk in enumerate(chunks):
                 first = HALF * chunk + P * g
-                nc.tensor.transpose(turned[:, chunk, :], windows[w % 3][:, first : first + P], ident[:])
-            pair = held([P, 2, P, 2], BF16, "pair%d_%d" % (w, g))
-            copy(pair[:], turned.rearrange("p c (q u e) -> p u (c q) e", u=2, e=2))
-            return pair
+                nc.tensor.transpose(turned[:, i, :], windows[w % 3][:, first : first + P], ident[:])
+            copy(pair[:, :, QUADRANT * chunks.start : QUADRANT * chunks.stop], turned[:].rearrange("p c (q u e) -> p u (c q) e", u=2, e=2))
 
         def turn_back(w, pair, g, number, copy):
             back = bank([P, 2, P], "back%d_%d" % (w, g), number)
@@ -399,7 +405,13 @@ def tile_list_gmu_relu_scatP_kernel(
             else:
                 woven[w] = [held([P, P * PACK], BF16, "woven%d_%d" % (w, g))[:] for g in range(GROUPS)]
             turn_banks = REGROUP_BANKS[w % 2] if w else FIRST_TURN_BANKS
-            pairs = [turn(w, g, bank([P, 4, P], "turned%d_%d" % (w, g), turn_banks[g])[:], turn_copies[g]) for g in range(GROUPS)]
+            pairs = [held([P, 2, P, 2], BF16, "pair%d_%d" % (w, g)) for g in range(GROUPS)]
+            for g in range(GROUPS):
+                if (w, g) == (SLABS - 1, GROUPS - 1):
+                    turn(w, g, pairs[g], range(0, 2), turn_banks[g], turn_copies[g])
+                    turn(w, g, pairs[g], range(2, 4), turn_banks[0], turn_copies[g])
+                else:
+                    turn(w, g, pairs[g], range(4), turn_banks[g], turn_copies[g])
             for g in range(GROUPS):
                 turn_back(w, pairs[g], g, REGROUP_BANKS[1 - w % 2][g], back_copies[g])
 
@@ -429,7 +441,7 @@ def tile_list_gmu_relu_scatP_kernel(
 
         hand_on("early_codes", [0, 1, 2], "work3", -4 * HALF, nc.scalar)
         last = SLABS - 1
-        regroup(last, on_scalar[:3] + [nc.vector.tensor_copy], on_scalar[:2] + [nc.vector.tensor_copy] * 2)
+        regroup(last, on_scalar[:3] + [nc.vector.tensor_copy], on_scalar[:3] + [nc.vector.tensor_copy])
         hand_on("last_codes", [last], "", 0, nc.scalar)
         for chunk in range(4):
             (nc.sync if chunk < 2 else nc.scalar).dma_start(

from contextlib import ExitStack

import concourse.mybir as mybir

K, L, N, T, J = 512, 1024, 512, 2048, 1024
FLOPS = 2 * N * J * (K + L) * 2

F32 = mybir.dt.float32
BF16 = mybir.dt.bfloat16
I32 = mybir.dt.int32
U32 = mybir.dt.uint32
U16 = mybir.dt.uint16
U8 = mybir.dt.uint8
FP8X4 = mybir.dt.float8_e4m3fn_x4
FP4X4 = mybir.dt.float4_e2m1fn_x4
ALU = mybir.AluOpType
ACT = mybir.ActivationFunctionType

P = 128
PACK = 4
HALF = 512
QUADRANT = 32
LIST_COLS = HALF // 16
LOADED_ROW = 3 * QUADRANT
SLABS = N // P
MATS = 4
GROUPS = 4
BLOCKS = HALF // P
BANK = 2048
BY_PORT = (0, 2, 1, 3)
WV, ZV, ZT0, ZT1 = range(MATS)
HT_BANKS = ((0, 1), (6, 7), (2, 3), (4, 5))
HV_BANKS = ((4, 5), (4, 5), (0, 1), (2, 3))
Z_BANKS = ((2, 3), (6, 7), (6, 7), (0, 1))
SUM_BANKS = (0, 2)
REGROUP_BANKS = ((0, 2, 6, 7), (4, 1, 3, 5))
FIRST_TURN_BANKS = (2, 0, 2, 0)


def tile_list_gmu_relu_scatP_kernel(
    tc, tab_words, tab_scales, tab2_words, tab2_scales, zv, zt, b, wv, wt_words, wt_scales, wgo, offs, offs2, out_0, out_1, out_2
):
    nc = tc.nc
    with ExitStack() as ctx:
        lists = ctx.enter_context(tc.tile_pool(name="lists", bufs=1))
        keep = ctx.enter_context(tc.tile_pool(name="keep", bufs=1))
        psum = ctx.enter_context(tc.psum_pool(name="psum", bufs=1))

        sizes = {F32: 4, I32: 4, U32: 4, BF16: 2, U8: 1}
        places = {"free": 0}

        def reserve(name, size):
            places[name] = places["free"]
            places["free"] = places["free"] + (size + 63) // 64 * 64

        def held(shape, dtype, name, over="", shift=0):
            if over:
                places[name] = places[over] + shift
            else:
                size = sizes[dtype]
                for count in shape[1:]:
                    size = size * count
                reserve(name, size)
            return keep.tile(shape, dtype, name=name, align_bytes=64, offset=places[name])

        def bank(shape, name, number):
            return psum.tile(shape, F32, name=name, offset=BANK * number)

        def words_view(words):
            return words[0].rearrange("p t i -> p (t i)").bitcast(I32)

        def scale_rows(tile, q):
            return tile[QUADRANT * q : QUADRANT * q + 4, :].bitcast(I32)

        def items_of(h):
            return slice(HALF * h, HALF * (h + 1))

        def offsets_of(tile, h):
            return tile[:, LIST_COLS * h : LIST_COLS * (h + 1)]

        list1 = lists.tile([P, J // 16], U16, name="list1")
        list2 = lists.tile([P, J // 16], U16, name="list2")
        for i in range(2):
            reserve("room_window%d" % i, 4 * T)
        reserve("room_v2_scales", T - 64)
        v2_scales = held([P, T], U8, "v2_scales", over="room_v2_scales")
        loaded = held([P, MATS * PACK * N + J + SLABS + BLOCKS], F32, "loaded")
        v_scales = held([P, T], U8, "v_scales")
        planes2 = held([P, 2 * J], U8, "planes2")
        wt_planes = held([P, 2 * N], U8, "wt_planes")
        v2_words = held([P, T], U32, "v2_words")
        v_words = held([P, T], U32, "v_words")
        both = [held([P, HALF], U32, "picked2_both%d" % h) for h in range(2)]
        wt_codes = {1: held([P, 2, 2 * P], I32, "wt_codes1", over="picked2_both1"), 0: held([P, 2, 2 * P], I32, "wt_codes0")}
        weight = loaded[:, MATS * PACK * N : MATS * PACK * N + J]
        bias = loaded[:, MATS * PACK * N + J : MATS * PACK * N + J + SLABS]
        weight_cols = loaded[:, MATS * PACK * N + J + SLABS :]

        for tile in (wt_planes, v_scales, planes2):
            nc.vector.memset(tile[:].bitcast(I32), 0)

        zeros = held([P, P], F32, "zeros", over="room_window1", shift=-2 * P)
        nc.vector.memset(zeros[:], 0.0)
        nc.vector.memset(v2_scales[0:LOADED_ROW, :].bitcast(I32), 0)
        ident = held([P, P], F32, "ident")
        nc.gpsimd.affine_select(
            out=ident[:], in_=zeros[:], compare_op=ALU.not_equal, fill=1.0, base=0, pattern=[[-1, P]], channel_multiplier=1
        )

        unread = held([P, 1], F32, "unread")
        nc.scalar.activation(unread[:], ident[:, 0:1], ACT.Sigmoid)

        sources = [wv, zv, zt[0:512, :], zt[512:1024, :]]

        def raw(m, first, count):
            start = PACK * (N * m + P * first)
            return loaded[:, start : start + PACK * P * count].rearrange("p (j n) -> p j n", j=PACK)

        def load_weight(m, first, count, tile=None):
            nc.sync.dma_start(raw(m, first, count) if tile is None else tile, sources[m].rearrange("(p j) n -> p j n", j=PACK)[:, :, P * first : P * (first + count)])

        def load_wt(u):
            nc.sync.dma_start(wt_codes[u][:], wt_words.rearrange("a p n i -> p a (n i)").bitcast(I32)[:, :, 2 * P * u : 2 * P * (u + 1)])

        def load_v_scales(q):
            nc.sync.dma_start(scale_rows(v_scales, q), tab_scales[0, 4 * q : 4 * q + 4, :].bitcast(I32))

        def load_wt_scales(q):
            nc.sync.dma_start(
                scale_rows(wt_planes, q).rearrange("r (a n) -> r a n", a=2),
                wt_scales[:, 4 * q : 4 * q + 4, :].bitcast(I32).rearrange("a r n -> r a n"),
            )

        nc.sync.dma_start(list2[:], offs2)
        nc.sync.dma_start(v2_scales[LOADED_ROW:P, :].bitcast(I32), tab2_scales.bitcast(I32).rearrange("a r t -> r a t"))
        nc.sync.dma_start(v2_words[:].bitcast(I32), words_view(tab2_words))
        nc.sync.dma_start(list1[:], offs)
        nc.sync.dma_start(v_words[:].bitcast(I32), words_view(tab_words))
        load_wt(0)
        for q in BY_PORT:
            load_wt_scales(q)
        picked2_scales = held([P, J], U8, "picked2_scales")
        nc.vector.tensor_copy(picked2_scales[:], v2_scales[:].indirect(list2[:]))
        for h in range(2):
            nc.vector.tensor_copy(both[h][:], v2_words[:].indirect(offsets_of(list2, h)))
        parted = [held([P, 2, 2 * HALF], U8, "picked2_words%d" % h) for h in range(2)]
        for h in range(2):
            nc.vector.tensor_copy(parted[h][:].bitcast(U16), both[h][:].bitcast(U16).rearrange("p (j d) -> p d j", d=2))
        load_weight(WV, 0, 2)
        for q in BY_PORT:
            nc.sync.dma_start(scale_rows(planes2, q), picked2_scales[LOADED_ROW + 8 * q : LOADED_ROW + 8 * (q + 1), :].bitcast(I32))
        load_weight(ZV, 0, 1)
        for q in BY_PORT:
            load_v_scales(q)
        load_weight(ZT0, 0, 1)
        last_first = held([P, PACK, P], F32, "last_first", over="v2_words", shift=J)
        load_weight(ZT1, 0, 1, last_first[:])
        with nc.allow_non_contiguous_dma(reason="one value a partition and column"):
            nc.sync.dma_start(bias, b.rearrange("(w p) -> p w", p=P))
        for m in (ZV, ZT0, ZT1):
            load_weight(m, 1, 1)
        load_wt(1)
        nc.sync.dma_start(weight, wgo)
        load_weight(WV, 2, 2)
        load_weight(ZV, 2, 2)
        load_weight(ZT0, 2, 2)
        last_late = held([P, PACK, 2 * P], F32, "last_late", over="v2_words", shift=4 * J)
        load_weight(ZT1, 2, 2, last_late[:])
        with nc.allow_non_contiguous_dma(reason="one value a partition and column"):
            nc.sync.dma_start(weight_cols, wgo[0, 0:HALF].rearrange("(c p) -> p c", p=P))

        windows = []

        def open_window(over, shift):
            windows.append(held([P, T], F32, "window%d" % len(windows), over=over, shift=shift))
            nc.gpsimd.memset(windows[-1][:], 0.0)

        made = {}

        def round_weight(grouped, rows):
            nc.scalar.copy(
                grouped.rearrange("p w (c i) j -> p w c j i", i=4),
                rows.rearrange("p j (w c i) -> p w c j i", i=4, c=P // 4),
            )

        def round_on_gpsimd(grouped, m, first, count):
            nc.gpsimd.tensor_scalar(grouped, raw(m, first, count).rearrange("p j c -> p c j"), 1.0, 0.0, ALU.mult, ALU.add)

        def quantise(grouped, parts, codes, over="", shift=0):
            planes = held([P, len(parts) * P], U8, "planes_%d_%d" % parts[0], over=over, shift=shift)
            nc.vector.quantize_mx(out=codes.bitcast(FP8X4), scales=planes[:], in_=grouped.rearrange("p a c j -> p (a c j)"))
            for i, part in enumerate(parts):
                made[part] = codes[:, P * i : P * (i + 1)].bitcast(FP8X4), planes[:, P * i : P * (i + 1)]

        def made_side(w, m):
            return made[w, m]

        def wt_side(w, a):
            first = P * (w % 2)
            return wt_codes[w // 2][:, a, first : first + P].bitcast(FP8X4), wt_planes[:, N * a + P * w : N * a + P * (w + 1)]

        def v_side(h):
            return picked_words[:, items_of(h)].bitcast(FP8X4), picked_scales[h][:]

        def v2_side(h, a):
            return parted[h][:, a].bitcast(FP4X4), planes2[:, J * a + HALF * h : J * a + HALF * (h + 1)]

        def product(acc, passes):
            for i, (lhs, rhs) in enumerate(passes):
                nc.tensor.matmul_mx(
                    out=acc, lhsT=lhs[0], lhsT_scale=lhs[1], rhs=rhs[0], rhs_scale=rhs[1],
                    start=(i == 0), stop=(i == len(passes) - 1),
                )
            return acc

        ats = {0: held([P, J], F32, "ats0")}
        at_of = {(0, h): ats[0][:, items_of(h)] for h in range(2)}
        gate_of = {}
        for h in range(2):
            reserve("room_gate%d" % h, 8 * HALF)
            gate_of[0, h] = held([P, HALF], F32, "gate0_%d" % h, over="room_gate%d" % h)[:]
        for w in range(1, SLABS):
            for h in range(2):
                gate_of[w, h] = held([P, HALF], F32, "gate%d_%d" % (w, h))[:]
        diffs = {}

        def make_gate(w, h):
            z = product(bank([P, HALF], "z%d_%d" % (w, h), Z_BANKS[w][h])[:], [(made_side(w, ZV), v_side(h)), (made_side(w, ZT0), v2_side(h, 0)), (made_side(w, ZT1), v2_side(h, 1))])
            nc.scalar.activation(gate_of[w, h], z, ACT.Sigmoid, bias=bias_of[w], scale=1.0)

        def make_at(w, h):
            ht = product(bank([P, HALF], "ht%d_%d" % (w, h), HT_BANKS[w][h])[:], [(wt_side(w, a), v2_side(h, a)) for a in range(2)])
            nc.scalar.activation(at_of[w, h], ht, ACT.Relu)

        def make_hv(w, h):
            return product(bank([P, HALF], "hv%d_%d" % (w, h), HV_BANKS[w][h])[:], [(made_side(w, WV), v_side(h))])

        def subtract_at(w, h, hv):
            nc.vector.scalar_tensor_tensor(diffs[w, h], hv, 0.0, at_of[w, h], ALU.max, ALU.subtract)

        def make_diff(w, h):
            subtract_at(w, h, make_hv(w, h))

        def scatter(w, h, result):
            nc.vector.tensor_copy(windows[w % 3][:].indirect(offsets_of(list1, h)), result)

        def store(w):
            nc.sync.dma_start(out_0[P * w : P * (w + 1), :], windows[w % 3][:])

        for i in range(2):
            open_window("room_window%d" % i, 0)
        picked_words = held([P, J], U32, "picked_words")
        nc.vector.tensor_copy(picked_words[:], v_words[:].indirect(list1[:]))

        reserve("room_scales", J - 64)
        reserve("room_early_wv", 2 * J - 64)
        reserve("room_first", 3 * J + 256 - 64)
        reserve("room_window2", 4 * T)
        early_wv = held([P, 2, P, PACK], BF16, "early_wv", over="room_early_wv")
        round_weight(early_wv[:], raw(WV, 0, 2))
        quantise(early_wv[:], [(0, WV), (1, WV)], held([P, 2 * P], U32, "codes_wv")[:])
        picked_scales = [held([P, HALF], U8, "picked_scales%d" % h, over="room_scales", shift=HALF * h) for h in range(2)]
        for h in range(2):
            nc.vector.tensor_copy(picked_scales[h][:], v_scales[:].indirect(offsets_of(list1, h)))
        for h in range(2):
            make_at(0, h)
        reserve("room_ats3", 4 * J)
        reserve("room_late_zt", 16 * HALF)
        second_bias = held([P, 32], F32, "second_bias", over="room_late_zt", shift=-64)
        nc.vector.tensor_copy(second_bias[:, 0:1], bias[:, 1:2])
        bias_of = [bias[:, 0:1], second_bias[:, 0:1], bias[:, 2:3], bias[:, 3:4]]
        gate_codes = held([P, 3 * P], U32, "gate_codes0")
        first = held([P, 3 * P * PACK + P], BF16, "first", over="room_first")[:, 0 : 3 * P * PACK].rearrange("p (m c j) -> p m c j", m=3, j=PACK)
        for i, m in enumerate((ZV, ZT0)):
            round_on_gpsimd(first[:, i], m, 0, 1)
        round_weight(first[:, 2:3], last_first[:])
        quantise(first[:, 0:2], [(0, ZV), (0, ZT0)], gate_codes[:, 0 : 2 * P])
        quantise(first[:, 2:3], [(0, ZT1)], gate_codes[:, 2 * P : 3 * P])
        open_window("room_window2", 0)
        for h in range(2):
            at_of[1, h] = held([P, HALF], F32, "at1_%d" % h, over="v2_words", shift=4 * HALF * h)[:]
            make_at(1, h)
        diffs[0, 1] = held([P, HALF], F32, "diff0_1", over="room_first", shift=128 - 4 * HALF)[:]
        diffs[0, 0] = held([P, HALF], F32, "diff0_0", over="room_first", shift=128)[:]
        for w in (1, 2):
            slab_diffs = held([P, J], F32, "diffs%d" % w)
            for h in range(2):
                diffs[w, h] = slab_diffs[:, items_of(h)]
        second_codes = held([P, 3 * P], U32, "gate_codes1")

        def second_part(i, m, over, shift):
            grouped = held([P, 1, P, PACK], BF16, "second%d" % i, over=over, shift=shift)
            round_weight(grouped[:], raw(m, 1, 1))
            quantise(grouped[:], [(1, m)], second_codes[:, P * i : P * (i + 1)], "codes_wv", P * i)

        make_diff(0, 0)
        make_gate(0, 0)
        second_part(0, ZV, "room_first", 128 + 4 * HALF)
        make_diff(0, 1)
        make_diff(1, 0)
        make_gate(0, 1)
        second_part(1, ZT0, "gate_codes0", 0)

        work0 = held([P, J], F32, "work0")
        nc.vector.tensor_tensor(work0[:, items_of(0)], diffs[0, 0], gate_of[0, 0], ALU.mult)
        make_diff(1, 1)
        nc.vector.tensor_tensor(work0[:, items_of(1)], diffs[0, 1], gate_of[0, 1], ALU.mult)
        second_part(2, ZT1, "room_gate0", 4 * HALF - HALF)
        for h in range(2):
            nc.vector.tensor_tensor(work0[:, items_of(h)], work0[:, items_of(h)], at_of[0, h], ALU.add)
        for h in range(2):
            at_of[2, h] = held([P, HALF], F32, "at2_%d" % h, over="room_gate0", shift=4 * HALF * h)[:]
            make_at(2, h)
        results0 = held([P, J], F32, "results0")
        for h in range(2):
            nc.vector.tensor_tensor(results0[:, items_of(h)], work0[:, items_of(h)], weight[:, items_of(h)], ALU.mult)
        nc.vector.tensor_copy(windows[0][:].indirect(list1[:]), results0[:])
        store(0)

        for h in range(2):
            make_gate(1, h)
        work1 = [held([P, HALF], F32, "work1_%d" % h, over="work0", shift=4 * HALF * h) for h in range(2)]
        for h in range(2):
            nc.gpsimd.tensor_tensor(work1[h][:], diffs[1, h], gate_of[1, h], ALU.mult)
        for h in range(2):
            nc.gpsimd.tensor_tensor(work1[h][:], work1[h][:], at_of[1, h], ALU.add)

        late = held([P, 2 * MATS, P, PACK], BF16, "late_zt", over="room_late_zt")
        late_wv = late[:, 0:2]
        late_zt = late[:, 2:].rearrange("p (w m) c j -> p w m c j", w=2)
        round_weight(late_wv, raw(WV, 2, 2))
        for i, rows in enumerate((raw(ZV, 2, 2), raw(ZT0, 2, 2), last_late[:])):
            round_weight(late_zt[:, :, i], rows)
        ats[3] = held([P, J], F32, "ats3", over="room_ats3")
        for h in range(2):
            at_of[3, h] = ats[3][:, items_of(h)]
            make_at(3, h)
        late_codes = held([P, 8 * P], U32, "late_codes")
        quantise(late_wv, [(2, WV), (3, WV)], late_codes[:, 0 : 2 * P], "last_late", 0)
        for i in range(2):
            parts = [(2 + i, m) for m in (ZV, ZT0, ZT1)]
            quantise(late_zt[:, i], parts, late_codes[:, (2 + 3 * i) * P : (5 + 3 * i) * P], "last_late", (2 + 3 * i) * P)
        result10 = held([P, HALF], F32, "result10", over="late_zt")
        nc.gpsimd.tensor_tensor(result10[:], work1[0][:], weight[:, items_of(0)], ALU.mult)
        result11 = held([P, HALF], F32, "result11", over="late_zt", shift=4 * HALF)
        nc.gpsimd.tensor_tensor(result11[:], work1[1][:], weight[:, items_of(1)], ALU.mult)
        diffs[3, 0] = held([P, HALF], F32, "diff3_0")[:]
        for w, h in ((2, 0), (2, 1), (3, 0)):
            make_diff(w, h)
        last_hv = make_hv(3, 1)
        for h in range(2):
            make_gate(2, h)
        for h in range(2):
            make_gate(3, h)
        scatter(1, 0, result10[:])
        diffs[3, 1] = held([P, HALF], F32, "diff3_1", over="work1_0")[:]
        subtract_at(3, 1, last_hv)
        scatter(1, 1, result11[:])
        store(1)

        work2 = [held([P, HALF], F32, "work2_%d" % h, over=("at1_0", "gate2_0")[h]) for h in range(2)]
        for h in range(2):
            nc.gpsimd.tensor_tensor(work2[h][:], diffs[2, h], gate_of[2, h], ALU.mult)
        nc.gpsimd.tensor_tensor(work2[1][:], work2[1][:], at_of[2, 1], ALU.add)
        nc.gpsimd.tensor_tensor(diffs[2, 1], work2[1][:], weight[:, items_of(1)], ALU.mult)
        summed = bank([P, BLOCKS, P], "summed", SUM_BANKS[0])
        for c in range(BLOCKS):
            cols = slice(P * c, P * (c + 1))
            nc.tensor.matmul(summed[:, c, :], lhsT=work2[0][:, cols], rhs=ident[:], is_transpose=True, start=True, stop=False)
            nc.tensor.matmul(summed[:, c, :], lhsT=at_of[2, 0][:, cols], rhs=ident[:], is_transpose=True, start=False, stop=True)
        weighted = held([P, BLOCKS, P], F32, "weighted")
        for c in range(BLOCKS):
            nc.scalar.activation(weighted[:, c, :], summed[:, c, :], ACT.Copy, scale=weight_cols[:, c : c + 1])
        upright = bank([P, BLOCKS, P], "upright", SUM_BANKS[1])
        for c in range(BLOCKS):
            nc.tensor.transpose(upright[:, c, :], weighted[:, c, :], ident[:])
        nc.scalar.copy(diffs[2, 0], upright[:].rearrange("p c j -> p (c j)"))
        work3 = held([P, J], F32, "work3", over="gate2_0")
        for h in range(2):
            nc.gpsimd.tensor_tensor(work3[:, items_of(h)], diffs[3, h], gate_of[3, h], ALU.mult)
        nc.gpsimd.tensor_tensor(work3[:], work3[:], ats[3][:], ALU.add)

        woven = {}
        whole_woven = {}
        out_scales = held([P, SLABS, HALF], U8, "out_scales")

        def turn(w, g, pair, chunks, number, copy):
            turned = bank([P, len(chunks), P], "turned%d_%d_%d" % (w, g, chunks[0]), number)
            for i, chunk in enumerate(chunks):
                first = HALF * chunk + P * g
                nc.tensor.transpose(turned[:, i, :], windows[w % 3][:, first : first + P], ident[:])
            copy(pair[:, :, QUADRANT * chunks.start : QUADRANT * chunks.stop], turned[:].rearrange("p c (q u e) -> p u (c q) e", u=2, e=2))

        def turn_back(w, pair, g, number, copy):
            back = bank([P, 2, P], "back%d_%d" % (w, g), number)
            words = pair[:].rearrange("p u m e -> p (u m e)").bitcast(F32)
            for u in range(2):
                nc.tensor.transpose(back[:, u, :], words[:, P * u : P * (u + 1)], ident[:])
            copy(woven[w][g].bitcast(F32).rearrange("p (c u) -> p c u", u=2), back[:].rearrange("p u c -> p c u"))

        def regroup(w, turn_copies, back_copies):
            if w < SLABS - 1:
                whole_woven[w] = held([P, HALF * PACK], BF16, "woven%d" % w)
                woven[w] = [whole_woven[w][:, P * PACK * g : P * PACK * (g + 1)] for g in range(GROUPS)]
            else:
                woven[w] = [held([P, P * PACK], BF16, "woven%d_%d" % (w, g))[:] for g in range(GROUPS)]
            turn_banks = REGROUP_BANKS[w % 2] if w else FIRST_TURN_BANKS
            pairs = [held([P, 2, P, 2], BF16, "pair%d_%d" % (w, g)) for g in range(GROUPS)]
            for g in range(GROUPS):
                if (w, g) == (SLABS - 1, GROUPS - 1):
                    turn(w, g, pairs[g], range(0, 2), turn_banks[g], turn_copies[g])
                    turn(w, g, pairs[g], range(2, 4), turn_banks[0], turn_copies[g])
                else:
                    turn(w, g, pairs[g], range(4), turn_banks[g], turn_copies[g])
            for g in range(GROUPS):
                turn_back(w, pairs[g], g, REGROUP_BANKS[1 - w % 2][g], back_copies[g])

        on_scalar = [nc.scalar.copy] * GROUPS
        regroup(0, on_scalar, on_scalar)
        regroup(1, on_scalar, on_scalar)
        for h in range(2):
            scatter(2, h, diffs[2, h])
        store(2)
        regroup(2, on_scalar, on_scalar)
        nc.vector.tensor_tensor(windows[0][:].indirect(list1[:]), work3[:], weight, ALU.mult)
        store(3)

        def hand_on(name, slabs, over, shift, other_queue):
            out_codes = held([P, len(slabs), HALF], U32, name, over=over, shift=shift)
            for i, w in enumerate(slabs):
                parts = woven[w] if w == SLABS - 1 else [whole_woven[w][:]]
                for part, rounded in enumerate(parts):
                    cols = slice(HALF // len(parts) * part, HALF // len(parts) * (part + 1))
                    nc.vector.quantize_mx(out=out_codes[:, i, cols].bitcast(FP8X4), scales=out_scales[:, w, cols], in_=rounded)
            rows = words_view(out_1).rearrange("(w q) t -> q w t", q=QUADRANT)
            for chunk in (0, 2, 1, 3):
                (nc.sync if chunk < 2 else other_queue).dma_start(
                    rows[:, slabs[0] : slabs[-1] + 1, HALF * chunk : HALF * (chunk + 1)],
                    out_codes[QUADRANT * chunk : QUADRANT * (chunk + 1)].bitcast(I32),
                )

        hand_on("early_codes", [0, 1, 2], "work3", -4 * HALF, nc.scalar)
        last = SLABS - 1
        regroup(last, on_scalar[:3] + [nc.vector.tensor_copy], on_scalar[:3] + [nc.vector.tensor_copy])
        hand_on("last_codes", [last], "", 0, nc.scalar)
        for chunk in range(4):
            (nc.sync if chunk < 2 else nc.scalar).dma_start(
                out_2[0].rearrange("(w r) t -> r w t", r=4)[:, :, HALF * chunk : HALF * (chunk + 1)].bitcast(I32),
                out_scales[QUADRANT * chunk : QUADRANT * chunk + 4].bitcast(I32),
            )
